import numpy as np
import ml_dtypes


def mxq(x, axis, fmt="e4m3"):
    dtype, down = {"e4m3": (ml_dtypes.float8_e4m3fn, 7), "e5m2": (ml_dtypes.float8_e5m2, 14)}[fmt]
    v = np.moveaxis(np.asarray(x, np.float32).astype(ml_dtypes.bfloat16).astype(np.float64), axis, -1)
    blocks = v.reshape(v.shape[:-1] + (-1, 32))
    amax = np.abs(blocks).max(-1, keepdims=True)
    byte = np.maximum(np.where(amax > 0, np.frexp(amax)[1] - 1 + 127, 0) - down, 1)
    scale = np.exp2(byte - 127.0)
    codes = (blocks / scale).astype(np.float32).astype(dtype).astype(np.float64)
    return np.moveaxis((codes * scale).reshape(v.shape), -1, axis)


WIDE = False


def mx_kscale(k):
    if not WIDE:
        return np.ones(k)
    levels = np.array([10, -10, 5, -5, 0])
    if k % 512:
        return np.exp2(np.random.permutation(np.resize(levels, k // 32))).repeat(32)
    a = np.empty((k // 512, 16))
    for p in range(k // 512):
        a[p, :8] = np.random.permutation(np.resize(levels, 8))
        for g in range(8):
            far = levels[np.abs(levels - a[p, g]) >= 10]
            a[p, g + 8] = far[np.random.randint(len(far))]
    return np.exp2(a.ravel()).repeat(32)


def f64(x):
    return np.asarray(x).astype(np.float64)


def striped(idx):
    return np.tile(idx.reshape(-1, 16).T, (8, 1)).astype(np.uint16)


def unstriped(offs):
    return offs[:16].T.reshape(-1).astype(np.int64)


E2M1 = np.array([0.0, 0.5, 1.0, 1.5, 2.0, 3.0, 4.0, 6.0, -0.0, -0.5, -1.0, -1.5, -2.0, -3.0, -4.0, -6.0])


def pack_weight(w, fmt):
    k, n = w.shape
    w = f64(np.asarray(w, np.float32).astype(ml_dtypes.bfloat16)).reshape(k // 32, 32, n)
    amax = np.abs(w).max(1)
    if fmt == "e4m3":
        byte = np.frexp(amax)[1] - 1 + 127 - 7
    else:
        mant, ex = np.frexp(amax / 6.0)
        byte = np.where(mant > 0.5, ex, ex - 1) + 127
    byte = np.clip(np.where(amax > 0, byte, 1), 1, 254)
    scaled = (w * np.exp2(127.0 - byte)[:, None, :]).reshape(k, n).astype(np.float32)
    by_word = np.ascontiguousarray(scaled.reshape(k // 512, 128, 4, n).transpose(0, 1, 3, 2))
    if fmt == "e4m3":
        words = by_word.astype(ml_dtypes.float8_e4m3fn).view(np.uint8)
    else:
        c = by_word.astype(ml_dtypes.float4_e2m1fn).view(np.uint8) & 0xF
        words = (c[..., 0::2] | (c[..., 1::2] << 4)).reshape(k // 512, 128, 2 * n)
    return np.ascontiguousarray(words), np.ascontiguousarray(byte.astype(np.uint8).reshape(k // 512, 16, n))


def unpack_weight(words, scales, fmt):
    g, _, n = scales.shape
    words = np.ascontiguousarray(words).reshape(g, 128, n, -1)
    if fmt == "e4m3":
        vals = words.view(ml_dtypes.float8_e4m3fn).astype(np.float64)
    else:
        nib = np.empty((g, 128, n, 4), np.uint8)
        nib[..., 0::2] = words & 0xF
        nib[..., 1::2] = words >> 4
        vals = E2M1[nib]
    vals = vals * np.repeat(np.exp2(scales.astype(np.float64) - 127.0), 8, axis=1)[..., None]
    return vals.transpose(0, 1, 3, 2).reshape(g * 512, n)


def gelu(v):
    return 0.5 * v * (1.0 + np.tanh(np.sqrt(2.0 / np.pi) * (v + 0.044715 * v**3)))


def bf(x):
    return np.asarray(x, np.float32).astype(ml_dtypes.bfloat16)

def planes(Y):
    n, m = Y.shape
    b = f64(bf(Y)).reshape(n // 32, 32, m)
    amax = np.abs(b).max(1)
    byte = np.clip(np.where(amax > 0, np.frexp(amax)[1] - 1 + 127 - 7, 1), 1, 254)
    codes = (b * np.exp2(127.0 - byte)[:, None, :]).reshape(n, m).astype(np.float32).astype(ml_dtypes.float8_e4m3fn).view(np.uint8)
    words = codes.reshape(n // 512, 128, 4, m).transpose(0, 1, 3, 2)
    return np.ascontiguousarray(words), np.ascontiguousarray(byte.astype(np.uint8).reshape(n // 512, 16, m))


D, K, T, S, T2, S2, N = 512, 1024, 2048, 1024, 1024, 512, 512

def setup_inputs():
    n = np.random.standard_normal
    s = np.tile(mx_kscale(D), K // D)[:, None]
    u = mx_kscale(S)
    beam = np.exp(0.8 * n(N))[None, :] / np.sqrt(2 * S)
    tab_words, tab_scales = pack_weight(n((K, T)) * s / np.sqrt(K), "e4m3")
    tab2_words, tab2_scales = pack_weight(n((K, T2)) / s, "e4m3")
    wi_words, wi_scales = pack_weight(n((S, N)) * beam / u[:, None], "e2m1")
    return {
        "tab_words": tab_words, "tab_scales": tab_scales,
        "tab2_words": tab2_words, "tab2_scales": tab2_scales,
        "offs": striped(np.random.permutation(T)[:S]),
        "offs2": striped(np.random.permutation(T2)[:S2]),
        "g_re": (np.exp(0.3 * n(S)) * u).astype(np.float32),
        "g_im": (np.exp(0.3 * n(S)) * u).astype(np.float32),
        "wr": (n((S, N)) * beam / u[:, None]).astype(np.float32),
        "wi_words": wi_words, "wi_scales": wi_scales,
        "power": np.exp(0.3 * n(S2)).astype(np.float32),
    }

def reference(tab_words, tab_scales, tab2_words, tab2_scales, offs, offs2, g_re, g_im, wr, wi_words, wi_scales, power):
    v = unpack_weight(tab_words, tab_scales, "e4m3")[:, unstriped(offs)]
    v2 = unpack_weight(tab2_words, tab2_scales, "e4m3")[:, unstriped(offs2)]
    re = v.T @ v2
    im = (v[D:].T @ v2[:D]) - (v[:D].T @ v2[D:])
    zr = mxq(f64(g_re)[:, None] * re, 0, "e4m3")
    zi = mxq(f64(g_im)[:, None] * im, 0, "e4m3")
    yr = mxq(f64(wr), 0, "e4m3").T @ zr
    yi = unpack_weight(wi_words, wi_scales, "e2m1").T @ zi
    y = (yr - yi) * f64(power)[None, :]
    words, scales = planes(y)
    return y, words, scales

@@ -1,0 +1,336 @@
+from contextlib import ExitStack
+
+import concourse.mybir as mybir
+from concourse.masks import make_identity
+
+D, K, T, S, T2, S2, N = 512, 1024, 2048, 1024, 1024, 512, 512
+FLOPS = 2 * (2 * K * S * S2 + 2 * S * N * S2)
+
+F32 = mybir.dt.float32
+BF16 = mybir.dt.bfloat16
+I32 = mybir.dt.int32
+U32 = mybir.dt.uint32
+U16 = mybir.dt.uint16
+U8 = mybir.dt.uint8
+FP8X4 = mybir.dt.float8_e4m3fn_x4
+FP4X4 = mybir.dt.float4_e2m1fn_x4
+MULT = mybir.AluOpType.mult
+ADD = mybir.AluOpType.add
+SUB = mybir.AluOpType.subtract
+COPY = mybir.ActivationFunctionType.Copy
+
+P = 128
+PACK = 4
+PASS = P * PACK
+CH = S2 // P
+
+
+def tile_list_mimo_beam_channel_kernel(
+    tc, tab_words, tab_scales, tab2_words, tab2_scales, offs, offs2, g_re, g_im, wr, wi_words, wi_scales, power,
+    out_0, out_1, out_2,
+):
+    nc = tc.nc
+    with ExitStack() as ctx:
+        keep = ctx.enter_context(tc.tile_pool(name="keep", bufs=1))
+        arena = ctx.enter_context(tc.tile_pool(name="arena", bufs=1))
+        psum = ctx.enter_context(tc.psum_pool(name="psum", bufs=8))
+
+        def sb(name, shape, dtype):
+            return keep.tile(shape, dtype, name=name, align_bytes=64)
+
+        def reuse(name, shape, dtype, offset):
+            return arena.tile(shape, dtype, name=name, align_bytes=64, offset=offset)
+
+        def bank(shape):
+            return psum.tile(shape, F32, name="bank", tag="bank")
+
+        idx = keep.tile([P, S // 16], U16, name="idx")
+        idx2 = keep.tile([P, S2 // 16], U16, name="idx2")
+        us = sb("us", [P, S2], U8)
+        vs = [sb("vs%d" % h, [P, PASS], U8) for h in range(2)]
+        gim = sb("gim", [P, 2, PACK], F32)
+        wbf = [sb("wbf%d" % h, [P, N, PACK], BF16) for h in range(2)]
+        wq = [sb("wq%d" % h, [P, N], U32) for h in range(2)]
+        ws = [sb("ws%d" % h, [P, N], U8) for h in range(2)]
+        ga = [[sb("ga%d_%d" % (h, t), [P, S2], F32) for t in range(PACK)] for h in range(2)]
+        zip_ = [sb("zip%d" % h, [P, PACK, S2], BF16) for h in range(2)]
+        zrp = [sb("zrp%d" % h, [P, PACK, S2], BF16) for h in range(2)]
+        ziq = [sb("ziq%d" % h, [P, S2], U32) for h in range(2)]
+        zis = [sb("zis%d" % h, [P, S2], U8) for h in range(2)]
+        zrq = [sb("zrq%d" % h, [P, S2], U32) for h in range(2)]
+        zrs = [sb("zrs%d" % h, [P, S2], U8) for h in range(2)]
+        yt = [sb("yt%d" % c, [P, PACK, P], F32) for c in range(CH)]
+        yf = [sb("yf%d" % c, [P, PACK, P], F32) for c in range(CH)]
+        yb = [sb("yb%d" % c, [P, P, PACK], BF16) for c in range(CH)]
+        yq = sb("yq", [P, S2], U32)
+        ys = sb("ys", [P, S2], U8)
+        ident = sb("ident", [P, P], F32)
+        acc = {}
+        held = {}
+
+        def load_words(dst, src):
+            nc.sync.dma_start(out=dst[:].bitcast(I32), in_=src.rearrange("p t i -> p (t i)").bitcast(I32))
+
+        def load_planes(engs, dst, src):
+            for q in range(4):
+                engs[q].dma_start(out=dst[32 * q : 32 * q + 8, :].bitcast(I32), in_=src[:, 4 * q : 4 * q + 4, :].bitcast(I32))
+
+        def load_wr(h):
+            nc.sync.dma_start(out=wraw[h][:], in_=wr[h * PASS : (h + 1) * PASS, :].rearrange("(p t) n -> p t n", t=PACK))
+
+        def load_g(dst, src):
+            nc.sync.dma_start(out=dst[:], in_=src.rearrange("(h p t) -> p h t", h=2, t=PACK))
+
+        def load_wi():
+            nc.sync.dma_start(out=wiw[:].bitcast(I32), in_=wi_words.bitcast(I32).rearrange("a p n -> p a n"))
+            for q in range(4):
+                nc.sync.dma_start(
+                    out=wis[32 * q : 32 * q + 4, :, :].bitcast(I32),
+                    in_=wi_scales[:, 4 * q : 4 * q + 4, :].bitcast(I32).rearrange("a r n -> r a n"),
+                )
+
+        def load_power():
+            with nc.allow_non_contiguous_dma(reason="one factor a partition"):
+                nc.sync.dma_start(out=pw[:], in_=power.rearrange("(c p) -> p c", p=P))
+
+        def half_list(h):
+            return idx[:, h * (PASS // 16) : (h + 1) * (PASS // 16)]
+
+        def gather_uw(a):
+            nc.vector.tensor_copy(uw[a][:], utab[a][:].indirect(idx2[:]))
+
+        def gather_us():
+            nc.vector.tensor_copy(us[:], ustab[:].indirect(idx2[:]))
+
+        def gather_vw(a, h):
+            nc.vector.tensor_copy(vw[a][h][:].rearrange("p (t m) -> p m t", t=PACK), vtab[a][:].indirect(half_list(h)))
+
+        def gather_vw_plain(a, h):
+            nc.vector.tensor_copy(vwg[a][h][:], vtab[a][:].indirect(half_list(h)))
+
+        def deal_vw(a, h):
+            nc.vector.tensor_copy(
+                vw[a][h][:].bitcast(I32).rearrange("p (t m) -> p t m", t=PACK),
+                vwg[a][h][:].bitcast(I32).rearrange("p (m t) -> p t m", t=PACK),
+            )
+
+        def gather_vs(h):
+            nc.vector.tensor_copy(vsg[h][:], vstab[:].indirect(half_list(h)))
+
+        def deal_vs(h):
+            nc.vector.tensor_copy(
+                vs[h][:].rearrange("p (t m) -> p t m", t=PACK), vsg[h][:].rearrange("p (m t) -> p t m", t=PACK)
+            )
+
+        def stage1(out, av, au, h, t, cols, start, stop):
+            m = slice(t * P, (t + 1) * P)
+            nc.tensor.matmul_mx(
+                out=out,
+                lhsT=vw[av][h][:, m].bitcast(FP8X4), lhsT_scale=vs[h][4 * av :, m],
+                rhs=uw[au][:, cols].bitcast(FP8X4), rhs_scale=us[4 * au :, cols],
+                start=start, stop=stop,
+            )
+
+        def im_first(h, t):
+            b = bank([P, S2])
+            stage1(b[:], 1, 0, h, t, slice(0, S2), True, True)
+            nc.scalar.activation(out=ga[h][t][:], in_=b[:], func=COPY, scale=gim[:, h, t : t + 1])
+
+        def im_second_mm(h, t):
+            b = bank([P, S2])
+            stage1(b[:], 0, 1, h, t, slice(0, S2), True, True)
+            held["b", h, t] = b
+
+        def im_second(h, t):
+            nc.vector.scalar_tensor_tensor(
+                out=zip_[h][:, t, :], in0=held["b", h, t][:], scalar=gim[:, h, t : t + 1], in1=ga[h][t][:], op0=MULT, op1=SUB
+            )
+
+        def weave(eng, dst, src, lo, hi):
+            o = dst[:, lo:hi, :].rearrange("p (c i) t -> p c t i", i=4)
+            s = src[:, :, lo:hi].rearrange("p t (c i) -> p c t i", i=4)
+            if eng == "s":
+                nc.scalar.copy(out=o, in_=s)
+            elif eng == "v":
+                nc.vector.tensor_copy(out=o, in_=s)
+            else:
+                nc.gpsimd.tensor_scalar(out=o, in0=s, scalar1=1.0, scalar2=0.0, op0=MULT, op1=ADD)
+
+        def quant(q, s, src, lo, hi):
+            nc.vector.quantize_mx(
+                out=q[:, lo:hi].bitcast(FP8X4), scales=s[:, lo:hi], in_=src[:, lo:hi, :].rearrange("p j t -> p (j t)")
+            )
+
+        def re_mm(h, c):
+            b = bank([P, PACK, P])
+            for t in range(PACK):
+                for a in range(2):
+                    stage1(b[:, t, :], a, a, h, t, slice(c * P, (c + 1) * P), a == 0, a == 1)
+            held["r", h, c] = b
+
+        def re_out(h, c):
+            nc.vector.tensor_tensor(
+                out=zrb[h][:, c * P : (c + 1) * P, :],
+                in0=held["r", h, c][:].rearrange("p t j -> p j t"),
+                in1=gre[:, h, :].unsqueeze(1).to_broadcast([P, P, PACK]),
+                op=MULT,
+            )
+
+        def re_plane(h, t):
+            b = bank([P, S2])
+            for a in range(2):
+                stage1(b[:], a, a, h, t, slice(0, S2), a == 0, a == 1)
+            nc.scalar.activation(out=zrp[h][:, t, :], in_=b[:], func=COPY, scale=gre[:, h, t : t + 1])
+
+        def stage2(kind, h, c, start, stop):
+            if start:
+                acc[c] = bank([P, N])
+            m = slice(c * P, (c + 1) * P)
+            if kind == "r":
+                nc.tensor.matmul_mx(
+                    out=acc[c][:], lhsT=zrq[h][:, m].bitcast(FP8X4), lhsT_scale=zrs[h][:, m],
+                    rhs=wq[h][:].bitcast(FP8X4), rhs_scale=ws[h][:], start=start, stop=stop,
+                )
+            else:
+                nc.tensor.matmul_mx(
+                    out=acc[c][:], lhsT=ziq[h][:, m].bitcast(FP8X4), lhsT_scale=zis[h][:, m],
+                    rhs=wiw[:, h, :].bitcast(FP4X4), rhs_scale=wis[:, h, :], start=start, stop=stop,
+                )
+
+        def y_scale(c):
+            nc.scalar.activation(
+                out=yt[c][:], in_=acc[c][:].rearrange("p (m t) -> p t m", t=PACK), func=COPY, scale=pw[:, c : c + 1]
+            )
+
+        def y_turn(c, eng):
+            b = bank([P, PACK, P])
+            for t in range(PACK):
+                nc.tensor.transpose(b[:, t, :], yt[c][:, t, :], ident[:])
+            if eng == "s":
+                nc.scalar.copy(out=yf[c][:], in_=b[:])
+            else:
+                nc.vector.tensor_copy(out=yf[c][:], in_=b[:])
+
+        def y_store(c):
+            nc.sync.dma_start(
+                out=out_0.rearrange("(p t) j -> p t j", t=PACK)[:, :, c * P : (c + 1) * P], in_=yf[c][:]
+            )
+
+        def y_quant(c):
+            nc.vector.quantize_mx(
+                out=yq[:, c * P : (c + 1) * P].bitcast(FP8X4), scales=ys[:, c * P : (c + 1) * P],
+                in_=yb[c][:].rearrange("p j t -> p (j t)"),
+            )
+
+        def store_codes(lo, hi):
+            nc.sync.dma_start(
+                out=out_1[0].rearrange("p m t -> p (m t)").bitcast(I32)[:, lo:hi], in_=yq[:, lo:hi].bitcast(I32)
+            )
+
+        def store_planes():
+            for q in range(4):
+                eng = nc.scalar if q % 2 else nc.sync
+                eng.dma_start(out=out_2[0, 4 * q : 4 * q + 4, :].bitcast(I32), in_=ys[32 * q : 32 * q + 4, :].bitcast(I32))
+
+        RA, RB, RC, RD, RE = 0, 10240, 20480, 30720, 38912
+        vtab, utab, wraw, uw, vsg, zib, zrb = {}, {}, {}, {}, {}, {}, {}
+        vw = [{}, {}]
+        vwg = [{}, {}]
+        utab[0] = reuse("utab0", [P, T2], U32, RE)
+        vtab[1] = reuse("vtab1", [P, T], U32, RD)
+        ustab = reuse("ustab", [P, T2], U8, RB + 7680)
+        vstab = reuse("vstab", [P, T], U8, RC + 7168)
+        vsg[0] = reuse("vsg0", [P, PASS], U8, RA + 7936)
+        uw[0] = sb("uw0", [P, S2], U32)
+        vw[0][0] = sb("vw00", [P, PASS], U32)
+        vw[0][1] = sb("vw01", [P, PASS], U32)
+        zrb[0] = sb("zrb0", [P, S2, PACK], BF16)
+        nc.gpsimd.memset(vstab[:].bitcast(I32), 0)
+        nc.vector.memset(ustab[:].bitcast(I32), 0)
+
+        nc.sync.dma_start(idx2[:], offs2)
+        nc.sync.dma_start(idx[:], offs)
+        load_words(utab[0], tab2_words[0])
+        nc.gpsimd.dma_start(out=vtab[1][:].bitcast(I32), in_=tab_words[1].rearrange("p t i -> p (t i)").bitcast(I32))
+        load_planes([nc.sync] * 4, vstab, tab_scales)
+        load_planes([nc.sync] * 4, ustab, tab2_scales)
+        nc.gpsimd.dma_start(out=gim[:], in_=g_im.rearrange("(h p t) -> p h t", h=2, t=PACK))
+        make_identity(nc, ident[:])
+
+        gather_uw(0)
+        utab[1] = reuse("utab1", [P, T2], U32, RE)
+        load_words(utab[1], tab2_words[1])
+        gather_vs(0)
+        deal_vs(0)
+        vtab[0] = reuse("vtab0", [P, T], U32, RA)
+        vw[1][0] = reuse("vw10", [P, PASS], U32, RA + 8192)
+        load_words(vtab[0], tab_words[0])
+        gather_vw(1, 0)
+        gather_us()
+        wraw[0] = reuse("wraw0", [P, PACK, N], F32, RB)
+        vsg[1] = reuse("vsg1", [P, PASS], U8, RB + 8192)
+        load_wr(0)
+        for t in range(PACK):
+            im_first(0, t)
+        gather_vs(1)
+        wraw[1] = reuse("wraw1", [P, PACK, N], F32, RC)
+        vw[1][1] = reuse("vw11", [P, PASS], U32, RC + 8192)
+        load_wr(1)
+        gather_vw(1, 1)
+        deal_vs(1)
+        wiw = reuse("wiw", [P, 2, 2 * N], U8, RB + 8192)
+        uw[1] = reuse("uw1", [P, S2], U32, RD)
+        wis = reuse("wis", [P, 2, N], U8, RD + 2048)
+        nc.gpsimd.memset(wis[:].bitcast(I32), 0)
+        for t in range(PACK):
+            im_first(1, t)
+        gather_uw(1)
+        gre = reuse("gre", [P, 2, PACK], F32, RE)
+        load_g(gre, g_re)
+        load_wi()
+        for h in range(2):
+            gather_vw(0, h)
+            for t in range(PACK):
+                im_second_mm(h, t)
+        pw = reuse("pw", [P, CH], F32, RA)
+        load_power()
+        weave("s", wbf[0], wraw[0], 0, N)
+        weave("s", wbf[1], wraw[1], 0, N)
+        zib[0] = reuse("zib0", [P, S2, PACK], BF16, RC)
+        zib[1] = reuse("zib1", [P, S2, PACK], BF16, RB)
+        for h in range(2):
+            for t in range(PACK):
+                im_second(h, t)
+            for c in range(CH):
+                re_mm(h, c)
+            for half in range(2):
+                weave("s", zib[h], zip_[h], half * 256, half * 256 + 256)
+        for c in range(CH):
+            re_out(0, c)
+        quant(wq[0], ws[0], wbf[0], 0, N)
+        quant(wq[1], ws[1], wbf[1], 0, N)
+        quant(zrq[0], zrs[0], zrb[0], 0, S2)
+        quant(ziq[0], zis[0], zib[0], 0, S2)
+        zrb[1] = reuse("zrb1", [P, S2, PACK], BF16, RC)
+        for c in range(CH):
+            stage2("r", 0, c, True, False)
+            stage2("i", 0, c, False, False)
+        re_out(1, 0)
+        for c in range(CH):
+            if c % 2 == 0:
+                quant(ziq[1], zis[1], zib[1], c * P, (c + 2) * P)
+            if c + 1 < CH:
+                re_out(1, c + 1)
+            quant(zrq[1], zrs[1], zrb[1], c * P, (c + 1) * P)
+            stage2("i", 1, c, False, False)
+            stage2("r", 1, c, False, True)
+            y_scale(c)
+        for c in range(CH):
+            y_turn(c, "s")
+            y_store(c)
+            weave("v", yb[c], yf[c], 0, P)
+        for c in range(CH):
+            y_quant(c)
+            if c % 2:
+                store_codes((c - 1) * P, (c + 1) * P)
+        store_planes()

@@ -33,7 +33,7 @@ def tile_list_mimo_beam_channel_kernel(
     with ExitStack() as ctx:
         keep = ctx.enter_context(tc.tile_pool(name="keep", bufs=1))
         arena = ctx.enter_context(tc.tile_pool(name="arena", bufs=1))
-        psum = ctx.enter_context(tc.psum_pool(name="psum", bufs=8))
+        psum = ctx.enter_context(tc.psum_pool(name="psum", bufs=4))
 
         def sb(name, shape, dtype):
             return keep.tile(shape, dtype, name=name, align_bytes=64)
@@ -41,8 +41,8 @@ def tile_list_mimo_beam_channel_kernel(
         def reuse(name, shape, dtype, offset):
             return arena.tile(shape, dtype, name=name, align_bytes=64, offset=offset)
 
-        def bank(shape):
-            return psum.tile(shape, F32, name="bank", tag="bank")
+        def bank(shape, tag):
+            return psum.tile(shape, F32, name=tag, tag=tag)
 
         idx = keep.tile([P, S // 16], U16, name="idx")
         idx2 = keep.tile([P, S2 // 16], U16, name="idx2")
@@ -50,9 +50,7 @@ def tile_list_mimo_beam_channel_kernel(
         vs = [sb("vs%d" % h, [P, PASS], U8) for h in range(2)]
         gim = sb("gim", [P, 2, PACK], F32)
         wbf = [sb("wbf%d" % h, [P, N, PACK], BF16) for h in range(2)]
-        wq = [sb("wq%d" % h, [P, N], U32) for h in range(2)]
         ws = [sb("ws%d" % h, [P, N], U8) for h in range(2)]
-        ga = [[sb("ga%d_%d" % (h, t), [P, S2], F32) for t in range(PACK)] for h in range(2)]
         zip_ = [sb("zip%d" % h, [P, PACK, S2], BF16) for h in range(2)]
         zrp = [sb("zrp%d" % h, [P, PACK, S2], BF16) for h in range(2)]
         ziq = [sb("ziq%d" % h, [P, S2], U32) for h in range(2)]
@@ -132,12 +130,12 @@ def tile_list_mimo_beam_channel_kernel(
             )
 
         def im_first(h, t):
-            b = bank([P, S2])
+            b = bank([P, S2], "x")
             stage1(b[:], 1, 0, h, t, slice(0, S2), True, True)
             nc.scalar.activation(out=ga[h][t][:], in_=b[:], func=COPY, scale=gim[:, h, t : t + 1])
 
         def im_second_mm(h, t):
-            b = bank([P, S2])
+            b = bank([P, S2], "y")
             stage1(b[:], 0, 1, h, t, slice(0, S2), True, True)
             held["b", h, t] = b
 
@@ -154,7 +152,10 @@ def tile_list_mimo_beam_channel_kernel(
             elif eng == "v":
                 nc.vector.tensor_copy(out=o, in_=s)
             else:
-                nc.gpsimd.tensor_scalar(out=o, in0=s, scalar1=1.0, scalar2=0.0, op0=MULT, op1=ADD)
+                nc.gpsimd.tensor_scalar(
+                    out=dst[:, lo:hi, :], in0=src[:, :, lo:hi].rearrange("p t j -> p j t"),
+                    scalar1=1.0, scalar2=0.0, op0=MULT, op1=ADD,
+                )
 
         def quant(q, s, src, lo, hi):
             nc.vector.quantize_mx(
@@ -162,7 +163,7 @@ def tile_list_mimo_beam_channel_kernel(
             )
 
         def re_mm(h, c):
-            b = bank([P, PACK, P])
+            b = bank([P, PACK, P], "y")
             for t in range(PACK):
                 for a in range(2):
                     stage1(b[:, t, :], a, a, h, t, slice(c * P, (c + 1) * P), a == 0, a == 1)
@@ -177,14 +178,14 @@ def tile_list_mimo_beam_channel_kernel(
             )
 
         def re_plane(h, t):
-            b = bank([P, S2])
+            b = bank([P, S2], "x")
             for a in range(2):
                 stage1(b[:], a, a, h, t, slice(0, S2), a == 0, a == 1)
             nc.scalar.activation(out=zrp[h][:, t, :], in_=b[:], func=COPY, scale=gre[:, h, t : t + 1])
 
         def stage2(kind, h, c, start, stop):
             if start:
-                acc[c] = bank([P, N])
+                acc[c] = bank([P, N], "x")
             m = slice(c * P, (c + 1) * P)
             if kind == "r":
                 nc.tensor.matmul_mx(
@@ -202,14 +203,35 @@ def tile_list_mimo_beam_channel_kernel(
                 out=yt[c][:], in_=acc[c][:].rearrange("p (m t) -> p t m", t=PACK), func=COPY, scale=pw[:, c : c + 1]
             )
 
+        def y_scale_v(c):
+            nc.vector.tensor_scalar(
+                out=yt[c][:], in0=acc[c][:].rearrange("p (m t) -> p t m", t=PACK), scalar1=pw[:, c : c + 1], scalar2=None,
+                op0=MULT,
+            )
+
         def y_turn(c, eng):
-            b = bank([P, PACK, P])
+            b = bank([P, PACK, P], "y")
             for t in range(PACK):
                 nc.tensor.transpose(b[:, t, :], yt[c][:, t, :], ident[:])
             if eng == "s":
                 nc.scalar.copy(out=yf[c][:], in_=b[:])
             else:
                 nc.vector.tensor_copy(out=yf[c][:], in_=b[:])
+
+        def y_turn_mm(c):
+            b = bank([P, PACK, P], "y")
+            for t in range(PACK):
+                nc.tensor.transpose(b[:, t, :], yt[c][:, t, :], ident[:])
+            held["y", c] = b
+
+        def y_out(c, eng):
+            if eng == "s":
+                nc.scalar.copy(out=yf[c][:], in_=held["y", c][:])
+            else:
+                nc.vector.tensor_copy(out=yf[c][:], in_=held["y", c][:])
+
+        def y_round(c):
+            nc.vector.tensor_copy(out=yb[c][:], in_=held["y", c][:].rearrange("p t j -> p j t"))
 
         def y_store(c):
             nc.sync.dma_start(
@@ -232,88 +254,99 @@ def tile_list_mimo_beam_channel_kernel(
                 eng = nc.scalar if q % 2 else nc.sync
                 eng.dma_start(out=out_2[0, 4 * q : 4 * q + 4, :].bitcast(I32), in_=ys[32 * q : 32 * q + 4, :].bitcast(I32))
 
-        RA, RB, RC, RD, RE = 0, 10240, 20480, 30720, 38912
-        vtab, utab, wraw, uw, vsg, zib, zrb = {}, {}, {}, {}, {}, {}, {}
+        RA, RB, RC, RD, RE, RF = 0, 8192, 16384, 24576, 32768, 37888
+        vtab, utab, wraw, uw, vsg, zib, zrb, wq = {}, {}, {}, {}, {}, {}, {}, {}
         vw = [{}, {}]
         vwg = [{}, {}]
+        ga = [[sb("ga%d_%d" % (h, t), [P, S2], F32) for t in range(PACK)] for h in range(2)]
+        vtab[0] = reuse("vtab0", [P, T], U32, RA)
+        vtab[1] = reuse("vtab1", [P, T], U32, RB)
+        vsg[0] = sb("vsg0", [P, PASS], U8)
+        ustab = reuse("ustab", [P, T2], U8, RD - 512)
         utab[0] = reuse("utab0", [P, T2], U32, RE)
-        vtab[1] = reuse("vtab1", [P, T], U32, RD)
-        ustab = reuse("ustab", [P, T2], U8, RB + 7680)
-        vstab = reuse("vstab", [P, T], U8, RC + 7168)
-        vsg[0] = reuse("vsg0", [P, PASS], U8, RA + 7936)
+        vstab = reuse("vstab", [P, T], U8, RF)
         uw[0] = sb("uw0", [P, S2], U32)
+        uw[1] = sb("uw1", [P, S2], U32)
         vw[0][0] = sb("vw00", [P, PASS], U32)
-        vw[0][1] = sb("vw01", [P, PASS], U32)
+        vw[1][0] = sb("vw10", [P, PASS], U32)
         zrb[0] = sb("zrb0", [P, S2, PACK], BF16)
+        gre = sb("gre", [P, 2, PACK], F32)
         nc.gpsimd.memset(vstab[:].bitcast(I32), 0)
         nc.vector.memset(ustab[:].bitcast(I32), 0)
 
         nc.sync.dma_start(idx2[:], offs2)
         nc.sync.dma_start(idx[:], offs)
         load_words(utab[0], tab2_words[0])
-        nc.gpsimd.dma_start(out=vtab[1][:].bitcast(I32), in_=tab_words[1].rearrange("p t i -> p (t i)").bitcast(I32))
+        for a in (1, 0):
+            nc.gpsimd.dma_start(out=vtab[a][:].bitcast(I32), in_=tab_words[a].rearrange("p t i -> p (t i)").bitcast(I32))
         load_planes([nc.sync] * 4, vstab, tab_scales)
         load_planes([nc.sync] * 4, ustab, tab2_scales)
         nc.gpsimd.dma_start(out=gim[:], in_=g_im.rearrange("(h p t) -> p h t", h=2, t=PACK))
+        nc.gpsimd.dma_start(out=gre[:], in_=g_re.rearrange("(h p t) -> p h t", h=2, t=PACK))
         make_identity(nc, ident[:])
 
         gather_uw(0)
+        gather_vs(0)
         utab[1] = reuse("utab1", [P, T2], U32, RE)
         load_words(utab[1], tab2_words[1])
-        gather_vs(0)
         deal_vs(0)
-        vtab[0] = reuse("vtab0", [P, T], U32, RA)
-        vw[1][0] = reuse("vw10", [P, PASS], U32, RA + 8192)
-        load_words(vtab[0], tab_words[0])
-        gather_vw(1, 0)
         gather_us()
-        wraw[0] = reuse("wraw0", [P, PACK, N], F32, RB)
-        vsg[1] = reuse("vsg1", [P, PASS], U8, RB + 8192)
+        wraw[0] = reuse("wraw0", [P, PACK, N], F32, RC)
+        wraw[1] = reuse("wraw1", [P, PACK, N], F32, RD)
         load_wr(0)
+        load_wr(1)
+        gather_vw(1, 0)
         for t in range(PACK):
             im_first(0, t)
+        gather_vw(0, 0)
+        gather_uw(1)
+        for t in range(PACK):
+            im_second_mm(0, t)
+        for t in range(PACK):
+            re_plane(0, t)
+        weave("s", zrb[0], zrp[0], 0, S2)
+        for c in range(CH):
+            weave("g", wbf[0], wraw[0], c * P, (c + 1) * P)
+        vw[1][1] = reuse("vw11", [P, PASS], U32, RE)
+        vsg[1] = reuse("vsg1", [P, PASS], U8, RE + 2048)
+        vw[0][1] = reuse("vw01", [P, PASS], U32, RE + 2560)
         gather_vs(1)
-        wraw[1] = reuse("wraw1", [P, PACK, N], F32, RC)
-        vw[1][1] = reuse("vw11", [P, PASS], U32, RC + 8192)
-        load_wr(1)
         gather_vw(1, 1)
         deal_vs(1)
-        wiw = reuse("wiw", [P, 2, 2 * N], U8, RB + 8192)
-        uw[1] = reuse("uw1", [P, S2], U32, RD)
-        wis = reuse("wis", [P, 2, N], U8, RD + 2048)
-        nc.gpsimd.memset(wis[:].bitcast(I32), 0)
+        wiw = reuse("wiw", [P, 2, 2 * N], U8, RF)
+        wis = reuse("wis", [P, 2, N], U8, RB)
         for t in range(PACK):
             im_first(1, t)
-        gather_uw(1)
-        gre = reuse("gre", [P, 2, PACK], F32, RE)
-        load_g(gre, g_re)
-        load_wi()
-        for h in range(2):
-            gather_vw(0, h)
-            for t in range(PACK):
-                im_second_mm(h, t)
-        pw = reuse("pw", [P, CH], F32, RA)
-        load_power()
-        weave("s", wbf[0], wraw[0], 0, N)
         weave("s", wbf[1], wraw[1], 0, N)
-        zib[0] = reuse("zib0", [P, S2, PACK], BF16, RC)
-        zib[1] = reuse("zib1", [P, S2, PACK], BF16, RB)
-        for h in range(2):
-            for t in range(PACK):
-                im_second(h, t)
-            for c in range(CH):
-                re_mm(h, c)
-            for half in range(2):
-                weave("s", zib[h], zip_[h], half * 256, half * 256 + 256)
+        gather_vw(0, 1)
+        nc.gpsimd.memset(wis[:].bitcast(I32), 0)
+        load_wi()
+        pw = reuse("pw", [P, CH], F32, RB + 1024)
+        load_power()
+        for t in range(PACK):
+            im_second_mm(1, t)
+        zib[0] = reuse("zib0", [P, S2, PACK], BF16, RA)
+        zib[1] = sb("zib1", [P, S2, PACK], BF16)
+        wq[0] = reuse("wq0", [P, N], U32, RA + 4096)
+        wq[1] = reuse("wq1", [P, N], U32, RA + 6144)
+        for t in range(PACK):
+            im_second(0, t)
         for c in range(CH):
-            re_out(0, c)
+            weave("g", zib[0], zip_[0], c * P, (c + 1) * P)
         quant(wq[0], ws[0], wbf[0], 0, N)
-        quant(wq[1], ws[1], wbf[1], 0, N)
         quant(zrq[0], zrs[0], zrb[0], 0, S2)
-        quant(ziq[0], zis[0], zib[0], 0, S2)
-        zrb[1] = reuse("zrb1", [P, S2, PACK], BF16, RC)
+        for t in range(PACK):
+            im_second(1, t)
         for c in range(CH):
             stage2("r", 0, c, True, False)
+        for c in range(CH):
+            re_mm(1, c)
+        for half in range(2):
+            weave("s", zib[1], zip_[1], half * 256, half * 256 + 256)
+        quant(ziq[0], zis[0], zib[0], 0, S2)
+        quant(wq[1], ws[1], wbf[1], 0, N)
+        zrb[1] = sb("zrb1", [P, S2, PACK], BF16)
+        for c in range(CH):
             stage2("i", 0, c, False, False)
         re_out(1, 0)
         for c in range(CH):
@@ -324,13 +357,30 @@ def tile_list_mimo_beam_channel_kernel(
             quant(zrq[1], zrs[1], zrb[1], c * P, (c + 1) * P)
             stage2("i", 1, c, False, False)
             stage2("r", 1, c, False, True)
-            y_scale(c)
         for c in range(CH):
-            y_turn(c, "s")
+            if "sssv"[c] == "s":
+                y_scale(c)
+            else:
+                y_scale_v(c)
+            y_turn_mm(c)
+            if "ssss"[c] == "d":
+                y_round(c)
+                y_out(c, "s")
+            elif "ssss"[c] == "e":
+                y_out(c, "s")
+                y_round(c)
+            elif "ssss"[c] == "v":
+                y_out(c, "v")
+                weave("v", yb[c], yf[c], 0, P)
+            elif "ssss"[c] == "g":
+                y_out(c, "s")
+                weave("g", yb[c], yf[c], 0, P)
+            else:
+                y_out(c, "s")
+                weave("v", yb[c], yf[c], 0, P)
             y_store(c)
-            weave("v", yb[c], yf[c], 0, P)
-        for c in range(CH):
-            y_quant(c)
-            if c % 2:
-                store_codes((c - 1) * P, (c + 1) * P)
+            if c:
+                y_quant(c - 1)
+        y_quant(CH - 1)
+        store_codes(0, S2)
         store_planes()

@@ -48,7 +48,6 @@ def tile_list_mimo_beam_channel_kernel(
         idx2 = keep.tile([P, S2 // 16], U16, name="idx2")
         us = sb("us", [P, S2], U8)
         vs = [sb("vs%d" % h, [P, PASS], U8) for h in range(2)]
-        gim = sb("gim", [P, 2, PACK], F32)
         wbf = [sb("wbf%d" % h, [P, N, PACK], BF16) for h in range(2)]
         ws = [sb("ws%d" % h, [P, N], U8) for h in range(2)]
         zip_ = [sb("zip%d" % h, [P, PACK, S2], BF16) for h in range(2)]
@@ -108,8 +107,8 @@ def tile_list_mimo_beam_channel_kernel(
 
         def deal_vw(a, h):
             nc.vector.tensor_copy(
-                vw[a][h][:].bitcast(I32).rearrange("p (t m) -> p t m", t=PACK),
-                vwg[a][h][:].bitcast(I32).rearrange("p (m t) -> p t m", t=PACK),
+                vw[a][h][:].bitcast(I32).rearrange("p (t c i) -> p c t i", t=PACK, i=4),
+                vwg[a][h][:].bitcast(I32).rearrange("p (c i t) -> p c t i", t=PACK, i=4),
             )
 
         def gather_vs(h):
@@ -254,108 +253,117 @@ def tile_list_mimo_beam_channel_kernel(
                 eng = nc.scalar if q % 2 else nc.sync
                 eng.dma_start(out=out_2[0, 4 * q : 4 * q + 4, :].bitcast(I32), in_=ys[32 * q : 32 * q + 4, :].bitcast(I32))
 
-        RA, RB, RC, RD, RE, RF = 0, 8192, 16384, 24576, 32768, 37888
+        RA, RB, RC, RD, RE, RF, RG = 0, 8192, 12800, 20992, 29184, 37376, 39424
         vtab, utab, wraw, uw, vsg, zib, zrb, wq = {}, {}, {}, {}, {}, {}, {}, {}
         vw = [{}, {}]
         vwg = [{}, {}]
-        ga = [[sb("ga%d_%d" % (h, t), [P, S2], F32) for t in range(PACK)] for h in range(2)]
-        vtab[0] = reuse("vtab0", [P, T], U32, RA)
-        vtab[1] = reuse("vtab1", [P, T], U32, RB)
-        vsg[0] = sb("vsg0", [P, PASS], U8)
-        ustab = reuse("ustab", [P, T2], U8, RD - 512)
-        utab[0] = reuse("utab0", [P, T2], U32, RE)
-        vstab = reuse("vstab", [P, T], U8, RF)
+        ga = [{}, {}]
+        vsg[0] = reuse("vsg0", [P, PASS], U8, RB - 256)
+        utab[0] = reuse("utab0", [P, T2], U32, RC - 64)
+        vtab[1] = reuse("vtab1", [P, T], U32, RE)
+        vstab = reuse("vstab", [P, T], U8, RD)
+        ustab = reuse("ustab", [P, T2], U8, RG)
         uw[0] = sb("uw0", [P, S2], U32)
         uw[1] = sb("uw1", [P, S2], U32)
         vw[0][0] = sb("vw00", [P, PASS], U32)
         vw[1][0] = sb("vw10", [P, PASS], U32)
+        vw[0][1] = sb("vw01", [P, PASS], U32)
+        vw[1][1] = sb("vw11", [P, PASS], U32)
+        vwg[0][0] = sb("vwg00", [P, PASS], U32)
+        vwg[1][0] = sb("vwg10", [P, PASS], U32)
         zrb[0] = sb("zrb0", [P, S2, PACK], BF16)
-        gre = sb("gre", [P, 2, PACK], F32)
+        zrb[1] = sb("zrb1", [P, S2, PACK], BF16)
+        zib[0] = sb("zib0", [P, S2, PACK], BF16)
+        zib[1] = sb("zib1", [P, S2, PACK], BF16)
         nc.gpsimd.memset(vstab[:].bitcast(I32), 0)
         nc.vector.memset(ustab[:].bitcast(I32), 0)
 
         nc.sync.dma_start(idx2[:], offs2)
         nc.sync.dma_start(idx[:], offs)
         load_words(utab[0], tab2_words[0])
-        for a in (1, 0):
-            nc.gpsimd.dma_start(out=vtab[a][:].bitcast(I32), in_=tab_words[a].rearrange("p t i -> p (t i)").bitcast(I32))
+        nc.gpsimd.dma_start(out=vtab[1][:].bitcast(I32), in_=tab_words[1].rearrange("p t i -> p (t i)").bitcast(I32))
         load_planes([nc.sync] * 4, vstab, tab_scales)
         load_planes([nc.sync] * 4, ustab, tab2_scales)
-        nc.gpsimd.dma_start(out=gim[:], in_=g_im.rearrange("(h p t) -> p h t", h=2, t=PACK))
-        nc.gpsimd.dma_start(out=gre[:], in_=g_re.rearrange("(h p t) -> p h t", h=2, t=PACK))
         make_identity(nc, ident[:])
 
         gather_uw(0)
-        gather_vs(0)
-        utab[1] = reuse("utab1", [P, T2], U32, RE)
-        load_words(utab[1], tab2_words[1])
-        deal_vs(0)
-        gather_us()
+        gim = reuse("gim", [P, 2, PACK], F32, RC - 64)
         wraw[0] = reuse("wraw0", [P, PACK, N], F32, RC)
-        wraw[1] = reuse("wraw1", [P, PACK, N], F32, RD)
         load_wr(0)
-        load_wr(1)
-        gather_vw(1, 0)
+        load_g(gim, g_im)
+        gather_vs(0)
+        gather_vw_plain(1, 0)
+        deal_vs(0)
+        utab[1] = reuse("utab1", [P, T2], U32, RB)
+        vtab[0] = reuse("vtab0", [P, T], U32, RA)
+        load_words(vtab[0], tab_words[0])
+        load_words(utab[1], tab2_words[1])
+        gather_us()
+        deal_vw(1, 0)
+        weave("s", wbf[0], wraw[0], 0, N)
         for t in range(PACK):
+            ga[0][t] = reuse("ga0_%d" % t, [P, S2], F32, RC + 2048 * t)
             im_first(0, t)
-        gather_vw(0, 0)
+        gre = reuse("gre", [P, 2, PACK], F32, RG)
+        load_g(gre, g_re)
+        vsg[1] = reuse("vsg1", [P, PASS], U8, RG + 64)
+        gather_vs(1)
+        wraw[1] = reuse("wraw1", [P, PACK, N], F32, RD)
+        load_wr(1)
+        gather_vw_plain(0, 0)
+        deal_vs(1)
         gather_uw(1)
-        for t in range(PACK):
-            im_second_mm(0, t)
+        deal_vw(0, 0)
         for t in range(PACK):
             re_plane(0, t)
-        weave("s", zrb[0], zrp[0], 0, S2)
-        for c in range(CH):
-            weave("g", wbf[0], wraw[0], c * P, (c + 1) * P)
-        vw[1][1] = reuse("vw11", [P, PASS], U32, RE)
-        vsg[1] = reuse("vsg1", [P, PASS], U8, RE + 2048)
-        vw[0][1] = reuse("vw01", [P, PASS], U32, RE + 2560)
-        gather_vs(1)
-        gather_vw(1, 1)
-        deal_vs(1)
-        wiw = reuse("wiw", [P, 2, 2 * N], U8, RF)
-        wis = reuse("wis", [P, 2, N], U8, RB)
         for t in range(PACK):
-            im_first(1, t)
-        weave("s", wbf[1], wraw[1], 0, N)
-        gather_vw(0, 1)
+            im_second_mm(0, t)
+        weave("s", zrb[0], zrp[0], 0, S2)
+        vwg[1][1] = reuse("vwg11", [P, PASS], U32, RB)
+        vwg[0][1] = reuse("vwg01", [P, PASS], U32, RB + 2048)
+        gather_vw_plain(1, 1)
+        gather_vw_plain(0, 1)
+        deal_vw(1, 1)
+        wiw = reuse("wiw", [P, 2, 2 * N], U8, RG + 64)
+        wis = reuse("wis", [P, 2, N], U8, RE)
+        pw = reuse("pw", [P, CH], F32, RE + 1024)
         nc.gpsimd.memset(wis[:].bitcast(I32), 0)
         load_wi()
-        pw = reuse("pw", [P, CH], F32, RB + 1024)
         load_power()
         for t in range(PACK):
-            im_second_mm(1, t)
-        zib[0] = reuse("zib0", [P, S2, PACK], BF16, RA)
-        zib[1] = sb("zib1", [P, S2, PACK], BF16)
-        wq[0] = reuse("wq0", [P, N], U32, RA + 4096)
-        wq[1] = reuse("wq1", [P, N], U32, RA + 6144)
+            ga[1][t] = sb("ga1_%d" % t, [P, S2], F32)
+            im_first(1, t)
+
+        deal_vw(0, 1)
+        wq[0] = reuse("wq0", [P, N], U32, RA)
+        wq[1] = reuse("wq1", [P, N], U32, RA + 2048)
         for t in range(PACK):
             im_second(0, t)
-        for c in range(CH):
-            weave("g", zib[0], zip_[0], c * P, (c + 1) * P)
+        weave("s", zib[0], zip_[0], 0, S2)
+        wbf[1] = reuse("wbf1", [P, N, PACK], BF16, RC)
+        weave("s", wbf[1], wraw[1], 0, N)
         quant(wq[0], ws[0], wbf[0], 0, N)
         quant(zrq[0], zrs[0], zrb[0], 0, S2)
         for t in range(PACK):
+            im_second_mm(1, t)
             im_second(1, t)
         for c in range(CH):
             stage2("r", 0, c, True, False)
         for c in range(CH):
             re_mm(1, c)
-        for half in range(2):
-            weave("s", zib[1], zip_[1], half * 256, half * 256 + 256)
         quant(ziq[0], zis[0], zib[0], 0, S2)
-        quant(wq[1], ws[1], wbf[1], 0, N)
-        zrb[1] = sb("zrb1", [P, S2, PACK], BF16)
         for c in range(CH):
             stage2("i", 0, c, False, False)
+        weave("v", zib[1], zip_[1], 0, S2)
         re_out(1, 0)
+        quant(ziq[1], zis[1], zib[1], 0, S2)
         for c in range(CH):
-            if c % 2 == 0:
-                quant(ziq[1], zis[1], zib[1], c * P, (c + 2) * P)
+            stage2("i", 1, c, False, False)
+        quant(wq[1], ws[1], wbf[1], 0, N)
+        for c in range(CH):
             if c + 1 < CH:
                 re_out(1, c + 1)
             quant(zrq[1], zrs[1], zrb[1], c * P, (c + 1) * P)
-            stage2("i", 1, c, False, False)
             stage2("r", 1, c, False, True)
         for c in range(CH):
             if "sssv"[c] == "s":
@@ -363,24 +371,12 @@ def tile_list_mimo_beam_channel_kernel(
             else:
                 y_scale_v(c)
             y_turn_mm(c)
-            if "ssss"[c] == "d":
-                y_round(c)
-                y_out(c, "s")
-            elif "ssss"[c] == "e":
-                y_out(c, "s")
-                y_round(c)
-            elif "ssss"[c] == "v":
-                y_out(c, "v")
-                weave("v", yb[c], yf[c], 0, P)
-            elif "ssss"[c] == "g":
-                y_out(c, "s")
-                weave("g", yb[c], yf[c], 0, P)
-            else:
-                y_out(c, "s")
-                weave("v", yb[c], yf[c], 0, P)
+            y_out(c, "s")
+            weave("v", yb[c], yf[c], 0, P)
             y_store(c)
             if c:
                 y_quant(c - 1)
+        store_codes(0, S2 - P)
         y_quant(CH - 1)
-        store_codes(0, S2)
+        store_codes(S2 - P, S2)
         store_planes()

@@ -3,7 +3,7 @@ from contextlib import ExitStack
 import concourse.mybir as mybir
 from concourse.masks import make_identity
 
-D, K, T, S, T2, S2, N = 512, 1024, 2048, 1024, 1024, 512, 512
+K, T, S, T2, S2, N = 1024, 2048, 1024, 1024, 512, 512
 FLOPS = 2 * (2 * K * S * S2 + 2 * S * N * S2)
 
 F32 = mybir.dt.float32
@@ -22,7 +22,19 @@ COPY = mybir.ActivationFunctionType.Copy
 P = 128
 PACK = 4
 PASS = P * PACK
-CH = S2 // P
+CHUNKS = S2 // P
+RUN = 4
+REAL, IMAG = 0, 1
+SCALED_ON_SCALAR = 2
+
+KB = 1024
+AT_V_REAL = 0
+AT_V_IMAG = 8 * KB
+AT_WR = 16 * KB
+AT_LATE = 32 * KB
+AT_V_FIRST = AT_LATE + 4 * KB + 512
+AT_V_SCALES = 40 * KB
+AT_PRODUCT = 42 * KB
 
 
 def tile_list_mimo_beam_channel_kernel(
@@ -32,351 +44,278 @@ def tile_list_mimo_beam_channel_kernel(
     nc = tc.nc
     with ExitStack() as ctx:
         keep = ctx.enter_context(tc.tile_pool(name="keep", bufs=1))
-        arena = ctx.enter_context(tc.tile_pool(name="arena", bufs=1))
+        reused = ctx.enter_context(tc.tile_pool(name="reused", bufs=1))
         psum = ctx.enter_context(tc.psum_pool(name="psum", bufs=4))
 
-        def sb(name, shape, dtype):
+        def own(name, shape, dtype):
             return keep.tile(shape, dtype, name=name, align_bytes=64)
 
-        def reuse(name, shape, dtype, offset):
-            return arena.tile(shape, dtype, name=name, align_bytes=64, offset=offset)
+        def at(offset, name, shape, dtype):
+            return reused.tile(shape, dtype, name=name, align_bytes=64, offset=offset)
 
-        def bank(shape, tag):
-            return psum.tile(shape, F32, name=tag, tag=tag)
+        def bank(ring, shape):
+            return psum.tile(shape, F32, name=ring, tag=ring)
 
-        idx = keep.tile([P, S // 16], U16, name="idx")
-        idx2 = keep.tile([P, S2 // 16], U16, name="idx2")
-        us = sb("us", [P, S2], U8)
-        vs = [sb("vs%d" % h, [P, PASS], U8) for h in range(2)]
-        wbf = [sb("wbf%d" % h, [P, N, PACK], BF16) for h in range(2)]
-        ws = [sb("ws%d" % h, [P, N], U8) for h in range(2)]
-        zip_ = [sb("zip%d" % h, [P, PACK, S2], BF16) for h in range(2)]
-        zrp = [sb("zrp%d" % h, [P, PACK, S2], BF16) for h in range(2)]
-        ziq = [sb("ziq%d" % h, [P, S2], U32) for h in range(2)]
-        zis = [sb("zis%d" % h, [P, S2], U8) for h in range(2)]
-        zrq = [sb("zrq%d" % h, [P, S2], U32) for h in range(2)]
-        zrs = [sb("zrs%d" % h, [P, S2], U8) for h in range(2)]
-        yt = [sb("yt%d" % c, [P, PACK, P], F32) for c in range(CH)]
-        yf = [sb("yf%d" % c, [P, PACK, P], F32) for c in range(CH)]
-        yb = [sb("yb%d" % c, [P, P, PACK], BF16) for c in range(CH)]
-        yq = sb("yq", [P, S2], U32)
-        ys = sb("ys", [P, S2], U8)
-        ident = sb("ident", [P, P], F32)
-        acc = {}
-        held = {}
+        def chunk(c):
+            return slice(c * P, (c + 1) * P)
 
-        def load_words(dst, src):
-            nc.sync.dma_start(out=dst[:].bitcast(I32), in_=src.rearrange("p t i -> p (t i)").bitcast(I32))
+        def load_words(queue, table, src):
+            queue.dma_start(out=table[:].bitcast(I32), in_=src.rearrange("p t i -> p (t i)").bitcast(I32))
 
-        def load_planes(engs, dst, src):
-            for q in range(4):
-                engs[q].dma_start(out=dst[32 * q : 32 * q + 8, :].bitcast(I32), in_=src[:, 4 * q : 4 * q + 4, :].bitcast(I32))
-
-        def load_wr(h):
-            nc.sync.dma_start(out=wraw[h][:], in_=wr[h * PASS : (h + 1) * PASS, :].rearrange("(p t) n -> p t n", t=PACK))
-
-        def load_g(dst, src):
-            nc.sync.dma_start(out=dst[:], in_=src.rearrange("(h p t) -> p h t", h=2, t=PACK))
-
-        def load_wi():
-            nc.sync.dma_start(out=wiw[:].bitcast(I32), in_=wi_words.bitcast(I32).rearrange("a p n -> p a n"))
+        def load_table_scales(table, src):
             for q in range(4):
                 nc.sync.dma_start(
-                    out=wis[32 * q : 32 * q + 4, :, :].bitcast(I32),
-                    in_=wi_scales[:, 4 * q : 4 * q + 4, :].bitcast(I32).rearrange("a r n -> r a n"),
+                    out=table[32 * q : 32 * q + 8, :].bitcast(I32), in_=src[:, 4 * q : 4 * q + 4, :].bitcast(I32)
                 )
 
-        def load_power():
-            with nc.allow_non_contiguous_dma(reason="one factor a partition"):
-                nc.sync.dma_start(out=pw[:], in_=power.rearrange("(c p) -> p c", p=P))
+        def load_gains(gains, src):
+            nc.gpsimd.dma_start(out=gains[:], in_=src.rearrange("(h p t) -> p h t", h=2, t=PACK))
 
         def half_list(h):
             return idx[:, h * (PASS // 16) : (h + 1) * (PASS // 16)]
 
-        def gather_uw(a):
-            nc.vector.tensor_copy(uw[a][:], utab[a][:].indirect(idx2[:]))
+        def gather_v_words(words, table, h):
+            nc.vector.tensor_copy(words[:].rearrange("p (t m) -> p m t", t=PACK), table[:].indirect(half_list(h)))
 
-        def gather_us():
-            nc.vector.tensor_copy(us[:], ustab[:].indirect(idx2[:]))
-
-        def gather_vw(a, h):
-            nc.vector.tensor_copy(vw[a][h][:].rearrange("p (t m) -> p m t", t=PACK), vtab[a][:].indirect(half_list(h)))
-
-        def gather_vw_plain(a, h):
-            nc.vector.tensor_copy(vwg[a][h][:], vtab[a][:].indirect(half_list(h)))
-
-        def deal_vw(a, h):
+        def deal_v_scales(h):
             nc.vector.tensor_copy(
-                vw[a][h][:].bitcast(I32).rearrange("p (t c i) -> p c t i", t=PACK, i=4),
-                vwg[a][h][:].bitcast(I32).rearrange("p (c i t) -> p c t i", t=PACK, i=4),
+                v_scales[h][:].rearrange("p (t m) -> p t m", t=PACK),
+                v_scales_listed[h][:].rearrange("p (m t) -> p t m", t=PACK),
             )
 
-        def gather_vs(h):
-            nc.vector.tensor_copy(vsg[h][:], vstab[:].indirect(half_list(h)))
-
-        def deal_vs(h):
-            nc.vector.tensor_copy(
-                vs[h][:].rearrange("p (t m) -> p t m", t=PACK), vsg[h][:].rearrange("p (m t) -> p t m", t=PACK)
-            )
-
-        def stage1(out, av, au, h, t, cols, start, stop):
-            m = slice(t * P, (t + 1) * P)
+        def first_stage(out, v_pass, u_pass, h, t, users, start, stop):
             nc.tensor.matmul_mx(
                 out=out,
-                lhsT=vw[av][h][:, m].bitcast(FP8X4), lhsT_scale=vs[h][4 * av :, m],
-                rhs=uw[au][:, cols].bitcast(FP8X4), rhs_scale=us[4 * au :, cols],
-                start=start, stop=stop,
+                lhsT=v_words[v_pass, h][:, chunk(t)].bitcast(FP8X4),
+                lhsT_scale=v_scales[h][4 * v_pass :, chunk(t)],
+                rhs=u_words[u_pass][:, users].bitcast(FP8X4),
+                rhs_scale=u_scales[4 * u_pass :, users],
+                start=start,
+                stop=stop,
             )
 
-        def im_first(h, t):
-            b = bank([P, S2], "x")
-            stage1(b[:], 1, 0, h, t, slice(0, S2), True, True)
-            nc.scalar.activation(out=ga[h][t][:], in_=b[:], func=COPY, scale=gim[:, h, t : t + 1])
+        def im_first_product(h):
+            for t in range(PACK):
+                sums = bank("s", [P, S2])
+                first_stage(sums[:], IMAG, REAL, h, t, slice(0, S2), True, True)
+                nc.scalar.activation(out=product[h][t][:], in_=sums[:], func=COPY, scale=gain_im[:, h, t : t + 1])
 
-        def im_second_mm(h, t):
-            b = bank([P, S2], "y")
-            stage1(b[:], 0, 1, h, t, slice(0, S2), True, True)
-            held["b", h, t] = b
+        def im_second_product(h):
+            banks = []
+            for t in range(PACK):
+                banks.append(bank("v", [P, S2]))
+                first_stage(banks[t][:], REAL, IMAG, h, t, slice(0, S2), True, True)
+            return banks
 
-        def im_second(h, t):
-            nc.vector.scalar_tensor_tensor(
-                out=zip_[h][:, t, :], in0=held["b", h, t][:], scalar=gim[:, h, t : t + 1], in1=ga[h][t][:], op0=MULT, op1=SUB
-            )
-
-        def weave(eng, dst, src, lo, hi):
-            o = dst[:, lo:hi, :].rearrange("p (c i) t -> p c t i", i=4)
-            s = src[:, :, lo:hi].rearrange("p t (c i) -> p c t i", i=4)
-            if eng == "s":
-                nc.scalar.copy(out=o, in_=s)
-            elif eng == "v":
-                nc.vector.tensor_copy(out=o, in_=s)
-            else:
-                nc.gpsimd.tensor_scalar(
-                    out=dst[:, lo:hi, :], in0=src[:, :, lo:hi].rearrange("p t j -> p j t"),
-                    scalar1=1.0, scalar2=0.0, op0=MULT, op1=ADD,
+        def minus_zi(h, banks):
+            for t in range(PACK):
+                nc.vector.scalar_tensor_tensor(
+                    out=zi_slices[h][:, t, :], in0=banks[t][:], scalar=gain_im[:, h, t : t + 1], in1=product[h][t][:],
+                    op0=MULT, op1=SUB,
                 )
 
-        def quant(q, s, src, lo, hi):
-            nc.vector.quantize_mx(
-                out=q[:, lo:hi].bitcast(FP8X4), scales=s[:, lo:hi], in_=src[:, lo:hi, :].rearrange("p j t -> p (j t)")
+        def weave(copy, woven, slices, cols):
+            copy(
+                out=woven[:, cols, :].rearrange("p (c i) t -> p c t i", i=RUN),
+                in_=slices[:, :, cols].rearrange("p t (c i) -> p c t i", i=RUN),
             )
 
-        def re_mm(h, c):
-            b = bank([P, PACK, P], "y")
-            for t in range(PACK):
-                for a in range(2):
-                    stage1(b[:, t, :], a, a, h, t, slice(c * P, (c + 1) * P), a == 0, a == 1)
-            held["r", h, c] = b
+        def quantise(codes, scales, woven, cols):
+            nc.vector.quantize_mx(
+                out=codes[:, cols].bitcast(FP8X4), scales=scales[:, cols], in_=woven[:, cols, :].rearrange("p j t -> p (j t)")
+            )
 
-        def re_out(h, c):
+        def real_pass(c, h, start, stop):
+            nc.tensor.matmul_mx(
+                out=y_t_sums[c][:], lhsT=zr_codes[h][:, chunk(c)].bitcast(FP8X4), lhsT_scale=zr_scales[h][:, chunk(c)],
+                rhs=wr_codes[h][:].bitcast(FP8X4), rhs_scale=wr_scales[h][:], start=start, stop=stop,
+            )
+
+        def imag_pass(c, h):
+            nc.tensor.matmul_mx(
+                out=y_t_sums[c][:], lhsT=zi_codes[h][:, chunk(c)].bitcast(FP8X4), lhsT_scale=zi_scales[h][:, chunk(c)],
+                rhs=wi_codes[:, h, :].bitcast(FP4X4), rhs_scale=wi_planes[:, h, :], start=False, stop=False,
+            )
+
+        def zr_second_half(c):
             nc.vector.tensor_tensor(
-                out=zrb[h][:, c * P : (c + 1) * P, :],
-                in0=held["r", h, c][:].rearrange("p t j -> p j t"),
-                in1=gre[:, h, :].unsqueeze(1).to_broadcast([P, P, PACK]),
+                out=zr_woven[1][:, chunk(c), :],
+                in0=re_sums[c][:].rearrange("p t j -> p j t"),
+                in1=gain_re[:, 1, :].unsqueeze(1).to_broadcast([P, P, PACK]),
                 op=MULT,
             )
 
-        def re_plane(h, t):
-            b = bank([P, S2], "x")
-            for a in range(2):
-                stage1(b[:], a, a, h, t, slice(0, S2), a == 0, a == 1)
-            nc.scalar.activation(out=zrp[h][:, t, :], in_=b[:], func=COPY, scale=gre[:, h, t : t + 1])
-
-        def stage2(kind, h, c, start, stop):
-            if start:
-                acc[c] = bank([P, N], "x")
-            m = slice(c * P, (c + 1) * P)
-            if kind == "r":
-                nc.tensor.matmul_mx(
-                    out=acc[c][:], lhsT=zrq[h][:, m].bitcast(FP8X4), lhsT_scale=zrs[h][:, m],
-                    rhs=wq[h][:].bitcast(FP8X4), rhs_scale=ws[h][:], start=start, stop=stop,
-                )
-            else:
-                nc.tensor.matmul_mx(
-                    out=acc[c][:], lhsT=ziq[h][:, m].bitcast(FP8X4), lhsT_scale=zis[h][:, m],
-                    rhs=wiw[:, h, :].bitcast(FP4X4), rhs_scale=wis[:, h, :], start=start, stop=stop,
-                )
-
-        def y_scale(c):
-            nc.scalar.activation(
-                out=yt[c][:], in_=acc[c][:].rearrange("p (m t) -> p t m", t=PACK), func=COPY, scale=pw[:, c : c + 1]
-            )
-
-        def y_scale_v(c):
-            nc.vector.tensor_scalar(
-                out=yt[c][:], in0=acc[c][:].rearrange("p (m t) -> p t m", t=PACK), scalar1=pw[:, c : c + 1], scalar2=None,
-                op0=MULT,
-            )
-
-        def y_turn(c, eng):
-            b = bank([P, PACK, P], "y")
-            for t in range(PACK):
-                nc.tensor.transpose(b[:, t, :], yt[c][:, t, :], ident[:])
-            if eng == "s":
-                nc.scalar.copy(out=yf[c][:], in_=b[:])
-            else:
-                nc.vector.tensor_copy(out=yf[c][:], in_=b[:])
-
-        def y_turn_mm(c):
-            b = bank([P, PACK, P], "y")
-            for t in range(PACK):
-                nc.tensor.transpose(b[:, t, :], yt[c][:, t, :], ident[:])
-            held["y", c] = b
-
-        def y_out(c, eng):
-            if eng == "s":
-                nc.scalar.copy(out=yf[c][:], in_=held["y", c][:])
-            else:
-                nc.vector.tensor_copy(out=yf[c][:], in_=held["y", c][:])
-
-        def y_round(c):
-            nc.vector.tensor_copy(out=yb[c][:], in_=held["y", c][:].rearrange("p t j -> p j t"))
-
-        def y_store(c):
-            nc.sync.dma_start(
-                out=out_0.rearrange("(p t) j -> p t j", t=PACK)[:, :, c * P : (c + 1) * P], in_=yf[c][:]
-            )
-
-        def y_quant(c):
+        def quantise_y(c):
             nc.vector.quantize_mx(
-                out=yq[:, c * P : (c + 1) * P].bitcast(FP8X4), scales=ys[:, c * P : (c + 1) * P],
-                in_=yb[c][:].rearrange("p j t -> p (j t)"),
+                out=y_codes[:, chunk(c)].bitcast(FP8X4), scales=y_scales[:, chunk(c)],
+                in_=y_woven[c][:].rearrange("p j t -> p (j t)"),
             )
 
-        def store_codes(lo, hi):
+        def store_codes(cols):
             nc.sync.dma_start(
-                out=out_1[0].rearrange("p m t -> p (m t)").bitcast(I32)[:, lo:hi], in_=yq[:, lo:hi].bitcast(I32)
+                out=out_1[0].rearrange("p m t -> p (m t)").bitcast(I32)[:, cols], in_=y_codes[:, cols].bitcast(I32)
             )
 
-        def store_planes():
-            for q in range(4):
-                eng = nc.scalar if q % 2 else nc.sync
-                eng.dma_start(out=out_2[0, 4 * q : 4 * q + 4, :].bitcast(I32), in_=ys[32 * q : 32 * q + 4, :].bitcast(I32))
+        halves = range(2)
+        everyone = slice(0, S2)
+        idx = keep.tile([P, S // 16], U16, name="idx")
+        idx2 = keep.tile([P, S2 // 16], U16, name="idx2")
+        u_words = [own("u_words%d" % a, [P, S2], U32) for a in (REAL, IMAG)]
+        u_scales = own("u_scales", [P, S2], U8)
+        v_scales = [own("v_scales%d" % h, [P, PASS], U8) for h in halves]
+        gain_re = own("gain_re", [P, 2, PACK], F32)
+        gain_im = own("gain_im", [P, 2, PACK], F32)
+        wr_scales = [own("wr_scales%d" % h, [P, N], U8) for h in halves]
+        zr_slices = own("zr_slices", [P, PACK, S2], BF16)
+        zi_slices = [own("zi_slices%d" % h, [P, PACK, S2], BF16) for h in halves]
+        zr_woven = [own("zr_woven%d" % h, [P, S2, PACK], BF16) for h in halves]
+        zi_woven = [own("zi_woven%d" % h, [P, S2, PACK], BF16) for h in halves]
+        zr_scales = [own("zr_scales%d" % h, [P, S2], U8) for h in halves]
+        zi_scales = [own("zi_scales%d" % h, [P, S2], U8) for h in halves]
+        zi_codes = [own("zi_codes%d" % h, [P, S2], U32) for h in halves]
+        y_t = [own("y_t%d" % c, [P, PACK, P], F32) for c in range(CHUNKS)]
+        y_rows = [own("y_rows%d" % c, [P, PACK, P], F32) for c in range(CHUNKS)]
+        y_woven = [own("y_woven%d" % c, [P, P, PACK], BF16) for c in range(CHUNKS)]
+        y_codes = own("y_codes", [P, S2], U32)
+        y_scales = own("y_scales", [P, S2], U8)
+        ident = own("ident", [P, P], F32)
+        product = [
+            [at(AT_PRODUCT + 2 * KB * (PACK * h + t), "product%d_%d" % (h, t), [P, S2], F32) for t in range(PACK)]
+            for h in halves
+        ]
+        u_table_real = at(AT_V_REAL, "u_table_real", [P, T2], U32)
+        v_table_imag = at(AT_V_IMAG, "v_table_imag", [P, T], U32)
+        u_scale_table = at(AT_WR + 8 * KB - 512, "u_scale_table", [P, T2], U8)
+        v_scale_table = at(AT_V_SCALES, "v_scale_table", [P, T], U8)
+        v_scales_listed = [at(AT_V_FIRST - 256, "v_scales_listed0", [P, PASS], U8)]
+        v_words = {(REAL, 0): own("v_words_real0", [P, PASS], U32)}
 
-        RA, RB, RC, RD, RE, RF, RG = 0, 8192, 12800, 20992, 29184, 37376, 39424
-        vtab, utab, wraw, uw, vsg, zib, zrb, wq = {}, {}, {}, {}, {}, {}, {}, {}
-        vw = [{}, {}]
-        vwg = [{}, {}]
-        ga = [{}, {}]
-        vsg[0] = reuse("vsg0", [P, PASS], U8, RB - 256)
-        utab[0] = reuse("utab0", [P, T2], U32, RC - 64)
-        vtab[1] = reuse("vtab1", [P, T], U32, RE)
-        vstab = reuse("vstab", [P, T], U8, RD)
-        ustab = reuse("ustab", [P, T2], U8, RG)
-        uw[0] = sb("uw0", [P, S2], U32)
-        uw[1] = sb("uw1", [P, S2], U32)
-        vw[0][0] = sb("vw00", [P, PASS], U32)
-        vw[1][0] = sb("vw10", [P, PASS], U32)
-        vw[0][1] = sb("vw01", [P, PASS], U32)
-        vw[1][1] = sb("vw11", [P, PASS], U32)
-        vwg[0][0] = sb("vwg00", [P, PASS], U32)
-        vwg[1][0] = sb("vwg10", [P, PASS], U32)
-        zrb[0] = sb("zrb0", [P, S2, PACK], BF16)
-        zrb[1] = sb("zrb1", [P, S2, PACK], BF16)
-        zib[0] = sb("zib0", [P, S2, PACK], BF16)
-        zib[1] = sb("zib1", [P, S2, PACK], BF16)
-        nc.gpsimd.memset(vstab[:].bitcast(I32), 0)
-        nc.vector.memset(ustab[:].bitcast(I32), 0)
+        nc.gpsimd.memset(v_scale_table[:].bitcast(I32), 0)
+        nc.vector.memset(u_scale_table[:].bitcast(I32), 0)
 
         nc.sync.dma_start(idx2[:], offs2)
         nc.sync.dma_start(idx[:], offs)
-        load_words(utab[0], tab2_words[0])
-        nc.gpsimd.dma_start(out=vtab[1][:].bitcast(I32), in_=tab_words[1].rearrange("p t i -> p (t i)").bitcast(I32))
-        load_planes([nc.sync] * 4, vstab, tab_scales)
-        load_planes([nc.sync] * 4, ustab, tab2_scales)
+        load_words(nc.sync, u_table_real, tab2_words[REAL])
+        load_words(nc.gpsimd, v_table_imag, tab_words[IMAG])
+        load_table_scales(v_scale_table, tab_scales)
+        load_table_scales(u_scale_table, tab2_scales)
+        load_gains(gain_im, g_im)
         make_identity(nc, ident[:])
+        load_gains(gain_re, g_re)
 
-        gather_uw(0)
-        gim = reuse("gim", [P, 2, PACK], F32, RC - 64)
-        wraw[0] = reuse("wraw0", [P, PACK, N], F32, RC)
-        load_wr(0)
-        load_g(gim, g_im)
-        gather_vs(0)
-        gather_vw_plain(1, 0)
-        deal_vs(0)
-        utab[1] = reuse("utab1", [P, T2], U32, RB)
-        vtab[0] = reuse("vtab0", [P, T], U32, RA)
-        load_words(vtab[0], tab_words[0])
-        load_words(utab[1], tab2_words[1])
-        gather_us()
-        deal_vw(1, 0)
-        weave("s", wbf[0], wraw[0], 0, N)
-        for t in range(PACK):
-            ga[0][t] = reuse("ga0_%d" % t, [P, S2], F32, RC + 2048 * t)
-            im_first(0, t)
-        gre = reuse("gre", [P, 2, PACK], F32, RG)
-        load_g(gre, g_re)
-        vsg[1] = reuse("vsg1", [P, PASS], U8, RG + 64)
-        gather_vs(1)
-        wraw[1] = reuse("wraw1", [P, PACK, N], F32, RD)
-        load_wr(1)
-        gather_vw_plain(0, 0)
-        deal_vs(1)
-        gather_uw(1)
-        deal_vw(0, 0)
-        for t in range(PACK):
-            re_plane(0, t)
-        for t in range(PACK):
-            im_second_mm(0, t)
-        weave("s", zrb[0], zrp[0], 0, S2)
-        vwg[1][1] = reuse("vwg11", [P, PASS], U32, RB)
-        vwg[0][1] = reuse("vwg01", [P, PASS], U32, RB + 2048)
-        gather_vw_plain(1, 1)
-        gather_vw_plain(0, 1)
-        deal_vw(1, 1)
-        wiw = reuse("wiw", [P, 2, 2 * N], U8, RG + 64)
-        wis = reuse("wis", [P, 2, N], U8, RE)
-        pw = reuse("pw", [P, CH], F32, RE + 1024)
-        nc.gpsimd.memset(wis[:].bitcast(I32), 0)
-        load_wi()
-        load_power()
-        for t in range(PACK):
-            ga[1][t] = sb("ga1_%d" % t, [P, S2], F32)
-            im_first(1, t)
+        nc.vector.tensor_copy(u_words[REAL][:], u_table_real[:].indirect(idx2[:]))
+        v_table_real = at(AT_V_REAL, "v_table_real", [P, T], U32)
+        load_words(nc.sync, v_table_real, tab_words[REAL])
+        nc.vector.tensor_copy(v_scales_listed[0][:], v_scale_table[:].indirect(half_list(0)))
+        deal_v_scales(0)
+        u_table_imag = at(AT_LATE + 512, "u_table_imag", [P, T2], U32)
+        v_words[IMAG, 0] = at(AT_V_FIRST, "v_words_imag0", [P, PASS], U32)
+        load_words(nc.sync, u_table_imag, tab2_words[IMAG])
+        gather_v_words(v_words[IMAG, 0], v_table_imag, 0)
+        nc.vector.tensor_copy(u_scales[:], u_scale_table[:].indirect(idx2[:]))
+        wr_rows = [at(AT_WR + 8 * KB * h, "wr_rows%d" % h, [P, PACK, N], F32) for h in halves]
+        for h in halves:
+            nc.sync.dma_start(
+                out=wr_rows[h][:], in_=wr[h * PASS : (h + 1) * PASS, :].rearrange("(p t) n -> p t n", t=PACK)
+            )
+        im_first_product(0)
+        gather_v_words(v_words[REAL, 0], v_table_real, 0)
+        nc.vector.tensor_copy(u_words[IMAG][:], u_table_imag[:].indirect(idx2[:]))
 
-        deal_vw(0, 1)
-        wq[0] = reuse("wq0", [P, N], U32, RA)
-        wq[1] = reuse("wq1", [P, N], U32, RA + 2048)
         for t in range(PACK):
-            im_second(0, t)
-        weave("s", zib[0], zip_[0], 0, S2)
-        wbf[1] = reuse("wbf1", [P, N, PACK], BF16, RC)
-        weave("s", wbf[1], wraw[1], 0, N)
-        quant(wq[0], ws[0], wbf[0], 0, N)
-        quant(zrq[0], zrs[0], zrb[0], 0, S2)
-        for t in range(PACK):
-            im_second_mm(1, t)
-            im_second(1, t)
-        for c in range(CH):
-            stage2("r", 0, c, True, False)
-        for c in range(CH):
-            re_mm(1, c)
-        quant(ziq[0], zis[0], zib[0], 0, S2)
-        for c in range(CH):
-            stage2("i", 0, c, False, False)
-        weave("v", zib[1], zip_[1], 0, S2)
-        re_out(1, 0)
-        quant(ziq[1], zis[1], zib[1], 0, S2)
-        for c in range(CH):
-            stage2("i", 1, c, False, False)
-        quant(wq[1], ws[1], wbf[1], 0, N)
-        for c in range(CH):
-            if c + 1 < CH:
-                re_out(1, c + 1)
-            quant(zrq[1], zrs[1], zrb[1], c * P, (c + 1) * P)
-            stage2("r", 1, c, False, True)
-        for c in range(CH):
-            if "sssv"[c] == "s":
-                y_scale(c)
+            sums = bank("s", [P, S2])
+            for a in (REAL, IMAG):
+                first_stage(sums[:], a, a, 0, t, everyone, a == REAL, a == IMAG)
+            nc.scalar.activation(out=zr_slices[:, t, :], in_=sums[:], func=COPY, scale=gain_re[:, 0, t : t + 1])
+        second_products = im_second_product(0)
+        weave(nc.scalar.copy, zr_woven[0], zr_slices, everyone)
+
+        v_words[IMAG, 1] = at(AT_LATE, "v_words_imag1", [P, PASS], U32)
+        v_scales_listed.append(at(AT_LATE + 2 * KB, "v_scales_listed1", [P, PASS], U8))
+        v_words[REAL, 1] = at(AT_LATE + 2 * KB + 512, "v_words_real1", [P, PASS], U32)
+        nc.vector.tensor_copy(v_scales_listed[1][:], v_scale_table[:].indirect(half_list(1)))
+        gather_v_words(v_words[IMAG, 1], v_table_imag, 1)
+        deal_v_scales(1)
+        wi_codes = at(AT_V_SCALES, "wi_codes", [P, 2, 2 * N], U8)
+        im_first_product(1)
+        gather_v_words(v_words[REAL, 1], v_table_real, 1)
+
+        wr_woven = [at(AT_V_REAL, "wr_woven0", [P, N, PACK], BF16), own("wr_woven1", [P, N, PACK], BF16)]
+        wi_planes = at(AT_V_IMAG, "wi_planes", [P, 2, N], U8)
+        nc.gpsimd.memset(wi_planes[:].bitcast(I32), 0)
+        for c in range(CHUNKS):
+            nc.gpsimd.tensor_scalar(
+                out=wr_woven[0][:, chunk(c), :], in0=wr_rows[0][:, :, chunk(c)].rearrange("p t n -> p n t"),
+                scalar1=1.0, scalar2=0.0, op0=MULT, op1=ADD,
+            )
+        nc.sync.dma_start(out=wi_codes[:].bitcast(I32), in_=wi_words.bitcast(I32).rearrange("a p n -> p a n"))
+        for q in range(4):
+            nc.sync.dma_start(
+                out=wi_planes[32 * q : 32 * q + 4, :, :].bitcast(I32),
+                in_=wi_scales[:, 4 * q : 4 * q + 4, :].bitcast(I32).rearrange("a r n -> r a n"),
+            )
+        user_power = at(AT_V_REAL + 4 * KB, "user_power", [P, CHUNKS], F32)
+        with nc.allow_non_contiguous_dma(reason="one factor for each partition and chunk"):
+            nc.sync.dma_start(out=user_power[:], in_=power.rearrange("(c p) -> p c", p=P))
+
+        later_products = im_second_product(1)
+        minus_zi(0, second_products)
+        weave(nc.scalar.copy, zi_woven[0], zi_slices[0], everyone)
+        weave(nc.scalar.copy, wr_woven[1], wr_rows[1], slice(0, N))
+        minus_zi(1, later_products)
+
+        wr_codes = [at(AT_PRODUCT + 14 * KB, "wr_codes0", [P, N], U32), own("wr_codes1", [P, N], U32)]
+        zr_codes = [at(AT_PRODUCT + 12 * KB, "zr_codes0", [P, S2], U32), own("zr_codes1", [P, S2], U32)]
+        quantise(wr_codes[0], wr_scales[0], wr_woven[0], slice(0, N))
+        quantise(zr_codes[0], zr_scales[0], zr_woven[0], everyone)
+        y_t_sums = []
+        for c in range(CHUNKS):
+            y_t_sums.append(bank("s", [P, N]))
+            real_pass(c, 0, True, False)
+        re_sums = []
+        for c in range(CHUNKS):
+            re_sums.append(bank("v", [P, PACK, P]))
+            for t in range(PACK):
+                for a in (REAL, IMAG):
+                    first_stage(re_sums[c][:, t, :], a, a, 1, t, chunk(c), a == REAL, a == IMAG)
+        weave(nc.vector.tensor_copy, zi_woven[1], zi_slices[1], slice(0, S2 // 2))
+        weave(nc.scalar.copy, zi_woven[1], zi_slices[1], slice(S2 // 2, S2))
+        quantise(zi_codes[0], zi_scales[0], zi_woven[0], everyone)
+        for c in range(CHUNKS):
+            imag_pass(c, 0)
+        quantise(wr_codes[1], wr_scales[1], wr_woven[1], slice(0, N))
+
+        zr_second_half(0)
+        for c in range(CHUNKS):
+            if c % 2 == 0:
+                quantise(zi_codes[1], zi_scales[1], zi_woven[1], slice(c * P, (c + 2) * P))
+            if c + 1 < CHUNKS:
+                zr_second_half(c + 1)
+            quantise(zr_codes[1], zr_scales[1], zr_woven[1], chunk(c))
+            imag_pass(c, 1)
+            real_pass(c, 1, False, True)
+
+        for c in range(CHUNKS):
+            dealt = y_t_sums[c][:].rearrange("p (m t) -> p t m", t=PACK)
+            if c < SCALED_ON_SCALAR:
+                nc.scalar.activation(out=y_t[c][:], in_=dealt, func=COPY, scale=user_power[:, c : c + 1])
             else:
-                y_scale_v(c)
-            y_turn_mm(c)
-            y_out(c, "s")
-            weave("v", yb[c], yf[c], 0, P)
-            y_store(c)
-            if c:
-                y_quant(c - 1)
-        store_codes(0, S2 - P)
-        y_quant(CH - 1)
-        store_codes(S2 - P, S2)
-        store_planes()
+                nc.vector.tensor_scalar(
+                    out=y_t[c][:], in0=dealt, scalar1=user_power[:, c : c + 1], scalar2=None, op0=MULT
+                )
+            turned = bank("v", [P, PACK, P])
+            for t in range(PACK):
+                nc.tensor.transpose(turned[:, t, :], y_t[c][:, t, :], ident[:])
+            nc.scalar.copy(out=y_rows[c][:], in_=turned[:])
+            weave(nc.vector.tensor_copy, y_woven[c], y_rows[c], slice(0, P))
+            nc.sync.dma_start(out=out_0.rearrange("(p t) j -> p t j", t=PACK)[:, :, chunk(c)], in_=y_rows[c][:])
+            if c > 0:
+                quantise_y(c - 1)
+        store_codes(slice(0, S2 - P))
+        quantise_y(CHUNKS - 1)
+        store_codes(slice(S2 - P, S2))
+        for q in range(4):
+            queue = nc.scalar if q % 2 else nc.sync
+            queue.dma_start(
+                out=out_2[0, 4 * q : 4 * q + 4, :].bitcast(I32), in_=y_scales[32 * q : 32 * q + 4, :].bitcast(I32)
+            )

@@ -28,13 +28,15 @@ REAL, IMAG = 0, 1
 SCALED_ON_SCALAR = 2
 
 KB = 1024
-AT_V_REAL = 0
-AT_V_IMAG = 8 * KB
-AT_WR = 16 * KB
-AT_LATE = 32 * KB
-AT_V_FIRST = AT_LATE + 4 * KB + 512
-AT_V_SCALES = 40 * KB
-AT_PRODUCT = 42 * KB
+AT_LISTED = 2 * KB - 256
+AT_V_REAL = 2 * KB + 192
+AT_U_REAL = 11 * KB
+AT_LATE = AT_U_REAL + 2 * KB
+AT_U_SCALES = 18 * KB
+AT_WR = 21 * KB
+AT_V_IMAG = 37 * KB
+AT_V_SCALES = AT_WR + 7 * KB
+AT_PRODUCT = 45 * KB
 
 
 def tile_list_mimo_beam_channel_kernel(
@@ -69,7 +71,7 @@ def tile_list_mimo_beam_channel_kernel(
                 )
 
         def load_gains(gains, src):
-            nc.gpsimd.dma_start(out=gains[:], in_=src.rearrange("(h p t) -> p h t", h=2, t=PACK))
+            nc.sync.dma_start(out=gains[:], in_=src.rearrange("(h p t) -> p h t", h=2, t=PACK))
 
         def half_list(h):
             return idx[:, h * (PASS // 16) : (h + 1) * (PASS // 16)]
@@ -94,16 +96,16 @@ def tile_list_mimo_beam_channel_kernel(
                 stop=stop,
             )
 
-        def im_first_product(h):
+        def im_first_product(h, ring):
             for t in range(PACK):
-                sums = bank("s", [P, S2])
+                sums = bank(ring, [P, S2])
                 first_stage(sums[:], IMAG, REAL, h, t, slice(0, S2), True, True)
                 nc.scalar.activation(out=product[h][t][:], in_=sums[:], func=COPY, scale=gain_im[:, h, t : t + 1])
 
         def im_second_product(h):
             banks = []
             for t in range(PACK):
-                banks.append(bank("v", [P, S2]))
+                banks.append(bank("y", [P, S2]))
                 first_stage(banks[t][:], REAL, IMAG, h, t, slice(0, S2), True, True)
             return banks
 
@@ -160,16 +162,14 @@ def tile_list_mimo_beam_channel_kernel(
         everyone = slice(0, S2)
         idx = keep.tile([P, S // 16], U16, name="idx")
         idx2 = keep.tile([P, S2 // 16], U16, name="idx2")
-        u_words = [own("u_words%d" % a, [P, S2], U32) for a in (REAL, IMAG)]
+        u_words = {IMAG: own("u_words_imag", [P, S2], U32)}
         u_scales = own("u_scales", [P, S2], U8)
-        v_scales = [own("v_scales%d" % h, [P, PASS], U8) for h in halves]
-        gain_re = own("gain_re", [P, 2, PACK], F32)
-        gain_im = own("gain_im", [P, 2, PACK], F32)
         wr_scales = [own("wr_scales%d" % h, [P, N], U8) for h in halves]
         zr_slices = own("zr_slices", [P, PACK, S2], BF16)
         zi_slices = [own("zi_slices%d" % h, [P, PACK, S2], BF16) for h in halves]
         zr_woven = [own("zr_woven%d" % h, [P, S2, PACK], BF16) for h in halves]
-        zi_woven = [own("zi_woven%d" % h, [P, S2, PACK], BF16) for h in halves]
+        zi_woven = [own("zi_woven0", [P, S2, PACK], BF16)]
+        zi_late = [own("zi_late0", [P, S2 // 2, PACK], BF16)]
         zr_scales = [own("zr_scales%d" % h, [P, S2], U8) for h in halves]
         zi_scales = [own("zi_scales%d" % h, [P, S2], U8) for h in halves]
         zi_codes = [own("zi_codes%d" % h, [P, S2], U32) for h in halves]
@@ -183,66 +183,67 @@ def tile_list_mimo_beam_channel_kernel(
             [at(AT_PRODUCT + 2 * KB * (PACK * h + t), "product%d_%d" % (h, t), [P, S2], F32) for t in range(PACK)]
             for h in halves
         ]
-        u_table_real = at(AT_V_REAL, "u_table_real", [P, T2], U32)
+        u_table_real = at(AT_U_REAL, "u_table_real", [P, T2], U32)
         v_table_imag = at(AT_V_IMAG, "v_table_imag", [P, T], U32)
-        u_scale_table = at(AT_WR + 8 * KB - 512, "u_scale_table", [P, T2], U8)
+        u_scale_table = at(AT_U_SCALES, "u_scale_table", [P, T2], U8)
         v_scale_table = at(AT_V_SCALES, "v_scale_table", [P, T], U8)
-        v_scales_listed = [at(AT_V_FIRST - 256, "v_scales_listed0", [P, PASS], U8)]
+        v_scales_listed = [at(AT_LISTED, "v_scales_listed0", [P, PASS], U8)]
         v_words = {(REAL, 0): own("v_words_real0", [P, PASS], U32)}
 
-        nc.gpsimd.memset(v_scale_table[:].bitcast(I32), 0)
-        nc.vector.memset(u_scale_table[:].bitcast(I32), 0)
-
-        nc.sync.dma_start(idx2[:], offs2)
+        wi_planes = own("wi_planes", [P, 2, N], U8)
+        for table in (v_scale_table, u_scale_table, wi_planes):
+            nc.gpsimd.memset(table[:].bitcast(I32), 0)
         nc.sync.dma_start(idx[:], offs)
-        load_words(nc.sync, u_table_real, tab2_words[REAL])
-        load_words(nc.gpsimd, v_table_imag, tab_words[IMAG])
+        nc.sync.dma_start(idx2[:], offs2)
         load_table_scales(v_scale_table, tab_scales)
         load_table_scales(u_scale_table, tab2_scales)
-        load_gains(gain_im, g_im)
+        load_words(nc.gpsimd, u_table_real, tab2_words[REAL])
+        load_words(nc.gpsimd, v_table_imag, tab_words[IMAG])
         make_identity(nc, ident[:])
-        load_gains(gain_re, g_re)
 
-        nc.vector.tensor_copy(u_words[REAL][:], u_table_real[:].indirect(idx2[:]))
+        nc.vector.tensor_copy(v_scales_listed[0][:], v_scale_table[:].indirect(half_list(0)))
+        nc.vector.tensor_copy(u_scales[:], u_scale_table[:].indirect(idx2[:]))
+        gain_im = at(AT_U_SCALES, "gain_im", [P, 2, PACK], F32)
+        gain_re = at(AT_U_SCALES + 64, "gain_re", [P, 2, PACK], F32)
+        v_scales = [at(AT_U_SCALES + 128, "v_scales0", [P, PASS], U8)]
+        u_words[REAL] = at(AT_U_SCALES + 640, "u_words_real", [P, S2], U32)
+        load_gains(gain_im, g_im)
+        load_gains(gain_re, g_re)
+        deal_v_scales(0)
         v_table_real = at(AT_V_REAL, "v_table_real", [P, T], U32)
         load_words(nc.sync, v_table_real, tab_words[REAL])
-        nc.vector.tensor_copy(v_scales_listed[0][:], v_scale_table[:].indirect(half_list(0)))
-        deal_v_scales(0)
-        u_table_imag = at(AT_LATE + 512, "u_table_imag", [P, T2], U32)
-        v_words[IMAG, 0] = at(AT_V_FIRST, "v_words_imag0", [P, PASS], U32)
+        nc.vector.tensor_copy(u_words[REAL][:], u_table_real[:].indirect(idx2[:]))
+        v_words[IMAG, 0] = at(0, "v_words_imag0", [P, PASS], U32)
+        v_scales_listed.append(at(AT_U_REAL, "v_scales_listed1", [P, PASS], U8))
+        u_table_imag = at(AT_LATE, "u_table_imag", [P, T2], U32)
         load_words(nc.sync, u_table_imag, tab2_words[IMAG])
         gather_v_words(v_words[IMAG, 0], v_table_imag, 0)
-        nc.vector.tensor_copy(u_scales[:], u_scale_table[:].indirect(idx2[:]))
+        im_first_product(0, "x")
+        nc.vector.tensor_copy(v_scales_listed[1][:], v_scale_table[:].indirect(half_list(1)))
         wr_rows = [at(AT_WR + 8 * KB * h, "wr_rows%d" % h, [P, PACK, N], F32) for h in halves]
         for h in halves:
             nc.sync.dma_start(
                 out=wr_rows[h][:], in_=wr[h * PASS : (h + 1) * PASS, :].rearrange("(p t) n -> p t n", t=PACK)
             )
-        im_first_product(0)
         gather_v_words(v_words[REAL, 0], v_table_real, 0)
         nc.vector.tensor_copy(u_words[IMAG][:], u_table_imag[:].indirect(idx2[:]))
-
         for t in range(PACK):
-            sums = bank("s", [P, S2])
+            sums = bank("x", [P, S2])
             for a in (REAL, IMAG):
                 first_stage(sums[:], a, a, 0, t, everyone, a == REAL, a == IMAG)
             nc.scalar.activation(out=zr_slices[:, t, :], in_=sums[:], func=COPY, scale=gain_re[:, 0, t : t + 1])
         second_products = im_second_product(0)
-        weave(nc.scalar.copy, zr_woven[0], zr_slices, everyone)
-
-        v_words[IMAG, 1] = at(AT_LATE, "v_words_imag1", [P, PASS], U32)
-        v_scales_listed.append(at(AT_LATE + 2 * KB, "v_scales_listed1", [P, PASS], U8))
-        v_words[REAL, 1] = at(AT_LATE + 2 * KB + 512, "v_words_real1", [P, PASS], U32)
-        nc.vector.tensor_copy(v_scales_listed[1][:], v_scale_table[:].indirect(half_list(1)))
-        gather_v_words(v_words[IMAG, 1], v_table_imag, 1)
+        v_scales.append(at(AT_LATE + 2 * KB, "v_scales1", [P, PASS], U8))
+        v_words[IMAG, 1] = at(AT_LATE + 2 * KB + 512, "v_words_imag1", [P, PASS], U32)
+        v_words[REAL, 1] = at(AT_LATE, "v_words_real1", [P, PASS], U32)
         deal_v_scales(1)
-        wi_codes = at(AT_V_SCALES, "wi_codes", [P, 2, 2 * N], U8)
-        im_first_product(1)
+        gather_v_words(v_words[IMAG, 1], v_table_imag, 1)
+        im_first_product(1, "x")
+        weave(nc.scalar.copy, zr_woven[0], zr_slices, everyone)
         gather_v_words(v_words[REAL, 1], v_table_real, 1)
+        wi_codes = at(AT_V_IMAG + 2 * KB, "wi_codes", [P, 2, 2 * N], U8)
 
-        wr_woven = [at(AT_V_REAL, "wr_woven0", [P, N, PACK], BF16), own("wr_woven1", [P, N, PACK], BF16)]
-        wi_planes = at(AT_V_IMAG, "wi_planes", [P, 2, N], U8)
-        nc.gpsimd.memset(wi_planes[:].bitcast(I32), 0)
+        wr_woven = [at(AT_V_REAL, "wr_woven0", [P, N, PACK], BF16), None]
         for c in range(CHUNKS):
             nc.gpsimd.tensor_scalar(
                 out=wr_woven[0][:, chunk(c), :], in0=wr_rows[0][:, :, chunk(c)].rearrange("p t n -> p n t"),
@@ -261,6 +262,7 @@ def tile_list_mimo_beam_channel_kernel(
         later_products = im_second_product(1)
         minus_zi(0, second_products)
         weave(nc.scalar.copy, zi_woven[0], zi_slices[0], everyone)
+        wr_woven[1] = at(AT_PRODUCT + 4 * KB, "wr_woven1", [P, N, PACK], BF16)
         weave(nc.scalar.copy, wr_woven[1], wr_rows[1], slice(0, N))
         minus_zi(1, later_products)
 
@@ -270,27 +272,36 @@ def tile_list_mimo_beam_channel_kernel(
         quantise(zr_codes[0], zr_scales[0], zr_woven[0], everyone)
         y_t_sums = []
         for c in range(CHUNKS):
-            y_t_sums.append(bank("s", [P, N]))
+            y_t_sums.append(bank("x", [P, N]))
             real_pass(c, 0, True, False)
         re_sums = []
         for c in range(CHUNKS):
-            re_sums.append(bank("v", [P, PACK, P]))
+            re_sums.append(bank("y", [P, PACK, P]))
             for t in range(PACK):
                 for a in (REAL, IMAG):
                     first_stage(re_sums[c][:, t, :], a, a, 1, t, chunk(c), a == REAL, a == IMAG)
-        weave(nc.vector.tensor_copy, zi_woven[1], zi_slices[1], slice(0, S2 // 2))
-        weave(nc.scalar.copy, zi_woven[1], zi_slices[1], slice(S2 // 2, S2))
+        zi_late.append(at(AT_WR + 8 * KB, "zi_late1", [P, S2 // 2, PACK], BF16))
+        for b, copy in enumerate((nc.vector.tensor_copy, nc.scalar.copy)):
+            copy(
+                out=zi_late[b][:].rearrange("p (c i) t -> p c t i", i=RUN),
+                in_=zi_slices[1][:, :, b * (S2 // 2) : (b + 1) * (S2 // 2)].rearrange("p t (c i) -> p c t i", i=RUN),
+            )
         quantise(zi_codes[0], zi_scales[0], zi_woven[0], everyone)
         for c in range(CHUNKS):
             imag_pass(c, 0)
-        quantise(wr_codes[1], wr_scales[1], wr_woven[1], slice(0, N))
 
         zr_second_half(0)
+        zr_second_half(1)
+        quantise(wr_codes[1], wr_scales[1], wr_woven[1], slice(0, N))
         for c in range(CHUNKS):
             if c % 2 == 0:
-                quantise(zi_codes[1], zi_scales[1], zi_woven[1], slice(c * P, (c + 2) * P))
-            if c + 1 < CHUNKS:
-                zr_second_half(c + 1)
+                pair = slice(c * P, (c + 2) * P)
+                nc.vector.quantize_mx(
+                    out=zi_codes[1][:, pair].bitcast(FP8X4), scales=zi_scales[1][:, pair],
+                    in_=zi_late[c // 2][:].rearrange("p j t -> p (j t)"),
+                )
+            if c + 2 < CHUNKS:
+                zr_second_half(c + 2)
             quantise(zr_codes[1], zr_scales[1], zr_woven[1], chunk(c))
             imag_pass(c, 1)
             real_pass(c, 1, False, True)
@@ -303,7 +314,7 @@ def tile_list_mimo_beam_channel_kernel(
                 nc.vector.tensor_scalar(
                     out=y_t[c][:], in0=dealt, scalar1=user_power[:, c : c + 1], scalar2=None, op0=MULT
                 )
-            turned = bank("v", [P, PACK, P])
+            turned = bank("y", [P, PACK, P])
             for t in range(PACK):
                 nc.tensor.transpose(turned[:, t, :], y_t[c][:, t, :], ident[:])
             nc.scalar.copy(out=y_rows[c][:], in_=turned[:])

@@ -25,18 +25,19 @@ PASS = P * PACK
 CHUNKS = S2 // P
 RUN = 4
 REAL, IMAG = 0, 1
-SCALED_ON_SCALAR = 2
+SCALED_ON_SCALAR = (0, 1)
 
 KB = 1024
-AT_LISTED = 2 * KB - 256
-AT_V_REAL = 2 * KB + 192
+AT_V_REAL = 0
+AT_U_SCALES = 8 * KB - 64
 AT_U_REAL = 11 * KB
 AT_LATE = AT_U_REAL + 2 * KB
-AT_U_SCALES = 18 * KB
+AT_LISTED = 18 * KB
 AT_WR = 21 * KB
 AT_V_IMAG = 37 * KB
 AT_V_SCALES = AT_WR + 7 * KB
 AT_PRODUCT = 45 * KB
+WR_ON_GPSIMD = 1
 
 
 def tile_list_mimo_beam_channel_kernel(
@@ -122,6 +123,21 @@ def tile_list_mimo_beam_channel_kernel(
                 in_=slices[:, :, cols].rearrange("p t (c i) -> p c t i", i=RUN),
             )
 
+        def users(b):
+            return slice(b * (S2 // 2), (b + 1) * (S2 // 2))
+
+        def weave_users(copy, woven, slices, cols):
+            copy(
+                out=woven.rearrange("p (c i) t -> p c t i", i=RUN),
+                in_=slices[:, :, cols].rearrange("p t (c i) -> p c t i", i=RUN),
+            )
+
+        def weave_wr_on_gpsimd(h, c):
+            nc.gpsimd.tensor_scalar(
+                out=wr_woven[h][:, chunk(c), :], in0=wr_rows[h][:, :, chunk(c)].rearrange("p t n -> p n t"),
+                scalar1=1.0, scalar2=0.0, op0=MULT, op1=ADD,
+            )
+
         def quantise(codes, scales, woven, cols):
             nc.vector.quantize_mx(
                 out=codes[:, cols].bitcast(FP8X4), scales=scales[:, cols], in_=woven[:, cols, :].rearrange("p j t -> p (j t)")
@@ -133,10 +149,10 @@ def tile_list_mimo_beam_channel_kernel(
                 rhs=wr_codes[h][:].bitcast(FP8X4), rhs_scale=wr_scales[h][:], start=start, stop=stop,
             )
 
-        def imag_pass(c, h):
+        def imag_pass(c, h, stop=False):
             nc.tensor.matmul_mx(
                 out=y_t_sums[c][:], lhsT=zi_codes[h][:, chunk(c)].bitcast(FP8X4), lhsT_scale=zi_scales[h][:, chunk(c)],
-                rhs=wi_codes[:, h, :].bitcast(FP4X4), rhs_scale=wi_planes[:, h, :], start=False, stop=False,
+                rhs=wi_codes[:, h, :].bitcast(FP4X4), rhs_scale=wi_planes[:, h, :], start=False, stop=stop,
             )
 
         def zr_second_half(c):
@@ -168,8 +184,7 @@ def tile_list_mimo_beam_channel_kernel(
         zr_slices = own("zr_slices", [P, PACK, S2], BF16)
         zi_slices = [own("zi_slices%d" % h, [P, PACK, S2], BF16) for h in halves]
         zr_woven = [own("zr_woven%d" % h, [P, S2, PACK], BF16) for h in halves]
-        zi_woven = [own("zi_woven0", [P, S2, PACK], BF16)]
-        zi_late = [own("zi_late0", [P, S2 // 2, PACK], BF16)]
+        zi_early = {1: own("zi_early1", [P, S2 // 2, PACK], BF16)}
         zr_scales = [own("zr_scales%d" % h, [P, S2], U8) for h in halves]
         zi_scales = [own("zi_scales%d" % h, [P, S2], U8) for h in halves]
         zi_codes = [own("zi_codes%d" % h, [P, S2], U32) for h in halves]
@@ -203,17 +218,17 @@ def tile_list_mimo_beam_channel_kernel(
 
         nc.vector.tensor_copy(v_scales_listed[0][:], v_scale_table[:].indirect(half_list(0)))
         nc.vector.tensor_copy(u_scales[:], u_scale_table[:].indirect(idx2[:]))
-        gain_im = at(AT_U_SCALES, "gain_im", [P, 2, PACK], F32)
-        gain_re = at(AT_U_SCALES + 64, "gain_re", [P, 2, PACK], F32)
-        v_scales = [at(AT_U_SCALES + 128, "v_scales0", [P, PASS], U8)]
-        u_words[REAL] = at(AT_U_SCALES + 640, "u_words_real", [P, S2], U32)
+        gain_im = at(AT_U_SCALES + 64, "gain_im", [P, 2, PACK], F32)
+        gain_re = at(AT_U_SCALES + 128, "gain_re", [P, 2, PACK], F32)
+        v_scales = [at(AT_U_SCALES + 192, "v_scales0", [P, PASS], U8)]
+        u_words[REAL] = at(AT_U_SCALES + 704, "u_words_real", [P, S2], U32)
+        v_table_real = at(AT_V_REAL, "v_table_real", [P, T], U32)
         load_gains(gain_im, g_im)
         load_gains(gain_re, g_re)
-        deal_v_scales(0)
-        v_table_real = at(AT_V_REAL, "v_table_real", [P, T], U32)
         load_words(nc.sync, v_table_real, tab_words[REAL])
+        deal_v_scales(0)
         nc.vector.tensor_copy(u_words[REAL][:], u_table_real[:].indirect(idx2[:]))
-        v_words[IMAG, 0] = at(0, "v_words_imag0", [P, PASS], U32)
+        v_words[IMAG, 0] = at(AT_LISTED, "v_words_imag0", [P, PASS], U32)
         v_scales_listed.append(at(AT_U_REAL, "v_scales_listed1", [P, PASS], U8))
         u_table_imag = at(AT_LATE, "u_table_imag", [P, T2], U32)
         load_words(nc.sync, u_table_imag, tab2_words[IMAG])
@@ -245,10 +260,7 @@ def tile_list_mimo_beam_channel_kernel(
 
         wr_woven = [at(AT_V_REAL, "wr_woven0", [P, N, PACK], BF16), None]
         for c in range(CHUNKS):
-            nc.gpsimd.tensor_scalar(
-                out=wr_woven[0][:, chunk(c), :], in0=wr_rows[0][:, :, chunk(c)].rearrange("p t n -> p n t"),
-                scalar1=1.0, scalar2=0.0, op0=MULT, op1=ADD,
-            )
+            weave_wr_on_gpsimd(0, c)
         nc.sync.dma_start(out=wi_codes[:].bitcast(I32), in_=wi_words.bitcast(I32).rearrange("a p n -> p a n"))
         for q in range(4):
             nc.sync.dma_start(
@@ -261,10 +273,19 @@ def tile_list_mimo_beam_channel_kernel(
 
         later_products = im_second_product(1)
         minus_zi(0, second_products)
-        weave(nc.scalar.copy, zi_woven[0], zi_slices[0], everyone)
+        weave_users(nc.scalar.copy, zi_early[1][:], zi_slices[0], users(1))
         wr_woven[1] = at(AT_PRODUCT + 4 * KB, "wr_woven1", [P, N, PACK], BF16)
-        weave(nc.scalar.copy, wr_woven[1], wr_rows[1], slice(0, N))
+        for c in range(WR_ON_GPSIMD):
+            weave_wr_on_gpsimd(1, c)
+        weave(nc.scalar.copy, wr_woven[1], wr_rows[1], slice(WR_ON_GPSIMD * P, N))
         minus_zi(1, later_products)
+        re_sums = []
+        for c in range(CHUNKS):
+            re_sums.append(bank("y", [P, PACK, P]))
+            for t in range(PACK):
+                for a in (REAL, IMAG):
+                    first_stage(re_sums[c][:, t, :], a, a, 1, t, chunk(c), a == REAL, a == IMAG)
+        zr_second_half(0)
 
         wr_codes = [at(AT_PRODUCT + 14 * KB, "wr_codes0", [P, N], U32), own("wr_codes1", [P, N], U32)]
         zr_codes = [at(AT_PRODUCT + 12 * KB, "zr_codes0", [P, S2], U32), own("zr_codes1", [P, S2], U32)]
@@ -274,41 +295,32 @@ def tile_list_mimo_beam_channel_kernel(
         for c in range(CHUNKS):
             y_t_sums.append(bank("x", [P, N]))
             real_pass(c, 0, True, False)
-        re_sums = []
+        zi_late = at(AT_WR + 8 * KB, "zi_late", [P, S2, PACK], BF16)
         for c in range(CHUNKS):
-            re_sums.append(bank("y", [P, PACK, P]))
-            for t in range(PACK):
-                for a in (REAL, IMAG):
-                    first_stage(re_sums[c][:, t, :], a, a, 1, t, chunk(c), a == REAL, a == IMAG)
-        zi_late.append(at(AT_WR + 8 * KB, "zi_late1", [P, S2 // 2, PACK], BF16))
-        for b, copy in enumerate((nc.vector.tensor_copy, nc.scalar.copy)):
-            copy(
-                out=zi_late[b][:].rearrange("p (c i) t -> p c t i", i=RUN),
-                in_=zi_slices[1][:, :, b * (S2 // 2) : (b + 1) * (S2 // 2)].rearrange("p t (c i) -> p c t i", i=RUN),
+            weave(nc.scalar.copy, zi_late, zi_slices[1], chunk(c))
+        zi_early[0] = at(AT_PRODUCT + 10 * KB, "zi_early0", [P, S2 // 2, PACK], BF16)
+        weave_users(nc.vector.tensor_copy, zi_early[0][:], zi_slices[0], users(0))
+        for b in (1, 0):
+            nc.vector.quantize_mx(
+                out=zi_codes[0][:, users(b)].bitcast(FP8X4), scales=zi_scales[0][:, users(b)],
+                in_=zi_early[b][:].rearrange("p j t -> p (j t)"),
             )
-        quantise(zi_codes[0], zi_scales[0], zi_woven[0], everyone)
+            if b:
+                zr_second_half(1)
         for c in range(CHUNKS):
             imag_pass(c, 0)
-
-        zr_second_half(0)
-        zr_second_half(1)
         quantise(wr_codes[1], wr_scales[1], wr_woven[1], slice(0, N))
         for c in range(CHUNKS):
-            if c % 2 == 0:
-                pair = slice(c * P, (c + 2) * P)
-                nc.vector.quantize_mx(
-                    out=zi_codes[1][:, pair].bitcast(FP8X4), scales=zi_scales[1][:, pair],
-                    in_=zi_late[c // 2][:].rearrange("p j t -> p (j t)"),
-                )
+            quantise(zr_codes[1], zr_scales[1], zr_woven[1], chunk(c))
+            quantise(zi_codes[1], zi_scales[1], zi_late, chunk(c))
             if c + 2 < CHUNKS:
                 zr_second_half(c + 2)
-            quantise(zr_codes[1], zr_scales[1], zr_woven[1], chunk(c))
-            imag_pass(c, 1)
-            real_pass(c, 1, False, True)
+            real_pass(c, 1, False, False)
+            imag_pass(c, 1, True)
 
         for c in range(CHUNKS):
             dealt = y_t_sums[c][:].rearrange("p (m t) -> p t m", t=PACK)
-            if c < SCALED_ON_SCALAR:
+            if c in SCALED_ON_SCALAR:
                 nc.scalar.activation(out=y_t[c][:], in_=dealt, func=COPY, scale=user_power[:, c : c + 1])
             else:
                 nc.vector.tensor_scalar(

@@ -25,19 +25,21 @@ PASS = P * PACK
 CHUNKS = S2 // P
 RUN = 4
 REAL, IMAG = 0, 1
-SCALED_ON_SCALAR = (0, 1)
+ON_VECTOR, ON_SCALAR = 0, 1
+WR_PIECES_ON_GPSIMD = 1
+SCALED_ON_SCALAR = 2
 
 KB = 1024
-AT_V_REAL = 0
-AT_U_SCALES = 8 * KB - 64
-AT_U_REAL = 11 * KB
-AT_LATE = AT_U_REAL + 2 * KB
+AT_U_IMAG = 0
+AT_U_SCALES = 4 * KB - 64
+AT_U_REAL = 7 * KB
+AT_V_REAL = AT_U_REAL + 2 * KB + 512
 AT_LISTED = 18 * KB
 AT_WR = 21 * KB
-AT_V_IMAG = 37 * KB
 AT_V_SCALES = AT_WR + 7 * KB
+AT_V_IMAG = 37 * KB
 AT_PRODUCT = 45 * KB
-WR_ON_GPSIMD = 1
+SLICE = 2 * KB
 
 
 def tile_list_mimo_beam_channel_kernel(
@@ -61,6 +63,9 @@ def tile_list_mimo_beam_channel_kernel(
 
         def chunk(c):
             return slice(c * P, (c + 1) * P)
+
+        def user_half(b):
+            return slice(b * (S2 // 2), (b + 1) * (S2 // 2))
 
         def load_words(queue, table, src):
             queue.dma_start(out=table[:].bitcast(I32), in_=src.rearrange("p t i -> p (t i)").bitcast(I32))
@@ -100,15 +105,13 @@ def tile_list_mimo_beam_channel_kernel(
         def im_first_product(h, ring):
             for t in range(PACK):
                 sums = bank(ring, [P, S2])
-                first_stage(sums[:], IMAG, REAL, h, t, slice(0, S2), True, True)
+                first_stage(sums[:], IMAG, REAL, h, t, everyone, True, True)
                 nc.scalar.activation(out=product[h][t][:], in_=sums[:], func=COPY, scale=gain_im[:, h, t : t + 1])
 
-        def im_second_product(h):
-            banks = []
-            for t in range(PACK):
-                banks.append(bank("y", [P, S2]))
-                first_stage(banks[t][:], REAL, IMAG, h, t, slice(0, S2), True, True)
-            return banks
+        def im_second_product(h, t, ring):
+            sums = bank(ring, [P, S2])
+            first_stage(sums[:], REAL, IMAG, h, t, everyone, True, True)
+            return sums
 
         def minus_zi(h, banks):
             for t in range(PACK):
@@ -117,19 +120,10 @@ def tile_list_mimo_beam_channel_kernel(
                     op0=MULT, op1=SUB,
                 )
 
-        def weave(copy, woven, slices, cols):
-            copy(
-                out=woven[:, cols, :].rearrange("p (c i) t -> p c t i", i=RUN),
-                in_=slices[:, :, cols].rearrange("p t (c i) -> p c t i", i=RUN),
-            )
-
-        def users(b):
-            return slice(b * (S2 // 2), (b + 1) * (S2 // 2))
-
-        def weave_users(copy, woven, slices, cols):
+        def weave(copy, woven, slices):
             copy(
                 out=woven.rearrange("p (c i) t -> p c t i", i=RUN),
-                in_=slices[:, :, cols].rearrange("p t (c i) -> p c t i", i=RUN),
+                in_=slices.rearrange("p t (c i) -> p c t i", i=RUN),
             )
 
         def weave_wr_on_gpsimd(h, c):
@@ -138,18 +132,16 @@ def tile_list_mimo_beam_channel_kernel(
                 scalar1=1.0, scalar2=0.0, op0=MULT, op1=ADD,
             )
 
-        def quantise(codes, scales, woven, cols):
-            nc.vector.quantize_mx(
-                out=codes[:, cols].bitcast(FP8X4), scales=scales[:, cols], in_=woven[:, cols, :].rearrange("p j t -> p (j t)")
-            )
+        def quantise(codes, scales, woven):
+            nc.vector.quantize_mx(out=codes.bitcast(FP8X4), scales=scales, in_=woven.rearrange("p j t -> p (j t)"))
 
-        def real_pass(c, h, start, stop):
+        def real_pass(c, h, start):
             nc.tensor.matmul_mx(
                 out=y_t_sums[c][:], lhsT=zr_codes[h][:, chunk(c)].bitcast(FP8X4), lhsT_scale=zr_scales[h][:, chunk(c)],
-                rhs=wr_codes[h][:].bitcast(FP8X4), rhs_scale=wr_scales[h][:], start=start, stop=stop,
+                rhs=wr_codes[h][:].bitcast(FP8X4), rhs_scale=wr_scales[h][:], start=start, stop=False,
             )
 
-        def imag_pass(c, h, stop=False):
+        def imag_pass(c, h, stop):
             nc.tensor.matmul_mx(
                 out=y_t_sums[c][:], lhsT=zi_codes[h][:, chunk(c)].bitcast(FP8X4), lhsT_scale=zi_scales[h][:, chunk(c)],
                 rhs=wi_codes[:, h, :].bitcast(FP4X4), rhs_scale=wi_planes[:, h, :], start=False, stop=stop,
@@ -158,16 +150,13 @@ def tile_list_mimo_beam_channel_kernel(
         def zr_second_half(c):
             nc.vector.tensor_tensor(
                 out=zr_woven[1][:, chunk(c), :],
-                in0=re_sums[c][:].rearrange("p t j -> p j t"),
+                in0=re_second[c][:].rearrange("p t j -> p j t"),
                 in1=gain_re[:, 1, :].unsqueeze(1).to_broadcast([P, P, PACK]),
                 op=MULT,
             )
 
         def quantise_y(c):
-            nc.vector.quantize_mx(
-                out=y_codes[:, chunk(c)].bitcast(FP8X4), scales=y_scales[:, chunk(c)],
-                in_=y_woven[c][:].rearrange("p j t -> p (j t)"),
-            )
+            quantise(y_codes[:, chunk(c)], y_scales[:, chunk(c)], y_woven[c][:])
 
         def store_codes(cols):
             nc.sync.dma_start(
@@ -178,13 +167,12 @@ def tile_list_mimo_beam_channel_kernel(
         everyone = slice(0, S2)
         idx = keep.tile([P, S // 16], U16, name="idx")
         idx2 = keep.tile([P, S2 // 16], U16, name="idx2")
-        u_words = {IMAG: own("u_words_imag", [P, S2], U32)}
         u_scales = own("u_scales", [P, S2], U8)
         wr_scales = [own("wr_scales%d" % h, [P, N], U8) for h in halves]
         zr_slices = own("zr_slices", [P, PACK, S2], BF16)
         zi_slices = [own("zi_slices%d" % h, [P, PACK, S2], BF16) for h in halves]
         zr_woven = [own("zr_woven%d" % h, [P, S2, PACK], BF16) for h in halves]
-        zi_early = {1: own("zi_early1", [P, S2 // 2, PACK], BF16)}
+        zi_first_woven = {ON_SCALAR: own("zi_first_woven_scalar", [P, S2 // 2, PACK], BF16)}
         zr_scales = [own("zr_scales%d" % h, [P, S2], U8) for h in halves]
         zi_scales = [own("zi_scales%d" % h, [P, S2], U8) for h in halves]
         zi_codes = [own("zi_codes%d" % h, [P, S2], U32) for h in halves]
@@ -195,7 +183,7 @@ def tile_list_mimo_beam_channel_kernel(
         y_scales = own("y_scales", [P, S2], U8)
         ident = own("ident", [P, P], F32)
         product = [
-            [at(AT_PRODUCT + 2 * KB * (PACK * h + t), "product%d_%d" % (h, t), [P, S2], F32) for t in range(PACK)]
+            [at(AT_PRODUCT + SLICE * (PACK * h + t), "product%d_%d" % (h, t), [P, S2], F32) for t in range(PACK)]
             for h in halves
         ]
         u_table_real = at(AT_U_REAL, "u_table_real", [P, T2], U32)
@@ -204,10 +192,11 @@ def tile_list_mimo_beam_channel_kernel(
         v_scale_table = at(AT_V_SCALES, "v_scale_table", [P, T], U8)
         v_scales_listed = [at(AT_LISTED, "v_scales_listed0", [P, PASS], U8)]
         v_words = {(REAL, 0): own("v_words_real0", [P, PASS], U32)}
-
         wi_planes = own("wi_planes", [P, 2, N], U8)
-        for table in (v_scale_table, u_scale_table, wi_planes):
-            nc.gpsimd.memset(table[:].bitcast(I32), 0)
+
+        for scale_tile in (v_scale_table, u_scale_table, wi_planes):
+            nc.gpsimd.memset(scale_tile[:].bitcast(I32), 0)
+
         nc.sync.dma_start(idx[:], offs)
         nc.sync.dma_start(idx2[:], offs2)
         load_table_scales(v_scale_table, tab_scales)
@@ -221,44 +210,50 @@ def tile_list_mimo_beam_channel_kernel(
         gain_im = at(AT_U_SCALES + 64, "gain_im", [P, 2, PACK], F32)
         gain_re = at(AT_U_SCALES + 128, "gain_re", [P, 2, PACK], F32)
         v_scales = [at(AT_U_SCALES + 192, "v_scales0", [P, PASS], U8)]
-        u_words[REAL] = at(AT_U_SCALES + 704, "u_words_real", [P, S2], U32)
-        v_table_real = at(AT_V_REAL, "v_table_real", [P, T], U32)
+        u_words = {REAL: at(AT_U_SCALES + 192 + PASS, "u_words_real", [P, S2], U32)}
+        u_table_imag = at(AT_U_IMAG, "u_table_imag", [P, T2], U32)
         load_gains(gain_im, g_im)
         load_gains(gain_re, g_re)
-        load_words(nc.sync, v_table_real, tab_words[REAL])
+        load_words(nc.sync, u_table_imag, tab2_words[IMAG])
         deal_v_scales(0)
         nc.vector.tensor_copy(u_words[REAL][:], u_table_real[:].indirect(idx2[:]))
         v_words[IMAG, 0] = at(AT_LISTED, "v_words_imag0", [P, PASS], U32)
         v_scales_listed.append(at(AT_U_REAL, "v_scales_listed1", [P, PASS], U8))
-        u_table_imag = at(AT_LATE, "u_table_imag", [P, T2], U32)
-        load_words(nc.sync, u_table_imag, tab2_words[IMAG])
+        v_table_real = at(AT_V_REAL, "v_table_real", [P, T], U32)
+        load_words(nc.sync, v_table_real, tab_words[REAL])
         gather_v_words(v_words[IMAG, 0], v_table_imag, 0)
         im_first_product(0, "x")
+
         nc.vector.tensor_copy(v_scales_listed[1][:], v_scale_table[:].indirect(half_list(1)))
         wr_rows = [at(AT_WR + 8 * KB * h, "wr_rows%d" % h, [P, PACK, N], F32) for h in halves]
         for h in halves:
             nc.sync.dma_start(
                 out=wr_rows[h][:], in_=wr[h * PASS : (h + 1) * PASS, :].rearrange("(p t) n -> p t n", t=PACK)
             )
-        gather_v_words(v_words[REAL, 0], v_table_real, 0)
-        nc.vector.tensor_copy(u_words[IMAG][:], u_table_imag[:].indirect(idx2[:]))
-        for t in range(PACK):
-            sums = bank("x", [P, S2])
-            for a in (REAL, IMAG):
-                first_stage(sums[:], a, a, 0, t, everyone, a == REAL, a == IMAG)
-            nc.scalar.activation(out=zr_slices[:, t, :], in_=sums[:], func=COPY, scale=gain_re[:, 0, t : t + 1])
-        second_products = im_second_product(0)
-        v_scales.append(at(AT_LATE + 2 * KB, "v_scales1", [P, PASS], U8))
-        v_words[IMAG, 1] = at(AT_LATE + 2 * KB + 512, "v_words_imag1", [P, PASS], U32)
-        v_words[REAL, 1] = at(AT_LATE, "v_words_real1", [P, PASS], U32)
-        deal_v_scales(1)
+        v_scales.append(own("v_scales1", [P, PASS], U8))
+        v_words[IMAG, 1] = at(AT_U_REAL + PASS, "v_words_imag1", [P, PASS], U32)
         gather_v_words(v_words[IMAG, 1], v_table_imag, 1)
-        im_first_product(1, "x")
-        weave(nc.scalar.copy, zr_woven[0], zr_slices, everyone)
-        gather_v_words(v_words[REAL, 1], v_table_real, 1)
-        wi_codes = at(AT_V_IMAG + 2 * KB, "wi_codes", [P, 2, 2 * N], U8)
+        deal_v_scales(1)
+        im_first_product(1, "y")
 
-        wr_woven = [at(AT_V_REAL, "wr_woven0", [P, N, PACK], BF16), None]
+        u_words[IMAG] = at(AT_V_IMAG, "u_words_imag", [P, S2], U32)
+        nc.vector.tensor_copy(u_words[IMAG][:], u_table_imag[:].indirect(idx2[:]))
+        re_first = []
+        for t in range(PACK):
+            re_first.append(bank("x", [P, S2]))
+            first_stage(re_first[t][:], IMAG, IMAG, 0, t, everyone, True, False)
+        gather_v_words(v_words[REAL, 0], v_table_real, 0)
+        second_products = [[], []]
+        for t in range(PACK):
+            first_stage(re_first[t][:], REAL, REAL, 0, t, everyone, False, True)
+            nc.scalar.activation(out=zr_slices[:, t, :], in_=re_first[t][:], func=COPY, scale=gain_re[:, 0, t : t + 1])
+            second_products[0].append(im_second_product(0, t, "y"))
+        weave(nc.scalar.copy, zr_woven[0][:], zr_slices[:])
+        v_words[REAL, 1] = own("v_words_real1", [P, PASS], U32)
+        gather_v_words(v_words[REAL, 1], v_table_real, 1)
+
+        wi_codes = at(AT_V_IMAG + 2 * KB, "wi_codes", [P, 2, 2 * N], U8)
+        wr_woven = [at(AT_V_REAL, "wr_woven0", [P, N, PACK], BF16)]
         for c in range(CHUNKS):
             weave_wr_on_gpsimd(0, c)
         nc.sync.dma_start(out=wi_codes[:].bitcast(I32), in_=wi_words.bitcast(I32).rearrange("a p n -> p a n"))
@@ -271,66 +266,65 @@ def tile_list_mimo_beam_channel_kernel(
         with nc.allow_non_contiguous_dma(reason="one factor for each partition and chunk"):
             nc.sync.dma_start(out=user_power[:], in_=power.rearrange("(c p) -> p c", p=P))
 
-        later_products = im_second_product(1)
-        minus_zi(0, second_products)
-        weave_users(nc.scalar.copy, zi_early[1][:], zi_slices[0], users(1))
-        wr_woven[1] = at(AT_PRODUCT + 4 * KB, "wr_woven1", [P, N, PACK], BF16)
-        for c in range(WR_ON_GPSIMD):
+        for t in range(PACK):
+            second_products[1].append(im_second_product(1, t, "x"))
+        minus_zi(0, second_products[0])
+        weave(nc.scalar.copy, zi_first_woven[ON_SCALAR][:], zi_slices[0][:, :, user_half(ON_SCALAR)])
+        wr_woven.append(at(AT_PRODUCT + 2 * SLICE, "wr_woven1", [P, N, PACK], BF16))
+        for c in range(WR_PIECES_ON_GPSIMD):
             weave_wr_on_gpsimd(1, c)
-        weave(nc.scalar.copy, wr_woven[1], wr_rows[1], slice(WR_ON_GPSIMD * P, N))
-        minus_zi(1, later_products)
-        re_sums = []
+        rest = slice(WR_PIECES_ON_GPSIMD * P, N)
+        weave(nc.scalar.copy, wr_woven[1][:, rest, :], wr_rows[1][:, :, rest])
+        minus_zi(1, second_products[1])
+        re_second = []
         for c in range(CHUNKS):
-            re_sums.append(bank("y", [P, PACK, P]))
+            re_second.append(bank("x", [P, PACK, P]))
             for t in range(PACK):
                 for a in (REAL, IMAG):
-                    first_stage(re_sums[c][:, t, :], a, a, 1, t, chunk(c), a == REAL, a == IMAG)
+                    first_stage(re_second[c][:, t, :], a, a, 1, t, chunk(c), a == REAL, a == IMAG)
         zr_second_half(0)
 
-        wr_codes = [at(AT_PRODUCT + 14 * KB, "wr_codes0", [P, N], U32), own("wr_codes1", [P, N], U32)]
-        zr_codes = [at(AT_PRODUCT + 12 * KB, "zr_codes0", [P, S2], U32), own("zr_codes1", [P, S2], U32)]
-        quantise(wr_codes[0], wr_scales[0], wr_woven[0], slice(0, N))
-        quantise(zr_codes[0], zr_scales[0], zr_woven[0], everyone)
+        wr_codes = [at(AT_PRODUCT + 7 * SLICE, "wr_codes0", [P, N], U32), own("wr_codes1", [P, N], U32)]
+        zr_codes = [at(AT_PRODUCT + 6 * SLICE, "zr_codes0", [P, S2], U32), own("zr_codes1", [P, S2], U32)]
+        quantise(wr_codes[0][:], wr_scales[0][:], wr_woven[0][:])
+        quantise(zr_codes[0][:], zr_scales[0][:], zr_woven[0][:])
         y_t_sums = []
         for c in range(CHUNKS):
-            y_t_sums.append(bank("x", [P, N]))
-            real_pass(c, 0, True, False)
-        zi_late = at(AT_WR + 8 * KB, "zi_late", [P, S2, PACK], BF16)
+            y_t_sums.append(bank("y", [P, N]))
+            real_pass(c, 0, True)
+        zi_second_woven = at(AT_WR + 8 * KB, "zi_second_woven", [P, S2, PACK], BF16)
         for c in range(CHUNKS):
-            weave(nc.scalar.copy, zi_late, zi_slices[1], chunk(c))
-        zi_early[0] = at(AT_PRODUCT + 10 * KB, "zi_early0", [P, S2 // 2, PACK], BF16)
-        weave_users(nc.vector.tensor_copy, zi_early[0][:], zi_slices[0], users(0))
-        for b in (1, 0):
-            nc.vector.quantize_mx(
-                out=zi_codes[0][:, users(b)].bitcast(FP8X4), scales=zi_scales[0][:, users(b)],
-                in_=zi_early[b][:].rearrange("p j t -> p (j t)"),
-            )
-            if b:
-                zr_second_half(1)
+            weave(nc.scalar.copy, zi_second_woven[:, chunk(c), :], zi_slices[1][:, :, chunk(c)])
+        zi_first_woven[ON_VECTOR] = at(AT_PRODUCT + 5 * SLICE, "zi_first_woven_vector", [P, S2 // 2, PACK], BF16)
+        weave(nc.vector.tensor_copy, zi_first_woven[ON_VECTOR][:], zi_slices[0][:, :, user_half(ON_VECTOR)])
+        quantise(zi_codes[0][:, user_half(ON_SCALAR)], zi_scales[0][:, user_half(ON_SCALAR)], zi_first_woven[ON_SCALAR][:])
+        zr_second_half(1)
+        quantise(zi_codes[0][:, user_half(ON_VECTOR)], zi_scales[0][:, user_half(ON_VECTOR)], zi_first_woven[ON_VECTOR][:])
         for c in range(CHUNKS):
-            imag_pass(c, 0)
-        quantise(wr_codes[1], wr_scales[1], wr_woven[1], slice(0, N))
+            imag_pass(c, 0, False)
+        quantise(wr_codes[1][:], wr_scales[1][:], wr_woven[1][:])
+
         for c in range(CHUNKS):
-            quantise(zr_codes[1], zr_scales[1], zr_woven[1], chunk(c))
-            quantise(zi_codes[1], zi_scales[1], zi_late, chunk(c))
+            quantise(zr_codes[1][:, chunk(c)], zr_scales[1][:, chunk(c)], zr_woven[1][:, chunk(c), :])
+            quantise(zi_codes[1][:, chunk(c)], zi_scales[1][:, chunk(c)], zi_second_woven[:, chunk(c), :])
             if c + 2 < CHUNKS:
                 zr_second_half(c + 2)
-            real_pass(c, 1, False, False)
+            real_pass(c, 1, False)
             imag_pass(c, 1, True)
 
         for c in range(CHUNKS):
             dealt = y_t_sums[c][:].rearrange("p (m t) -> p t m", t=PACK)
-            if c in SCALED_ON_SCALAR:
+            if c < SCALED_ON_SCALAR:
                 nc.scalar.activation(out=y_t[c][:], in_=dealt, func=COPY, scale=user_power[:, c : c + 1])
             else:
                 nc.vector.tensor_scalar(
                     out=y_t[c][:], in0=dealt, scalar1=user_power[:, c : c + 1], scalar2=None, op0=MULT
                 )
-            turned = bank("y", [P, PACK, P])
+            turned = bank("x", [P, PACK, P])
             for t in range(PACK):
                 nc.tensor.transpose(turned[:, t, :], y_t[c][:, t, :], ident[:])
             nc.scalar.copy(out=y_rows[c][:], in_=turned[:])
-            weave(nc.vector.tensor_copy, y_woven[c], y_rows[c], slice(0, P))
+            weave(nc.vector.tensor_copy, y_woven[c][:], y_rows[c][:])
             nc.sync.dma_start(out=out_0.rearrange("(p t) j -> p t j", t=PACK)[:, :, chunk(c)], in_=y_rows[c][:])
             if c > 0:
                 quantise_y(c - 1)

@@ -25,20 +25,15 @@ PASS = P * PACK
 CHUNKS = S2 // P
 RUN = 4
 REAL, IMAG = 0, 1
-ON_VECTOR, ON_SCALAR = 0, 1
-WR_PIECES_ON_GPSIMD = 1
-SCALED_ON_SCALAR = 2
-
 KB = 1024
 AT_U_IMAG = 0
-AT_U_SCALES = 4 * KB - 64
-AT_U_REAL = 7 * KB
-AT_V_REAL = AT_U_REAL + 2 * KB + 512
-AT_LISTED = 18 * KB
-AT_WR = 21 * KB
-AT_V_SCALES = AT_WR + 7 * KB
-AT_V_IMAG = 37 * KB
-AT_PRODUCT = 45 * KB
+AT_V_IMAG = 4 * KB
+AT_U_REAL = 2 * KB
+AT_V_REAL = 12 * KB
+AT_WR = 20 * KB
+AT_U_SCALES = AT_WR + 4 * KB - 512
+AT_PRODUCT = AT_WR + 12 * KB
+AT_V_WORDS = AT_PRODUCT + 16 * KB
 SLICE = 2 * KB
 
 
@@ -76,8 +71,11 @@ def tile_list_mimo_beam_channel_kernel(
                     out=table[32 * q : 32 * q + 8, :].bitcast(I32), in_=src[:, 4 * q : 4 * q + 4, :].bitcast(I32)
                 )
 
-        def load_gains(gains, src):
-            nc.sync.dma_start(out=gains[:], in_=src.rearrange("(h p t) -> p h t", h=2, t=PACK))
+        def load_wr(queue, rows, h, cols):
+            queue.dma_start(out=rows[:], in_=wr[h * PASS : (h + 1) * PASS, cols].rearrange("(p t) n -> p t n", t=PACK))
+
+        def load_gains(queue, gains, src):
+            queue.dma_start(out=gains[:], in_=src.rearrange("(h p t) -> p h t", h=2, t=PACK))
 
         def half_list(h):
             return idx[:, h * (PASS // 16) : (h + 1) * (PASS // 16)]
@@ -85,17 +83,11 @@ def tile_list_mimo_beam_channel_kernel(
         def gather_v_words(words, table, h):
             nc.vector.tensor_copy(words[:].rearrange("p (t m) -> p m t", t=PACK), table[:].indirect(half_list(h)))
 
-        def deal_v_scales(h):
-            nc.vector.tensor_copy(
-                v_scales[h][:].rearrange("p (t m) -> p t m", t=PACK),
-                v_scales_listed[h][:].rearrange("p (m t) -> p t m", t=PACK),
-            )
-
         def first_stage(out, v_pass, u_pass, h, t, users, start, stop):
             nc.tensor.matmul_mx(
                 out=out,
                 lhsT=v_words[v_pass, h][:, chunk(t)].bitcast(FP8X4),
-                lhsT_scale=v_scales[h][4 * v_pass :, chunk(t)],
+                lhsT_scale=v_scales[4 * v_pass :, h, chunk(t)],
                 rhs=u_words[u_pass][:, users].bitcast(FP8X4),
                 rhs_scale=u_scales[4 * u_pass :, users],
                 start=start,
@@ -126,25 +118,25 @@ def tile_list_mimo_beam_channel_kernel(
                 in_=slices.rearrange("p t (c i) -> p c t i", i=RUN),
             )
 
-        def weave_wr_on_gpsimd(h, c):
+        def weave_wr_on_gpsimd(h):
             nc.gpsimd.tensor_scalar(
-                out=wr_woven[h][:, chunk(c), :], in0=wr_rows[h][:, :, chunk(c)].rearrange("p t n -> p n t"),
+                out=wr_woven[h][:], in0=wr_rows[h][:].rearrange("p t n -> p n t"),
                 scalar1=1.0, scalar2=0.0, op0=MULT, op1=ADD,
             )
 
         def quantise(codes, scales, woven):
             nc.vector.quantize_mx(out=codes.bitcast(FP8X4), scales=scales, in_=woven.rearrange("p j t -> p (j t)"))
 
-        def real_pass(c, h, start):
+        def real_pass(c, h):
             nc.tensor.matmul_mx(
                 out=y_t_sums[c][:], lhsT=zr_codes[h][:, chunk(c)].bitcast(FP8X4), lhsT_scale=zr_scales[h][:, chunk(c)],
-                rhs=wr_codes[h][:].bitcast(FP8X4), rhs_scale=wr_scales[h][:], start=start, stop=False,
+                rhs=wr_codes[h][:].bitcast(FP8X4), rhs_scale=wr_scales[h][:], start=False, stop=False,
             )
 
-        def imag_pass(c, h, stop):
+        def imag_pass(c, h, start, stop):
             nc.tensor.matmul_mx(
                 out=y_t_sums[c][:], lhsT=zi_codes[h][:, chunk(c)].bitcast(FP8X4), lhsT_scale=zi_scales[h][:, chunk(c)],
-                rhs=wi_codes[:, h, :].bitcast(FP4X4), rhs_scale=wi_planes[:, h, :], start=False, stop=stop,
+                rhs=wi_codes[:, h, :].bitcast(FP4X4), rhs_scale=wi_planes[:, h, :], start=start, stop=stop,
             )
 
         def zr_second_half(c):
@@ -168,164 +160,173 @@ def tile_list_mimo_beam_channel_kernel(
         idx = keep.tile([P, S // 16], U16, name="idx")
         idx2 = keep.tile([P, S2 // 16], U16, name="idx2")
         u_scales = own("u_scales", [P, S2], U8)
+        v_scales = own("v_scales", [P, 2, PASS], U8)
+        u_words = {a: own("u_words%d" % a, [P, S2], U32) for a in (REAL, IMAG)}
+        v_words = {(IMAG, h): own("v_words_imag%d" % h, [P, PASS], U32) for h in halves}
+        v_words[REAL, 0] = at(AT_V_WORDS, "v_words_real0", [P, PASS], U32)
+        v_words[REAL, 1] = own("v_words_real1", [P, PASS], U32)
         wr_scales = [own("wr_scales%d" % h, [P, N], U8) for h in halves]
         zr_slices = own("zr_slices", [P, PACK, S2], BF16)
         zi_slices = [own("zi_slices%d" % h, [P, PACK, S2], BF16) for h in halves]
         zr_woven = [own("zr_woven%d" % h, [P, S2, PACK], BF16) for h in halves]
-        zi_first_woven = {ON_SCALAR: own("zi_first_woven_scalar", [P, S2 // 2, PACK], BF16)}
         zr_scales = [own("zr_scales%d" % h, [P, S2], U8) for h in halves]
         zi_scales = [own("zi_scales%d" % h, [P, S2], U8) for h in halves]
-        zi_codes = [own("zi_codes%d" % h, [P, S2], U32) for h in halves]
         y_t = [own("y_t%d" % c, [P, PACK, P], F32) for c in range(CHUNKS)]
         y_rows = [own("y_rows%d" % c, [P, PACK, P], F32) for c in range(CHUNKS)]
         y_woven = [own("y_woven%d" % c, [P, P, PACK], BF16) for c in range(CHUNKS)]
         y_codes = own("y_codes", [P, S2], U32)
         y_scales = own("y_scales", [P, S2], U8)
         ident = own("ident", [P, P], F32)
+        gain_im = own("gain_im", [P, 2, PACK], F32)
+        wi_planes = own("wi_planes", [P, 2, N], U8)
         product = [
-            [at(AT_PRODUCT + SLICE * (PACK * h + t), "product%d_%d" % (h, t), [P, S2], F32) for t in range(PACK)]
+            [at(AT_PRODUCT + SLICE * (7 - PACK * h - t), "product%d_%d" % (h, t), [P, S2], F32) for t in range(PACK)]
             for h in halves
         ]
         u_table_real = at(AT_U_REAL, "u_table_real", [P, T2], U32)
-        v_table_imag = at(AT_V_IMAG, "v_table_imag", [P, T], U32)
         u_scale_table = at(AT_U_SCALES, "u_scale_table", [P, T2], U8)
-        v_scale_table = at(AT_V_SCALES, "v_scale_table", [P, T], U8)
-        v_scales_listed = [at(AT_LISTED, "v_scales_listed0", [P, PASS], U8)]
-        v_words = {(REAL, 0): own("v_words_real0", [P, PASS], U32)}
-        wi_planes = own("wi_planes", [P, 2, N], U8)
+        v_scale_table = at(AT_V_REAL, "v_scale_table", [P, T], U8)
+        v_scales_listed = own("v_scales_listed", [P, S], U8)
+        gain_re = own("gain_re", [P, 2, PACK], F32)
 
         for scale_tile in (v_scale_table, u_scale_table, wi_planes):
             nc.gpsimd.memset(scale_tile[:].bitcast(I32), 0)
+        wr_early = own("wr_early", [P, PACK, N // 2], F32)
+        load_gains(nc.gpsimd, gain_re, g_re)
+        load_wr(nc.gpsimd, wr_early, 0, slice(0, N // 2))
+        make_identity(nc, ident[:])
+        wr_early_woven = own("wr_early_woven", [P, N // 2, PACK], BF16)
+        weave(nc.scalar.copy, wr_early_woven[:], wr_early[:])
 
-        nc.sync.dma_start(idx[:], offs)
         nc.sync.dma_start(idx2[:], offs2)
+        load_words(nc.sync, u_table_real, tab2_words[REAL])
+        nc.sync.dma_start(idx[:], offs)
+        load_gains(nc.sync, gain_im, g_im)
         load_table_scales(v_scale_table, tab_scales)
         load_table_scales(u_scale_table, tab2_scales)
-        load_words(nc.gpsimd, u_table_real, tab2_words[REAL])
-        load_words(nc.gpsimd, v_table_imag, tab_words[IMAG])
-        make_identity(nc, ident[:])
-
-        nc.vector.tensor_copy(v_scales_listed[0][:], v_scale_table[:].indirect(half_list(0)))
-        nc.vector.tensor_copy(u_scales[:], u_scale_table[:].indirect(idx2[:]))
-        gain_im = at(AT_U_SCALES + 64, "gain_im", [P, 2, PACK], F32)
-        gain_re = at(AT_U_SCALES + 128, "gain_re", [P, 2, PACK], F32)
-        v_scales = [at(AT_U_SCALES + 192, "v_scales0", [P, PASS], U8)]
-        u_words = {REAL: at(AT_U_SCALES + 192 + PASS, "u_words_real", [P, S2], U32)}
-        u_table_imag = at(AT_U_IMAG, "u_table_imag", [P, T2], U32)
-        load_gains(gain_im, g_im)
-        load_gains(gain_re, g_re)
-        load_words(nc.sync, u_table_imag, tab2_words[IMAG])
-        deal_v_scales(0)
-        nc.vector.tensor_copy(u_words[REAL][:], u_table_real[:].indirect(idx2[:]))
-        v_words[IMAG, 0] = at(AT_LISTED, "v_words_imag0", [P, PASS], U32)
-        v_scales_listed.append(at(AT_U_REAL, "v_scales_listed1", [P, PASS], U8))
-        v_table_real = at(AT_V_REAL, "v_table_real", [P, T], U32)
-        load_words(nc.sync, v_table_real, tab_words[REAL])
-        gather_v_words(v_words[IMAG, 0], v_table_imag, 0)
-        im_first_product(0, "x")
-
-        nc.vector.tensor_copy(v_scales_listed[1][:], v_scale_table[:].indirect(half_list(1)))
-        wr_rows = [at(AT_WR + 8 * KB * h, "wr_rows%d" % h, [P, PACK, N], F32) for h in halves]
-        for h in halves:
-            nc.sync.dma_start(
-                out=wr_rows[h][:], in_=wr[h * PASS : (h + 1) * PASS, :].rearrange("(p t) n -> p t n", t=PACK)
-            )
-        v_scales.append(own("v_scales1", [P, PASS], U8))
-        v_words[IMAG, 1] = at(AT_U_REAL + PASS, "v_words_imag1", [P, PASS], U32)
-        gather_v_words(v_words[IMAG, 1], v_table_imag, 1)
-        deal_v_scales(1)
-        im_first_product(1, "y")
-
-        u_words[IMAG] = at(AT_V_IMAG, "u_words_imag", [P, S2], U32)
-        nc.vector.tensor_copy(u_words[IMAG][:], u_table_imag[:].indirect(idx2[:]))
-        re_first = []
-        for t in range(PACK):
-            re_first.append(bank("x", [P, S2]))
-            first_stage(re_first[t][:], IMAG, IMAG, 0, t, everyone, True, False)
-        gather_v_words(v_words[REAL, 0], v_table_real, 0)
-        second_products = [[], []]
-        for t in range(PACK):
-            first_stage(re_first[t][:], REAL, REAL, 0, t, everyone, False, True)
-            nc.scalar.activation(out=zr_slices[:, t, :], in_=re_first[t][:], func=COPY, scale=gain_re[:, 0, t : t + 1])
-            second_products[0].append(im_second_product(0, t, "y"))
-        weave(nc.scalar.copy, zr_woven[0][:], zr_slices[:])
-        v_words[REAL, 1] = own("v_words_real1", [P, PASS], U32)
-        gather_v_words(v_words[REAL, 1], v_table_real, 1)
-
-        wi_codes = at(AT_V_IMAG + 2 * KB, "wi_codes", [P, 2, 2 * N], U8)
-        wr_woven = [at(AT_V_REAL, "wr_woven0", [P, N, PACK], BF16)]
-        for c in range(CHUNKS):
-            weave_wr_on_gpsimd(0, c)
-        nc.sync.dma_start(out=wi_codes[:].bitcast(I32), in_=wi_words.bitcast(I32).rearrange("a p n -> p a n"))
         for q in range(4):
             nc.sync.dma_start(
                 out=wi_planes[32 * q : 32 * q + 4, :, :].bitcast(I32),
                 in_=wi_scales[:, 4 * q : 4 * q + 4, :].bitcast(I32).rearrange("a r n -> r a n"),
             )
-        user_power = at(AT_V_REAL + 4 * KB, "user_power", [P, CHUNKS], F32)
+
+        nc.vector.tensor_copy(u_words[REAL][:], u_table_real[:].indirect(idx2[:]))
+        v_table_imag = at(AT_V_IMAG, "v_table_imag", [P, T], U32)
+        u_table_imag = at(AT_U_IMAG, "u_table_imag", [P, T2], U32)
+        load_words(nc.sync, v_table_imag, tab_words[IMAG])
+        load_words(nc.sync, u_table_imag, tab2_words[IMAG])
+        nc.vector.tensor_copy(v_scales_listed[:], v_scale_table[:].indirect(idx[:]))
+        v_table_real = at(AT_V_REAL, "v_table_real", [P, T], U32)
+        load_words(nc.sync, v_table_real, tab_words[REAL])
+        nc.vector.tensor_copy(u_scales[:], u_scale_table[:].indirect(idx2[:]))
+        wr_rows = [at(AT_WR, "wr_rows0", [P, PACK, N // 2], F32), at(AT_WR + 4 * KB, "wr_rows1", [P, PACK, N], F32)]
+        load_wr(nc.sync, wr_rows[0], 0, slice(N // 2, N))
+        load_wr(nc.sync, wr_rows[1], 1, slice(0, N))
+        nc.vector.tensor_copy(
+            v_scales[:].rearrange("p h (t m) -> p h t m", t=PACK),
+            v_scales_listed[:].rearrange("p (h m t) -> p h t m", h=2, t=PACK),
+        )
+        for h, ring in ((0, "x"), (1, "y")):
+            gather_v_words(v_words[IMAG, h], v_table_imag, h)
+            im_first_product(h, ring)
+        wi_codes = at(AT_V_IMAG, "wi_codes", [P, 2, 2 * N], U8)
+        nc.sync.dma_start(out=wi_codes[:].bitcast(I32), in_=wi_words.bitcast(I32).rearrange("a p n -> p a n"))
+        user_power = at(AT_V_IMAG + 2 * KB, "user_power", [P, CHUNKS], F32)
         with nc.allow_non_contiguous_dma(reason="one factor for each partition and chunk"):
             nc.sync.dma_start(out=user_power[:], in_=power.rearrange("(c p) -> p c", p=P))
 
-        for t in range(PACK):
-            second_products[1].append(im_second_product(1, t, "x"))
+        nc.vector.tensor_copy(u_words[IMAG][:], u_table_imag[:].indirect(idx2[:]))
+        gather_v_words(v_words[REAL, 0], v_table_real, 0)
+        second_products = [[im_second_product(0, t, "x") for t in range(PACK)], []]
+        gather_v_words(v_words[REAL, 1], v_table_real, 1)
         minus_zi(0, second_products[0])
-        weave(nc.scalar.copy, zi_first_woven[ON_SCALAR][:], zi_slices[0][:, :, user_half(ON_SCALAR)])
-        wr_woven.append(at(AT_PRODUCT + 2 * SLICE, "wr_woven1", [P, N, PACK], BF16))
-        for c in range(WR_PIECES_ON_GPSIMD):
-            weave_wr_on_gpsimd(1, c)
-        rest = slice(WR_PIECES_ON_GPSIMD * P, N)
-        weave(nc.scalar.copy, wr_woven[1][:, rest, :], wr_rows[1][:, :, rest])
+
+        wr_woven = [at(AT_V_REAL, "wr_woven0", [P, N // 2, PACK], BF16), at(AT_V_REAL + 4 * KB, "wr_woven1", [P, N, PACK], BF16)]
+        for h in halves:
+            weave_wr_on_gpsimd(h)
+
+        for t in range(PACK):
+            sums = bank("y", [P, S2])
+            for a in (IMAG, REAL):
+                first_stage(sums[:], a, a, 0, t, everyone, a == IMAG, a == REAL)
+            nc.scalar.activation(out=zr_slices[:, t, :], in_=sums[:], func=COPY, scale=gain_re[:, 0, t : t + 1])
+            second_products[1].append(im_second_product(1, t, "x"))
         minus_zi(1, second_products[1])
+        zi_woven = [at(AT_V_WORDS, "zi_woven0", [P, S2, PACK], BF16), own("zi_woven1", [P, S2, PACK], BF16)]
+        for b in halves:
+            weave(nc.scalar.copy, zi_woven[0][:, user_half(b), :], zi_slices[0][:, :, user_half(b)])
+            weave(nc.scalar.copy, zr_woven[0][:, user_half(b), :], zr_slices[:, :, user_half(b)])
         re_second = []
         for c in range(CHUNKS):
-            re_second.append(bank("x", [P, PACK, P]))
+            re_second.append(bank("y", [P, PACK, P]))
             for t in range(PACK):
                 for a in (REAL, IMAG):
                     first_stage(re_second[c][:, t, :], a, a, 1, t, chunk(c), a == REAL, a == IMAG)
+        for c in range(CHUNKS - 1):
+            weave(nc.scalar.copy, zi_woven[1][:, chunk(c), :], zi_slices[1][:, :, chunk(c)])
+        zi_last_woven = at(AT_WR + 8 * KB, "zi_last_woven", [P, P, PACK], BF16)
+
+        wr_codes = [at(AT_PRODUCT - KB, "wr_codes0", [P, N], U32), at(AT_PRODUCT + KB, "wr_codes1", [P, N], U32)]
+        zi_codes = [at(AT_WR + 4 * KB, "zi_codes0", [P, S2], U32), own("zi_codes1", [P, S2], U32)]
+        zr_codes = [own("zr_codes0", [P, S2], U32), at(AT_WR + 6 * KB, "zr_codes1", [P, S2], U32)]
+        def quantise_users(codes, scales, woven, users):
+            quantise(codes[:, users], scales[:, users], woven[:, users, :])
+
+        y_t_sums = [bank("x", [P, N]) for c in range(CHUNKS)]
         zr_second_half(0)
-
-        wr_codes = [at(AT_PRODUCT + 7 * SLICE, "wr_codes0", [P, N], U32), own("wr_codes1", [P, N], U32)]
-        zr_codes = [at(AT_PRODUCT + 6 * SLICE, "zr_codes0", [P, S2], U32), own("zr_codes1", [P, S2], U32)]
-        quantise(wr_codes[0][:], wr_scales[0][:], wr_woven[0][:])
-        quantise(zr_codes[0][:], zr_scales[0][:], zr_woven[0][:])
-        y_t_sums = []
-        for c in range(CHUNKS):
-            y_t_sums.append(bank("y", [P, N]))
-            real_pass(c, 0, True)
-        zi_second_woven = at(AT_WR + 8 * KB, "zi_second_woven", [P, S2, PACK], BF16)
-        for c in range(CHUNKS):
-            weave(nc.scalar.copy, zi_second_woven[:, chunk(c), :], zi_slices[1][:, :, chunk(c)])
-        zi_first_woven[ON_VECTOR] = at(AT_PRODUCT + 5 * SLICE, "zi_first_woven_vector", [P, S2 // 2, PACK], BF16)
-        weave(nc.vector.tensor_copy, zi_first_woven[ON_VECTOR][:], zi_slices[0][:, :, user_half(ON_VECTOR)])
-        quantise(zi_codes[0][:, user_half(ON_SCALAR)], zi_scales[0][:, user_half(ON_SCALAR)], zi_first_woven[ON_SCALAR][:])
         zr_second_half(1)
-        quantise(zi_codes[0][:, user_half(ON_VECTOR)], zi_scales[0][:, user_half(ON_VECTOR)], zi_first_woven[ON_VECTOR][:])
-        for c in range(CHUNKS):
-            imag_pass(c, 0, False)
+        quantise_users(zi_codes[0], zi_scales[0], zi_woven[0], user_half(0))
+        for c in (0, 1):
+            imag_pass(c, 0, True, False)
         quantise(wr_codes[1][:], wr_scales[1][:], wr_woven[1][:])
+        quantise_users(zr_codes[1], zr_scales[1], zr_woven[1], user_half(0))
+        for c in (0, 1):
+            real_pass(c, 1)
+        quantise(wr_codes[0][:, : N // 2], wr_scales[0][:, : N // 2], wr_early_woven[:])
+        quantise(wr_codes[0][:, N // 2 :], wr_scales[0][:, N // 2 :], wr_woven[0][:])
+        quantise_users(zr_codes[0], zr_scales[0], zr_woven[0], user_half(0))
+        for c in (0, 1):
+            real_pass(c, 0)
+        quantise_users(zi_codes[0], zi_scales[0], zi_woven[0], user_half(1))
+        for c in (2, 3):
+            imag_pass(c, 0, True, False)
+        zr_second_half(2)
+        quantise_users(zr_codes[0], zr_scales[0], zr_woven[0], user_half(1))
+        for c in (2, 3):
+            real_pass(c, 0)
+        zr_second_half(3)
+        weave(nc.vector.tensor_copy, zi_last_woven[:], zi_slices[1][:, :, chunk(CHUNKS - 1)])
 
-        for c in range(CHUNKS):
-            quantise(zr_codes[1][:, chunk(c)], zr_scales[1][:, chunk(c)], zr_woven[1][:, chunk(c), :])
-            quantise(zi_codes[1][:, chunk(c)], zi_scales[1][:, chunk(c)], zi_second_woven[:, chunk(c), :])
-            if c + 2 < CHUNKS:
-                zr_second_half(c + 2)
-            real_pass(c, 1, False)
-            imag_pass(c, 1, True)
-
-        for c in range(CHUNKS):
+        def scale_y(c):
             dealt = y_t_sums[c][:].rearrange("p (m t) -> p t m", t=PACK)
-            if c < SCALED_ON_SCALAR:
+            if c < CHUNKS - 1:
                 nc.scalar.activation(out=y_t[c][:], in_=dealt, func=COPY, scale=user_power[:, c : c + 1])
             else:
                 nc.vector.tensor_scalar(
                     out=y_t[c][:], in0=dealt, scalar1=user_power[:, c : c + 1], scalar2=None, op0=MULT
                 )
-            turned = bank("x", [P, PACK, P])
+
+        def turn_y(c):
+            turned = bank("y", [P, PACK, P])
             for t in range(PACK):
                 nc.tensor.transpose(turned[:, t, :], y_t[c][:, t, :], ident[:])
-            nc.scalar.copy(out=y_rows[c][:], in_=turned[:])
-            weave(nc.vector.tensor_copy, y_woven[c][:], y_rows[c][:])
+            copy = nc.vector.tensor_copy if c == 1 else nc.scalar.copy
+            copy(out=y_rows[c][:], in_=turned[:])
             nc.sync.dma_start(out=out_0.rearrange("(p t) j -> p t j", t=PACK)[:, :, chunk(c)], in_=y_rows[c][:])
+
+        for c in range(CHUNKS):
+            if c >= 2:
+                quantise_users(zr_codes[1], zr_scales[1], zr_woven[1], chunk(c))
+                real_pass(c, 1)
+            woven = zi_last_woven[:] if c == CHUNKS - 1 else zi_woven[1][:, chunk(c), :]
+            quantise(zi_codes[1][:, chunk(c)], zi_scales[1][:, chunk(c)], woven)
+            imag_pass(c, 1, False, True)
+        for c in range(CHUNKS):
+            scale_y(c)
+        for c in range(CHUNKS):
+            turn_y(c)
+        for c in range(CHUNKS):
+            weave(nc.vector.tensor_copy, y_woven[c][:], y_rows[c][:])
             if c > 0:
                 quantise_y(c - 1)
         store_codes(slice(0, S2 - P))

@@ -26,13 +26,10 @@ CHUNKS = S2 // P
 RUN = 4
 REAL, IMAG = 0, 1
 KB = 1024
-AT_U_IMAG = 0
-AT_V_IMAG = 4 * KB
-AT_U_REAL = 2 * KB
-AT_V_REAL = 12 * KB
-AT_WR = 20 * KB
-AT_U_SCALES = AT_WR + 4 * KB - 512
+AT_V_REAL = 0
+AT_WR = 8 * KB
 AT_PRODUCT = AT_WR + 12 * KB
+AT_WR_EARLY = AT_PRODUCT + 11 * KB
 AT_V_WORDS = AT_PRODUCT + 16 * KB
 SLICE = 2 * KB
 
@@ -62,8 +59,8 @@ def tile_list_mimo_beam_channel_kernel(
         def user_half(b):
             return slice(b * (S2 // 2), (b + 1) * (S2 // 2))
 
-        def load_words(queue, table, src):
-            queue.dma_start(out=table[:].bitcast(I32), in_=src.rearrange("p t i -> p (t i)").bitcast(I32))
+        def load_words(table, src):
+            nc.sync.dma_start(out=table[:].bitcast(I32), in_=src.rearrange("p t i -> p (t i)").bitcast(I32))
 
         def load_table_scales(table, src):
             for q in range(4):
@@ -71,11 +68,11 @@ def tile_list_mimo_beam_channel_kernel(
                     out=table[32 * q : 32 * q + 8, :].bitcast(I32), in_=src[:, 4 * q : 4 * q + 4, :].bitcast(I32)
                 )
 
-        def load_wr(queue, rows, h, cols):
-            queue.dma_start(out=rows[:], in_=wr[h * PASS : (h + 1) * PASS, cols].rearrange("(p t) n -> p t n", t=PACK))
+        def load_wr(rows, h, cols):
+            nc.sync.dma_start(out=rows[:], in_=wr[h * PASS : (h + 1) * PASS, cols].rearrange("(p t) n -> p t n", t=PACK))
 
-        def load_gains(queue, gains, src):
-            queue.dma_start(out=gains[:], in_=src.rearrange("(h p t) -> p h t", h=2, t=PACK))
+        def load_gains(gains, src):
+            nc.sync.dma_start(out=gains[:], in_=src.rearrange("(h p t) -> p h t", h=2, t=PACK))
 
         def half_list(h):
             return idx[:, h * (PASS // 16) : (h + 1) * (PASS // 16)]
@@ -179,49 +176,54 @@ def tile_list_mimo_beam_channel_kernel(
         ident = own("ident", [P, P], F32)
         gain_im = own("gain_im", [P, 2, PACK], F32)
         wi_planes = own("wi_planes", [P, 2, N], U8)
-        product = [
-            [at(AT_PRODUCT + SLICE * (7 - PACK * h - t), "product%d_%d" % (h, t), [P, S2], F32) for t in range(PACK)]
-            for h in halves
-        ]
-        u_table_real = at(AT_U_REAL, "u_table_real", [P, T2], U32)
-        u_scale_table = at(AT_U_SCALES, "u_scale_table", [P, T2], U8)
-        v_scale_table = at(AT_V_REAL, "v_scale_table", [P, T], U8)
+        u_tables = [own("u_table%d" % a, [P, T2], U32) for a in (REAL, IMAG)]
+        v_table_imag = own("v_table_imag", [P, T], U32)
+        v_table_real = at(AT_V_REAL, "v_table_real", [P, T], U32)
+        u_scale_table = own("u_scale_table", [P, T2], U8)
+        v_scale_table = own("v_scale_table", [P, T], U8)
         v_scales_listed = own("v_scales_listed", [P, S], U8)
         gain_re = own("gain_re", [P, 2, PACK], F32)
+        wr_early = at(AT_WR_EARLY, "wr_early", [P, PACK, N // 2], F32)
+        wr_early_woven = own("wr_early_woven", [P, N // 2, PACK], BF16)
+        wr_rows = [at(AT_WR, "wr_rows0", [P, PACK, N // 2], F32), at(AT_WR + 4 * KB, "wr_rows1", [P, PACK, N], F32)]
+        wi_codes = own("wi_codes", [P, 2, 2 * N], U8)
+        user_power = own("user_power", [P, CHUNKS], F32)
 
         for scale_tile in (v_scale_table, u_scale_table, wi_planes):
             nc.gpsimd.memset(scale_tile[:].bitcast(I32), 0)
-        wr_early = own("wr_early", [P, PACK, N // 2], F32)
-        load_gains(nc.gpsimd, gain_re, g_re)
-        load_wr(nc.gpsimd, wr_early, 0, slice(0, N // 2))
-        make_identity(nc, ident[:])
-        wr_early_woven = own("wr_early_woven", [P, N // 2, PACK], BF16)
-        weave(nc.scalar.copy, wr_early_woven[:], wr_early[:])
+        nc.scalar.mul(out=ident[:].bitcast(U32), in_=ident[:].bitcast(U32), mul=0.0)
+        make_identity(nc, ident[:], nomemset=True)
 
         nc.sync.dma_start(idx2[:], offs2)
-        load_words(nc.sync, u_table_real, tab2_words[REAL])
+        load_words(u_tables[REAL], tab2_words[REAL])
         nc.sync.dma_start(idx[:], offs)
-        load_gains(nc.sync, gain_im, g_im)
+        load_gains(gain_im, g_im)
         load_table_scales(v_scale_table, tab_scales)
         load_table_scales(u_scale_table, tab2_scales)
+        load_wr(wr_early, 0, slice(0, N // 2))
+        load_words(v_table_imag, tab_words[IMAG])
+        load_words(u_tables[IMAG], tab2_words[IMAG])
+        load_words(v_table_real, tab_words[REAL])
+        load_gains(gain_re, g_re)
+        load_wr(wr_rows[0], 0, slice(N // 2, N))
+        load_wr(wr_rows[1], 1, slice(0, N))
+        nc.sync.dma_start(out=wi_codes[:].bitcast(I32), in_=wi_words.bitcast(I32).rearrange("a p n -> p a n"))
         for q in range(4):
             nc.sync.dma_start(
                 out=wi_planes[32 * q : 32 * q + 4, :, :].bitcast(I32),
                 in_=wi_scales[:, 4 * q : 4 * q + 4, :].bitcast(I32).rearrange("a r n -> r a n"),
             )
+        with nc.allow_non_contiguous_dma(reason="one factor for each partition and chunk"):
+            nc.sync.dma_start(out=user_power[:], in_=power.rearrange("(c p) -> p c", p=P))
 
-        nc.vector.tensor_copy(u_words[REAL][:], u_table_real[:].indirect(idx2[:]))
-        v_table_imag = at(AT_V_IMAG, "v_table_imag", [P, T], U32)
-        u_table_imag = at(AT_U_IMAG, "u_table_imag", [P, T2], U32)
-        load_words(nc.sync, v_table_imag, tab_words[IMAG])
-        load_words(nc.sync, u_table_imag, tab2_words[IMAG])
+        weave(nc.scalar.copy, wr_early_woven[:], wr_early[:])
+        product = [
+            [at(AT_PRODUCT + SLICE * (7 - PACK * h - t), "product%d_%d" % (h, t), [P, S2], F32) for t in range(PACK)]
+            for h in halves
+        ]
+        nc.vector.tensor_copy(u_words[REAL][:], u_tables[REAL][:].indirect(idx2[:]))
         nc.vector.tensor_copy(v_scales_listed[:], v_scale_table[:].indirect(idx[:]))
-        v_table_real = at(AT_V_REAL, "v_table_real", [P, T], U32)
-        load_words(nc.sync, v_table_real, tab_words[REAL])
         nc.vector.tensor_copy(u_scales[:], u_scale_table[:].indirect(idx2[:]))
-        wr_rows = [at(AT_WR, "wr_rows0", [P, PACK, N // 2], F32), at(AT_WR + 4 * KB, "wr_rows1", [P, PACK, N], F32)]
-        load_wr(nc.sync, wr_rows[0], 0, slice(N // 2, N))
-        load_wr(nc.sync, wr_rows[1], 1, slice(0, N))
         nc.vector.tensor_copy(
             v_scales[:].rearrange("p h (t m) -> p h t m", t=PACK),
             v_scales_listed[:].rearrange("p (h m t) -> p h t m", h=2, t=PACK),
@@ -229,15 +231,17 @@ def tile_list_mimo_beam_channel_kernel(
         for h, ring in ((0, "x"), (1, "y")):
             gather_v_words(v_words[IMAG, h], v_table_imag, h)
             im_first_product(h, ring)
-        wi_codes = at(AT_V_IMAG, "wi_codes", [P, 2, 2 * N], U8)
-        nc.sync.dma_start(out=wi_codes[:].bitcast(I32), in_=wi_words.bitcast(I32).rearrange("a p n -> p a n"))
-        user_power = at(AT_V_IMAG + 2 * KB, "user_power", [P, CHUNKS], F32)
-        with nc.allow_non_contiguous_dma(reason="one factor for each partition and chunk"):
-            nc.sync.dma_start(out=user_power[:], in_=power.rearrange("(c p) -> p c", p=P))
 
-        nc.vector.tensor_copy(u_words[IMAG][:], u_table_imag[:].indirect(idx2[:]))
+        nc.vector.tensor_copy(u_words[IMAG][:], u_tables[IMAG][:].indirect(idx2[:]))
+        re_first = [bank("x", [P, S2]) for t in range(PACK)]
+        for t in range(PACK):
+            first_stage(re_first[t][:], IMAG, IMAG, 0, t, everyone, True, False)
         gather_v_words(v_words[REAL, 0], v_table_real, 0)
-        second_products = [[im_second_product(0, t, "x") for t in range(PACK)], []]
+        second_products = [[], []]
+        for t in range(PACK):
+            second_products[0].append(im_second_product(0, t, "y"))
+            first_stage(re_first[t][:], REAL, REAL, 0, t, everyone, False, True)
+            nc.scalar.activation(out=zr_slices[:, t, :], in_=re_first[t][:], func=COPY, scale=gain_re[:, 0, t : t + 1])
         gather_v_words(v_words[REAL, 1], v_table_real, 1)
         minus_zi(0, second_products[0])
 
@@ -246,10 +250,6 @@ def tile_list_mimo_beam_channel_kernel(
             weave_wr_on_gpsimd(h)
 
         for t in range(PACK):
-            sums = bank("y", [P, S2])
-            for a in (IMAG, REAL):
-                first_stage(sums[:], a, a, 0, t, everyone, a == IMAG, a == REAL)
-            nc.scalar.activation(out=zr_slices[:, t, :], in_=sums[:], func=COPY, scale=gain_re[:, 0, t : t + 1])
             second_products[1].append(im_second_product(1, t, "x"))
         minus_zi(1, second_products[1])
         zi_woven = [at(AT_V_WORDS, "zi_woven0", [P, S2, PACK], BF16), own("zi_woven1", [P, S2, PACK], BF16)]
@@ -262,9 +262,8 @@ def tile_list_mimo_beam_channel_kernel(
             for t in range(PACK):
                 for a in (REAL, IMAG):
                     first_stage(re_second[c][:, t, :], a, a, 1, t, chunk(c), a == REAL, a == IMAG)
-        for c in range(CHUNKS - 1):
+        for c in range(CHUNKS):
             weave(nc.scalar.copy, zi_woven[1][:, chunk(c), :], zi_slices[1][:, :, chunk(c)])
-        zi_last_woven = at(AT_WR + 8 * KB, "zi_last_woven", [P, P, PACK], BF16)
 
         wr_codes = [at(AT_PRODUCT - KB, "wr_codes0", [P, N], U32), at(AT_PRODUCT + KB, "wr_codes1", [P, N], U32)]
         zi_codes = [at(AT_WR + 4 * KB, "zi_codes0", [P, S2], U32), own("zi_codes1", [P, S2], U32)]
@@ -273,33 +272,30 @@ def tile_list_mimo_beam_channel_kernel(
             quantise(codes[:, users], scales[:, users], woven[:, users, :])
 
         y_t_sums = [bank("x", [P, N]) for c in range(CHUNKS)]
-        zr_second_half(0)
-        zr_second_half(1)
         quantise_users(zi_codes[0], zi_scales[0], zi_woven[0], user_half(0))
         for c in (0, 1):
             imag_pass(c, 0, True, False)
-        quantise(wr_codes[1][:], wr_scales[1][:], wr_woven[1][:])
-        quantise_users(zr_codes[1], zr_scales[1], zr_woven[1], user_half(0))
-        for c in (0, 1):
-            real_pass(c, 1)
+        zr_second_half(0)
         quantise(wr_codes[0][:, : N // 2], wr_scales[0][:, : N // 2], wr_early_woven[:])
         quantise(wr_codes[0][:, N // 2 :], wr_scales[0][:, N // 2 :], wr_woven[0][:])
         quantise_users(zr_codes[0], zr_scales[0], zr_woven[0], user_half(0))
         for c in (0, 1):
             real_pass(c, 0)
+        quantise(wr_codes[1][:], wr_scales[1][:], wr_woven[1][:])
+        quantise_users(zr_codes[1], zr_scales[1], zr_woven[1], chunk(0))
+        real_pass(0, 1)
         quantise_users(zi_codes[0], zi_scales[0], zi_woven[0], user_half(1))
         for c in (2, 3):
             imag_pass(c, 0, True, False)
-        zr_second_half(2)
+        zr_second_half(1)
         quantise_users(zr_codes[0], zr_scales[0], zr_woven[0], user_half(1))
         for c in (2, 3):
             real_pass(c, 0)
-        zr_second_half(3)
-        weave(nc.vector.tensor_copy, zi_last_woven[:], zi_slices[1][:, :, chunk(CHUNKS - 1)])
+        zr_second_half(2)
 
         def scale_y(c):
             dealt = y_t_sums[c][:].rearrange("p (m t) -> p t m", t=PACK)
-            if c < CHUNKS - 1:
+            if c % 2 == 0:
                 nc.scalar.activation(out=y_t[c][:], in_=dealt, func=COPY, scale=user_power[:, c : c + 1])
             else:
                 nc.vector.tensor_scalar(
@@ -315,12 +311,13 @@ def tile_list_mimo_beam_channel_kernel(
             nc.sync.dma_start(out=out_0.rearrange("(p t) j -> p t j", t=PACK)[:, :, chunk(c)], in_=y_rows[c][:])
 
         for c in range(CHUNKS):
-            if c >= 2:
+            if c > 0:
                 quantise_users(zr_codes[1], zr_scales[1], zr_woven[1], chunk(c))
                 real_pass(c, 1)
-            woven = zi_last_woven[:] if c == CHUNKS - 1 else zi_woven[1][:, chunk(c), :]
-            quantise(zi_codes[1][:, chunk(c)], zi_scales[1][:, chunk(c)], woven)
+            quantise_users(zi_codes[1], zi_scales[1], zi_woven[1], chunk(c))
             imag_pass(c, 1, False, True)
+            if c == 1:
+                zr_second_half(3)
         for c in range(CHUNKS):
             scale_y(c)
         for c in range(CHUNKS):

@@ -115,26 +115,28 @@ def tile_list_mimo_beam_channel_kernel(
                 in_=slices.rearrange("p t (c i) -> p c t i", i=RUN),
             )
 
-        def weave_wr_on_gpsimd(h):
+        def weave_wr_on_gpsimd(woven, rows):
             nc.gpsimd.tensor_scalar(
-                out=wr_woven[h][:], in0=wr_rows[h][:].rearrange("p t n -> p n t"),
-                scalar1=1.0, scalar2=0.0, op0=MULT, op1=ADD,
+                out=woven, in0=rows.rearrange("p t (m s) -> p s m t", s=PACK), scalar1=1.0, scalar2=0.0, op0=MULT, op1=ADD
             )
 
         def quantise(codes, scales, woven):
             nc.vector.quantize_mx(out=codes.bitcast(FP8X4), scales=scales, in_=woven.rearrange("p j t -> p (j t)"))
 
-        def real_pass(c, h):
-            nc.tensor.matmul_mx(
-                out=y_t_sums[c][:], lhsT=zr_codes[h][:, chunk(c)].bitcast(FP8X4), lhsT_scale=zr_scales[h][:, chunk(c)],
-                rhs=wr_codes[h][:].bitcast(FP8X4), rhs_scale=wr_scales[h][:], start=False, stop=False,
-            )
+        def second_stage(c, weights, weight_scales, dtype, codes, scales, start, stop):
+            width = weights.shape[1] // PACK
+            for t in range(PACK):
+                nc.tensor.matmul_mx(
+                    out=y_sums[c][:, t, :], lhsT=weights[:, t * width : (t + 1) * width].bitcast(dtype),
+                    lhsT_scale=weight_scales[:, chunk(t)], rhs=codes[:, chunk(c)].bitcast(FP8X4),
+                    rhs_scale=scales[:, chunk(c)], start=start and t == 0, stop=stop and t == PACK - 1,
+                )
+
+        def real_pass(c, h, start):
+            second_stage(c, wr_codes[h][:], wr_scales[h][:], FP8X4, zr_codes[h], zr_scales[h], start, False)
 
         def imag_pass(c, h, start, stop):
-            nc.tensor.matmul_mx(
-                out=y_t_sums[c][:], lhsT=zi_codes[h][:, chunk(c)].bitcast(FP8X4), lhsT_scale=zi_scales[h][:, chunk(c)],
-                rhs=wi_codes[:, h, :].bitcast(FP4X4), rhs_scale=wi_planes[:, h, :], start=start, stop=stop,
-            )
+            second_stage(c, wi_dealt[:, h, :], wi_scales_dealt[:, h, :], FP4X4, zi_codes[h], zi_scales[h], start, stop)
 
         def zr_second_half(c):
             nc.vector.tensor_tensor(
@@ -161,14 +163,12 @@ def tile_list_mimo_beam_channel_kernel(
         u_words = {a: own("u_words%d" % a, [P, S2], U32) for a in (REAL, IMAG)}
         v_words = {(IMAG, h): own("v_words_imag%d" % h, [P, PASS], U32) for h in halves}
         v_words[REAL, 0] = at(AT_V_WORDS, "v_words_real0", [P, PASS], U32)
-        v_words[REAL, 1] = own("v_words_real1", [P, PASS], U32)
         wr_scales = [own("wr_scales%d" % h, [P, N], U8) for h in halves]
         zr_slices = own("zr_slices", [P, PACK, S2], BF16)
         zi_slices = [own("zi_slices%d" % h, [P, PACK, S2], BF16) for h in halves]
         zr_woven = [own("zr_woven%d" % h, [P, S2, PACK], BF16) for h in halves]
         zr_scales = [own("zr_scales%d" % h, [P, S2], U8) for h in halves]
         zi_scales = [own("zi_scales%d" % h, [P, S2], U8) for h in halves]
-        y_t = [own("y_t%d" % c, [P, PACK, P], F32) for c in range(CHUNKS)]
         y_rows = [own("y_rows%d" % c, [P, PACK, P], F32) for c in range(CHUNKS)]
         y_woven = [own("y_woven%d" % c, [P, P, PACK], BF16) for c in range(CHUNKS)]
         y_codes = own("y_codes", [P, S2], U32)
@@ -184,8 +184,9 @@ def tile_list_mimo_beam_channel_kernel(
         v_scales_listed = own("v_scales_listed", [P, S], U8)
         gain_re = own("gain_re", [P, 2, PACK], F32)
         wr_early = at(AT_WR_EARLY, "wr_early", [P, PACK, N // 2], F32)
-        wr_early_woven = own("wr_early_woven", [P, N // 2, PACK], BF16)
-        wr_rows = [at(AT_WR, "wr_rows0", [P, PACK, N // 2], F32), at(AT_WR + 4 * KB, "wr_rows1", [P, PACK, N], F32)]
+        wr_first_woven = own("wr_first_woven", [P, PACK, P, PACK], BF16)
+        wr_rows = [at(AT_WR + 8 * KB, "wr_rows0", [P, PACK, N // 2], F32), at(AT_WR, "wr_rows1", [P, PACK, N], F32)]
+        power_rows = own("power_rows", [P, S2], F32)
         wi_codes = own("wi_codes", [P, 2, 2 * N], U8)
         user_power = own("user_power", [P, CHUNKS], F32)
 
@@ -200,23 +201,27 @@ def tile_list_mimo_beam_channel_kernel(
         load_gains(gain_im, g_im)
         load_table_scales(v_scale_table, tab_scales)
         load_table_scales(u_scale_table, tab2_scales)
+        with nc.allow_non_contiguous_dma(reason="one factor for each partition and chunk"):
+            nc.sync.dma_start(out=user_power[:], in_=power.rearrange("(c p) -> p c", p=P))
         load_wr(wr_early, 0, slice(0, N // 2))
         load_words(v_table_imag, tab_words[IMAG])
         load_words(u_tables[IMAG], tab2_words[IMAG])
-        load_words(v_table_real, tab_words[REAL])
-        load_gains(gain_re, g_re)
-        load_wr(wr_rows[0], 0, slice(N // 2, N))
-        load_wr(wr_rows[1], 1, slice(0, N))
         nc.sync.dma_start(out=wi_codes[:].bitcast(I32), in_=wi_words.bitcast(I32).rearrange("a p n -> p a n"))
         for q in range(4):
             nc.sync.dma_start(
                 out=wi_planes[32 * q : 32 * q + 4, :, :].bitcast(I32),
                 in_=wi_scales[:, 4 * q : 4 * q + 4, :].bitcast(I32).rearrange("a r n -> r a n"),
             )
-        with nc.allow_non_contiguous_dma(reason="one factor for each partition and chunk"):
-            nc.sync.dma_start(out=user_power[:], in_=power.rearrange("(c p) -> p c", p=P))
+        load_words(v_table_real, tab_words[REAL])
+        load_gains(gain_re, g_re)
+        load_wr(wr_rows[1], 1, slice(0, N))
+        load_wr(wr_rows[0], 0, slice(N // 2, N))
 
-        weave(nc.scalar.copy, wr_early_woven[:], wr_early[:])
+        nc.scalar.copy(out=wr_first_woven[:, :, : P // 2, :], in_=wr_early[:].rearrange("p t (m s) -> p s m t", s=PACK))
+        spread = bank("y", [P, S2])
+        for c in range(CHUNKS):
+            nc.tensor.transpose(spread[:, chunk(c)], user_power[:, c : c + 1].to_broadcast([P, P]), ident[:])
+        nc.scalar.copy(out=power_rows[:], in_=spread[:])
         product = [
             [at(AT_PRODUCT + SLICE * (7 - PACK * h - t), "product%d_%d" % (h, t), [P, S2], F32) for t in range(PACK)]
             for h in halves
@@ -236,18 +241,29 @@ def tile_list_mimo_beam_channel_kernel(
         re_first = [bank("x", [P, S2]) for t in range(PACK)]
         for t in range(PACK):
             first_stage(re_first[t][:], IMAG, IMAG, 0, t, everyone, True, False)
+        wi_dealt = own("wi_dealt", [P, 2, 2 * N], U8)
+        wi_scales_dealt = own("wi_scales_dealt", [P, 2, N], U8)
+        nc.vector.tensor_copy(
+            wi_dealt[:].bitcast(U16).rearrange("p h (s m) -> p h s m", s=PACK),
+            wi_codes[:].bitcast(U16).rearrange("p h (m s) -> p h s m", s=PACK),
+        )
+        nc.vector.tensor_copy(
+            wi_scales_dealt[:].rearrange("p h (s m) -> p h s m", s=PACK),
+            wi_planes[:].rearrange("p h (m s) -> p h s m", s=PACK),
+        )
         gather_v_words(v_words[REAL, 0], v_table_real, 0)
         second_products = [[], []]
         for t in range(PACK):
             second_products[0].append(im_second_product(0, t, "y"))
             first_stage(re_first[t][:], REAL, REAL, 0, t, everyone, False, True)
             nc.scalar.activation(out=zr_slices[:, t, :], in_=re_first[t][:], func=COPY, scale=gain_re[:, 0, t : t + 1])
+        v_words[REAL, 1] = own("v_words_real1", [P, PASS], U32)
         gather_v_words(v_words[REAL, 1], v_table_real, 1)
         minus_zi(0, second_products[0])
 
-        wr_woven = [at(AT_V_REAL, "wr_woven0", [P, N // 2, PACK], BF16), at(AT_V_REAL + 4 * KB, "wr_woven1", [P, N, PACK], BF16)]
-        for h in halves:
-            weave_wr_on_gpsimd(h)
+        wr_second_woven = at(AT_V_REAL, "wr_second_woven", [P, PACK, P, PACK], BF16)
+        weave_wr_on_gpsimd(wr_second_woven[:], wr_rows[1][:])
+        weave_wr_on_gpsimd(wr_first_woven[:, :, P // 2 :, :], wr_rows[0][:])
 
         for t in range(PACK):
             second_products[1].append(im_second_product(1, t, "x"))
@@ -262,70 +278,70 @@ def tile_list_mimo_beam_channel_kernel(
             for t in range(PACK):
                 for a in (REAL, IMAG):
                     first_stage(re_second[c][:, t, :], a, a, 1, t, chunk(c), a == REAL, a == IMAG)
-        for c in range(CHUNKS):
+        zr_last_slices = own("zr_last_slices", [P, PACK, P], BF16)
+        zr_last_woven = own("zr_last_woven", [P, P, PACK], BF16)
+        for c in (0, 1):
             weave(nc.scalar.copy, zi_woven[1][:, chunk(c), :], zi_slices[1][:, :, chunk(c)])
+        for t in range(PACK):
+            nc.scalar.activation(
+                out=zr_last_slices[:, t, :], in_=re_second[CHUNKS - 1][:, t, :], func=COPY, scale=gain_re[:, 1, t : t + 1]
+            )
+        weave(nc.scalar.copy, zi_woven[1][:, chunk(2), :], zi_slices[1][:, :, chunk(2)])
+        weave(nc.scalar.copy, zr_last_woven[:], zr_last_slices[:])
+        weave(nc.scalar.copy, zi_woven[1][:, chunk(3), :], zi_slices[1][:, :, chunk(3)])
 
         wr_codes = [at(AT_PRODUCT - KB, "wr_codes0", [P, N], U32), at(AT_PRODUCT + KB, "wr_codes1", [P, N], U32)]
-        zi_codes = [at(AT_WR + 4 * KB, "zi_codes0", [P, S2], U32), own("zi_codes1", [P, S2], U32)]
-        zr_codes = [own("zr_codes0", [P, S2], U32), at(AT_WR + 6 * KB, "zr_codes1", [P, S2], U32)]
+        zi_codes = [at(AT_WR, "zi_codes0", [P, S2], U32), own("zi_codes1", [P, S2], U32)]
+        zr_codes = [own("zr_codes0", [P, S2], U32), at(AT_WR + 2 * KB, "zr_codes1", [P, S2], U32)]
         def quantise_users(codes, scales, woven, users):
             quantise(codes[:, users], scales[:, users], woven[:, users, :])
 
-        y_t_sums = [bank("x", [P, N]) for c in range(CHUNKS)]
-        quantise_users(zi_codes[0], zi_scales[0], zi_woven[0], user_half(0))
-        for c in (0, 1):
-            imag_pass(c, 0, True, False)
-        zr_second_half(0)
-        quantise(wr_codes[0][:, : N // 2], wr_scales[0][:, : N // 2], wr_early_woven[:])
-        quantise(wr_codes[0][:, N // 2 :], wr_scales[0][:, N // 2 :], wr_woven[0][:])
-        quantise_users(zr_codes[0], zr_scales[0], zr_woven[0], user_half(0))
-        for c in (0, 1):
-            real_pass(c, 0)
-        quantise(wr_codes[1][:], wr_scales[1][:], wr_woven[1][:])
-        quantise_users(zr_codes[1], zr_scales[1], zr_woven[1], chunk(0))
-        real_pass(0, 1)
-        quantise_users(zi_codes[0], zi_scales[0], zi_woven[0], user_half(1))
-        for c in (2, 3):
-            imag_pass(c, 0, True, False)
-        zr_second_half(1)
-        quantise_users(zr_codes[0], zr_scales[0], zr_woven[0], user_half(1))
-        for c in (2, 3):
-            real_pass(c, 0)
-        zr_second_half(2)
+        y_sums = [bank("x", [P, PACK, P]) for c in range(CHUNKS)]
 
-        def scale_y(c):
-            dealt = y_t_sums[c][:].rearrange("p (m t) -> p t m", t=PACK)
-            if c % 2 == 0:
-                nc.scalar.activation(out=y_t[c][:], in_=dealt, func=COPY, scale=user_power[:, c : c + 1])
-            else:
-                nc.vector.tensor_scalar(
-                    out=y_t[c][:], in0=dealt, scalar1=user_power[:, c : c + 1], scalar2=None, op0=MULT
-                )
-
-        def turn_y(c):
-            turned = bank("y", [P, PACK, P])
-            for t in range(PACK):
-                nc.tensor.transpose(turned[:, t, :], y_t[c][:, t, :], ident[:])
-            copy = nc.vector.tensor_copy if c == 1 else nc.scalar.copy
-            copy(out=y_rows[c][:], in_=turned[:])
-            nc.sync.dma_start(out=out_0.rearrange("(p t) j -> p t j", t=PACK)[:, :, chunk(c)], in_=y_rows[c][:])
-
-        for c in range(CHUNKS):
-            if c > 0:
-                quantise_users(zr_codes[1], zr_scales[1], zr_woven[1], chunk(c))
-                real_pass(c, 1)
+        def close(c):
+            woven = zr_last_woven[:] if c == CHUNKS - 1 else zr_woven[1][:, chunk(c), :]
+            quantise(zr_codes[1][:, chunk(c)], zr_scales[1][:, chunk(c)], woven)
+            real_pass(c, 1, False)
             quantise_users(zi_codes[1], zi_scales[1], zi_woven[1], chunk(c))
             imag_pass(c, 1, False, True)
-            if c == 1:
-                zr_second_half(3)
-        for c in range(CHUNKS):
-            scale_y(c)
-        for c in range(CHUNKS):
-            turn_y(c)
-        for c in range(CHUNKS):
-            weave(nc.vector.tensor_copy, y_woven[c][:], y_rows[c][:])
-            if c > 0:
-                quantise_y(c - 1)
+
+        def first_real(b):
+            quantise_users(zr_codes[0], zr_scales[0], zr_woven[0], user_half(b))
+            for c in (2 * b, 2 * b + 1):
+                real_pass(c, 0, False)
+
+        def first_imag(b):
+            quantise_users(zi_codes[0], zi_scales[0], zi_woven[0], user_half(b))
+            for c in (2 * b, 2 * b + 1):
+                imag_pass(c, 0, True, False)
+
+        def scale_y(c):
+            nc.vector.tensor_tensor(
+                out=y_rows[c][:], in0=y_sums[c][:],
+                in1=power_rows[:, chunk(c)].unsqueeze(1).to_broadcast([P, PACK, P]), op=MULT,
+            )
+            nc.sync.dma_start(out=out_0.rearrange("(p t) j -> p t j", t=PACK)[:, :, chunk(c)], in_=y_rows[c][:])
+            weave(nc.vector.tensor_copy if c == CHUNKS - 1 else nc.scalar.copy, y_woven[c][:], y_rows[c][:])
+
+        first_imag(0)
+        quantise(wr_codes[0][:], wr_scales[0][:], wr_first_woven[:].rearrange("p s m t -> p (s m) t"))
+        first_real(0)
+        zr_second_half(0)
+        first_imag(1)
+        quantise(wr_codes[1][:], wr_scales[1][:], wr_second_woven[:].rearrange("p s m t -> p (s m) t"))
+        first_real(1)
+        zr_second_half(1)
+        close(0)
+        zr_second_half(2)
+        close(1)
+        scale_y(0)
+        close(2)
+        scale_y(1)
+        close(3)
+        scale_y(2)
+        scale_y(3)
+        for c in range(CHUNKS - 1):
+            quantise_y(c)
         store_codes(slice(0, S2 - P))
         quantise_y(CHUNKS - 1)
         store_codes(slice(S2 - P, S2))

@@ -117,7 +117,8 @@ def tile_list_mimo_beam_channel_kernel(
 
         def weave_wr_on_gpsimd(woven, rows):
             nc.gpsimd.tensor_scalar(
-                out=woven, in0=rows.rearrange("p t (m s) -> p s m t", s=PACK), scalar1=1.0, scalar2=0.0, op0=MULT, op1=ADD
+                out=woven.rearrange("p s m t -> p m t s"), in0=rows.rearrange("p t (m s) -> p m t s", s=PACK),
+                scalar1=1.0, scalar2=0.0, op0=MULT, op1=ADD,
             )
 
         def quantise(codes, scales, woven):
@@ -217,7 +218,10 @@ def tile_list_mimo_beam_channel_kernel(
         load_wr(wr_rows[1], 1, slice(0, N))
         load_wr(wr_rows[0], 0, slice(N // 2, N))
 
-        nc.scalar.copy(out=wr_first_woven[:, :, : P // 2, :], in_=wr_early[:].rearrange("p t (m s) -> p s m t", s=PACK))
+        nc.scalar.copy(
+            out=wr_first_woven[:, :, : P // 2, :].rearrange("p s m t -> p m t s"),
+            in_=wr_early[:].rearrange("p t (m s) -> p m t s", s=PACK),
+        )
         spread = bank("y", [P, S2])
         for c in range(CHUNKS):
             nc.tensor.transpose(spread[:, chunk(c)], user_power[:, c : c + 1].to_broadcast([P, P]), ident[:])

@@ -1,7 +1,6 @@
 from contextlib import ExitStack
 
 import concourse.mybir as mybir
-from concourse.masks import make_identity
 
 K, T, S, T2, S2, N = 1024, 2048, 1024, 1024, 512, 512
 FLOPS = 2 * (2 * K * S * S2 + 2 * S * N * S2)
@@ -28,7 +27,7 @@ REAL, IMAG = 0, 1
 KB = 1024
 AT_V_REAL = 0
 AT_WR = 8 * KB
-AT_PRODUCT = AT_WR + 12 * KB
+AT_PRODUCT = AT_WR + 13 * KB
 AT_WR_EARLY = AT_PRODUCT + 11 * KB
 AT_V_WORDS = AT_PRODUCT + 16 * KB
 SLICE = 2 * KB
@@ -117,7 +116,7 @@ def tile_list_mimo_beam_channel_kernel(
 
         def weave_wr_on_gpsimd(woven, rows):
             nc.gpsimd.tensor_scalar(
-                out=woven.rearrange("p s m t -> p m t s"), in0=rows.rearrange("p t (m s) -> p m t s", s=PACK),
+                out=woven.rearrange("p s m t -> p m s t"), in0=rows.rearrange("p t (m s) -> p m s t", s=PACK),
                 scalar1=1.0, scalar2=0.0, op0=MULT, op1=ADD,
             )
 
@@ -174,7 +173,6 @@ def tile_list_mimo_beam_channel_kernel(
         y_woven = [own("y_woven%d" % c, [P, P, PACK], BF16) for c in range(CHUNKS)]
         y_codes = own("y_codes", [P, S2], U32)
         y_scales = own("y_scales", [P, S2], U8)
-        ident = own("ident", [P, P], F32)
         gain_im = own("gain_im", [P, 2, PACK], F32)
         wi_planes = own("wi_planes", [P, 2, N], U8)
         u_tables = [own("u_table%d" % a, [P, T2], U32) for a in (REAL, IMAG)]
@@ -185,16 +183,13 @@ def tile_list_mimo_beam_channel_kernel(
         v_scales_listed = own("v_scales_listed", [P, S], U8)
         gain_re = own("gain_re", [P, 2, PACK], F32)
         wr_early = at(AT_WR_EARLY, "wr_early", [P, PACK, N // 2], F32)
-        wr_first_woven = own("wr_first_woven", [P, PACK, P, PACK], BF16)
+        wr_shared_woven = own("wr_shared_woven", [P, PACK, P, PACK], BF16)
         wr_rows = [at(AT_WR + 8 * KB, "wr_rows0", [P, PACK, N // 2], F32), at(AT_WR, "wr_rows1", [P, PACK, N], F32)]
         power_rows = own("power_rows", [P, S2], F32)
         wi_codes = own("wi_codes", [P, 2, 2 * N], U8)
-        user_power = own("user_power", [P, CHUNKS], F32)
 
         for scale_tile in (v_scale_table, u_scale_table, wi_planes):
             nc.gpsimd.memset(scale_tile[:].bitcast(I32), 0)
-        nc.scalar.mul(out=ident[:].bitcast(U32), in_=ident[:].bitcast(U32), mul=0.0)
-        make_identity(nc, ident[:], nomemset=True)
 
         nc.sync.dma_start(idx2[:], offs2)
         load_words(u_tables[REAL], tab2_words[REAL])
@@ -202,9 +197,7 @@ def tile_list_mimo_beam_channel_kernel(
         load_gains(gain_im, g_im)
         load_table_scales(v_scale_table, tab_scales)
         load_table_scales(u_scale_table, tab2_scales)
-        with nc.allow_non_contiguous_dma(reason="one factor for each partition and chunk"):
-            nc.sync.dma_start(out=user_power[:], in_=power.rearrange("(c p) -> p c", p=P))
-        load_wr(wr_early, 0, slice(0, N // 2))
+        load_wr(wr_early, 1, slice(0, N // 2))
         load_words(v_table_imag, tab_words[IMAG])
         load_words(u_tables[IMAG], tab2_words[IMAG])
         nc.sync.dma_start(out=wi_codes[:].bitcast(I32), in_=wi_words.bitcast(I32).rearrange("a p n -> p a n"))
@@ -215,17 +208,14 @@ def tile_list_mimo_beam_channel_kernel(
             )
         load_words(v_table_real, tab_words[REAL])
         load_gains(gain_re, g_re)
-        load_wr(wr_rows[1], 1, slice(0, N))
-        load_wr(wr_rows[0], 0, slice(N // 2, N))
+        load_wr(wr_rows[1], 0, slice(0, N))
+        load_wr(wr_rows[0], 1, slice(N // 2, N))
+        nc.sync.dma_start(out=power_rows[:], in_=power.partition_broadcast(P))
 
         nc.scalar.copy(
-            out=wr_first_woven[:, :, : P // 2, :].rearrange("p s m t -> p m t s"),
+            out=wr_shared_woven[:, :, : P // 2, :].rearrange("p s m t -> p m t s"),
             in_=wr_early[:].rearrange("p t (m s) -> p m t s", s=PACK),
         )
-        spread = bank("y", [P, S2])
-        for c in range(CHUNKS):
-            nc.tensor.transpose(spread[:, chunk(c)], user_power[:, c : c + 1].to_broadcast([P, P]), ident[:])
-        nc.scalar.copy(out=power_rows[:], in_=spread[:])
         product = [
             [at(AT_PRODUCT + SLICE * (7 - PACK * h - t), "product%d_%d" % (h, t), [P, S2], F32) for t in range(PACK)]
             for h in halves
@@ -265,9 +255,9 @@ def tile_list_mimo_beam_channel_kernel(
         gather_v_words(v_words[REAL, 1], v_table_real, 1)
         minus_zi(0, second_products[0])
 
-        wr_second_woven = at(AT_V_REAL, "wr_second_woven", [P, PACK, P, PACK], BF16)
-        weave_wr_on_gpsimd(wr_second_woven[:], wr_rows[1][:])
-        weave_wr_on_gpsimd(wr_first_woven[:, :, P // 2 :, :], wr_rows[0][:])
+        wr_whole_woven = at(AT_V_REAL, "wr_whole_woven", [P, PACK, P, PACK], BF16)
+        weave_wr_on_gpsimd(wr_whole_woven[:], wr_rows[1][:])
+        weave_wr_on_gpsimd(wr_shared_woven[:, :, P // 2 :, :], wr_rows[0][:])
 
         for t in range(PACK):
             second_products[1].append(im_second_product(1, t, "x"))
@@ -325,14 +315,15 @@ def tile_list_mimo_beam_channel_kernel(
                 in1=power_rows[:, chunk(c)].unsqueeze(1).to_broadcast([P, PACK, P]), op=MULT,
             )
             nc.sync.dma_start(out=out_0.rearrange("(p t) j -> p t j", t=PACK)[:, :, chunk(c)], in_=y_rows[c][:])
-            weave(nc.vector.tensor_copy if c == CHUNKS - 1 else nc.scalar.copy, y_woven[c][:], y_rows[c][:])
+            if c < CHUNKS - 1:
+                weave(nc.scalar.copy, y_woven[c][:], y_rows[c][:])
 
         first_imag(0)
-        quantise(wr_codes[0][:], wr_scales[0][:], wr_first_woven[:].rearrange("p s m t -> p (s m) t"))
+        quantise(wr_codes[0][:], wr_scales[0][:], wr_whole_woven[:].rearrange("p s m t -> p (s m) t"))
         first_real(0)
         zr_second_half(0)
         first_imag(1)
-        quantise(wr_codes[1][:], wr_scales[1][:], wr_second_woven[:].rearrange("p s m t -> p (s m) t"))
+        quantise(wr_codes[1][:], wr_scales[1][:], wr_shared_woven[:].rearrange("p s m t -> p (s m) t"))
         first_real(1)
         zr_second_half(1)
         close(0)
@@ -340,12 +331,14 @@ def tile_list_mimo_beam_channel_kernel(
         close(1)
         scale_y(0)
         close(2)
-        scale_y(1)
         close(3)
+        scale_y(1)
         scale_y(2)
+        quantise_y(0)
         scale_y(3)
-        for c in range(CHUNKS - 1):
-            quantise_y(c)
+        quantise_y(1)
+        weave(nc.vector.tensor_copy, y_woven[3][:], y_rows[3][:])
+        quantise_y(2)
         store_codes(slice(0, S2 - P))
         quantise_y(CHUNKS - 1)
         store_codes(slice(S2 - P, S2))

@@ -318,14 +318,14 @@ def tile_list_mimo_beam_channel_kernel(
             if c < CHUNKS - 1:
                 weave(nc.scalar.copy, y_woven[c][:], y_rows[c][:])
 
+        zr_second_half(0)
+        zr_second_half(1)
         first_imag(0)
         quantise(wr_codes[0][:], wr_scales[0][:], wr_whole_woven[:].rearrange("p s m t -> p (s m) t"))
         first_real(0)
-        zr_second_half(0)
         first_imag(1)
         quantise(wr_codes[1][:], wr_scales[1][:], wr_shared_woven[:].rearrange("p s m t -> p (s m) t"))
         first_real(1)
-        zr_second_half(1)
         close(0)
         zr_second_half(2)
         close(1)

@@ -180,7 +180,7 @@ def tile_list_mimo_beam_channel_kernel(
         v_table_real = at(AT_V_REAL, "v_table_real", [P, T], U32)
         u_scale_table = own("u_scale_table", [P, T2], U8)
         v_scale_table = own("v_scale_table", [P, T], U8)
-        v_scales_listed = own("v_scales_listed", [P, S], U8)
+        v_scales_listed = own("v_scales_listed", [P, 2, PASS], U8)
         gain_re = own("gain_re", [P, 2, PACK], F32)
         wr_early = at(AT_WR_EARLY, "wr_early", [P, PACK, N // 2], F32)
         wr_shared_woven = own("wr_shared_woven", [P, PACK, P, PACK], BF16)
@@ -188,17 +188,17 @@ def tile_list_mimo_beam_channel_kernel(
         power_rows = own("power_rows", [P, S2], F32)
         wi_codes = own("wi_codes", [P, 2, 2 * N], U8)
 
-        for scale_tile in (v_scale_table, u_scale_table, wi_planes):
+        for scale_tile in (u_scale_table, v_scale_table, wi_planes):
             nc.gpsimd.memset(scale_tile[:].bitcast(I32), 0)
 
         nc.sync.dma_start(idx2[:], offs2)
-        load_words(u_tables[REAL], tab2_words[REAL])
         nc.sync.dma_start(idx[:], offs)
-        load_gains(gain_im, g_im)
-        load_table_scales(v_scale_table, tab_scales)
+        load_words(u_tables[REAL], tab2_words[REAL])
         load_table_scales(u_scale_table, tab2_scales)
+        load_table_scales(v_scale_table, tab_scales)
         load_wr(wr_early, 1, slice(0, N // 2))
         load_words(v_table_imag, tab_words[IMAG])
+        load_gains(gain_im, g_im)
         load_words(u_tables[IMAG], tab2_words[IMAG])
         nc.sync.dma_start(out=wi_codes[:].bitcast(I32), in_=wi_words.bitcast(I32).rearrange("a p n -> p a n"))
         for q in range(4):
@@ -221,12 +221,14 @@ def tile_list_mimo_beam_channel_kernel(
             for h in halves
         ]
         nc.vector.tensor_copy(u_words[REAL][:], u_tables[REAL][:].indirect(idx2[:]))
-        nc.vector.tensor_copy(v_scales_listed[:], v_scale_table[:].indirect(idx[:]))
         nc.vector.tensor_copy(u_scales[:], u_scale_table[:].indirect(idx2[:]))
-        nc.vector.tensor_copy(
-            v_scales[:].rearrange("p h (t m) -> p h t m", t=PACK),
-            v_scales_listed[:].rearrange("p (h m t) -> p h t m", h=2, t=PACK),
-        )
+        for h in halves:
+            nc.vector.tensor_copy(v_scales_listed[:, h, :], v_scale_table[:].indirect(half_list(h)))
+        for h in halves:
+            nc.vector.tensor_copy(
+                v_scales[:, h, :].rearrange("p (t m) -> p t m", t=PACK),
+                v_scales_listed[:, h, :].rearrange("p (m t) -> p t m", t=PACK),
+            )
         for h, ring in ((0, "x"), (1, "y")):
             gather_v_words(v_words[IMAG, h], v_table_imag, h)
             im_first_product(h, ring)
@@ -263,9 +265,16 @@ def tile_list_mimo_beam_channel_kernel(
             second_products[1].append(im_second_product(1, t, "x"))
         minus_zi(1, second_products[1])
         zi_woven = [at(AT_V_WORDS, "zi_woven0", [P, S2, PACK], BF16), own("zi_woven1", [P, S2, PACK], BF16)]
-        for b in halves:
-            weave(nc.scalar.copy, zi_woven[0][:, user_half(b), :], zi_slices[0][:, :, user_half(b)])
+        nc.gpsimd.tensor_scalar(
+            out=zi_woven[0][:, chunk(3), :], in0=zi_slices[0][:, :, chunk(3)].rearrange("p t j -> p j t"),
+            scalar1=1.0, scalar2=0.0, op0=MULT, op1=ADD,
+        )
+        for b, users in ((0, user_half(0)), (1, chunk(2))):
+            weave(nc.scalar.copy, zi_woven[0][:, users, :], zi_slices[0][:, :, users])
             weave(nc.scalar.copy, zr_woven[0][:, user_half(b), :], zr_slices[:, :, user_half(b)])
+            if b == 0:
+                for c in (0, 1):
+                    weave(nc.scalar.copy, zi_woven[1][:, chunk(c), :], zi_slices[1][:, :, chunk(c)])
         re_second = []
         for c in range(CHUNKS):
             re_second.append(bank("y", [P, PACK, P]))
@@ -274,8 +283,6 @@ def tile_list_mimo_beam_channel_kernel(
                     first_stage(re_second[c][:, t, :], a, a, 1, t, chunk(c), a == REAL, a == IMAG)
         zr_last_slices = own("zr_last_slices", [P, PACK, P], BF16)
         zr_last_woven = own("zr_last_woven", [P, P, PACK], BF16)
-        for c in (0, 1):
-            weave(nc.scalar.copy, zi_woven[1][:, chunk(c), :], zi_slices[1][:, :, chunk(c)])
         for t in range(PACK):
             nc.scalar.activation(
                 out=zr_last_slices[:, t, :], in_=re_second[CHUNKS - 1][:, t, :], func=COPY, scale=gain_re[:, 1, t : t + 1]
@@ -323,12 +330,12 @@ def tile_list_mimo_beam_channel_kernel(
         first_imag(0)
         quantise(wr_codes[0][:], wr_scales[0][:], wr_whole_woven[:].rearrange("p s m t -> p (s m) t"))
         first_real(0)
-        first_imag(1)
         quantise(wr_codes[1][:], wr_scales[1][:], wr_shared_woven[:].rearrange("p s m t -> p (s m) t"))
-        first_real(1)
         close(0)
-        zr_second_half(2)
         close(1)
+        first_imag(1)
+        first_real(1)
+        zr_second_half(2)
         scale_y(0)
         close(2)
         close(3)

@@ -24,11 +24,12 @@ PASS = P * PACK
 CHUNKS = S2 // P
 RUN = 4
 REAL, IMAG = 0, 1
+WR_EARLY = 128
 KB = 1024
 AT_V_REAL = 0
 AT_WR = 8 * KB
-AT_PRODUCT = AT_WR + 13 * KB
-AT_WR_EARLY = AT_PRODUCT + 11 * KB
+AT_PRODUCT = AT_WR + 17 * KB
+AT_WR_EARLY = AT_PRODUCT + 13 * KB
 AT_V_WORDS = AT_PRODUCT + 16 * KB
 SLICE = 2 * KB
 
@@ -182,9 +183,9 @@ def tile_list_mimo_beam_channel_kernel(
         v_scale_table = own("v_scale_table", [P, T], U8)
         v_scales_listed = own("v_scales_listed", [P, 2, PASS], U8)
         gain_re = own("gain_re", [P, 2, PACK], F32)
-        wr_early = at(AT_WR_EARLY, "wr_early", [P, PACK, N // 2], F32)
+        wr_early = at(AT_WR_EARLY, "wr_early", [P, PACK, WR_EARLY], F32)
         wr_shared_woven = own("wr_shared_woven", [P, PACK, P, PACK], BF16)
-        wr_rows = [at(AT_WR + 8 * KB, "wr_rows0", [P, PACK, N // 2], F32), at(AT_WR, "wr_rows1", [P, PACK, N], F32)]
+        wr_rows = [at(AT_WR + 8 * KB, "wr_rows0", [P, PACK, N - WR_EARLY], F32), at(AT_WR, "wr_rows1", [P, PACK, N], F32)]
         power_rows = own("power_rows", [P, S2], F32)
         wi_codes = own("wi_codes", [P, 2, 2 * N], U8)
 
@@ -196,7 +197,7 @@ def tile_list_mimo_beam_channel_kernel(
         load_words(u_tables[REAL], tab2_words[REAL])
         load_table_scales(u_scale_table, tab2_scales)
         load_table_scales(v_scale_table, tab_scales)
-        load_wr(wr_early, 1, slice(0, N // 2))
+        load_wr(wr_early, 1, slice(0, WR_EARLY))
         load_words(v_table_imag, tab_words[IMAG])
         load_gains(gain_im, g_im)
         load_words(u_tables[IMAG], tab2_words[IMAG])
@@ -209,11 +210,11 @@ def tile_list_mimo_beam_channel_kernel(
         load_words(v_table_real, tab_words[REAL])
         load_gains(gain_re, g_re)
         load_wr(wr_rows[1], 0, slice(0, N))
-        load_wr(wr_rows[0], 1, slice(N // 2, N))
+        load_wr(wr_rows[0], 1, slice(WR_EARLY, N))
         nc.sync.dma_start(out=power_rows[:], in_=power.partition_broadcast(P))
 
         nc.scalar.copy(
-            out=wr_shared_woven[:, :, : P // 2, :].rearrange("p s m t -> p m t s"),
+            out=wr_shared_woven[:, :, : WR_EARLY // PACK, :].rearrange("p s m t -> p m t s"),
             in_=wr_early[:].rearrange("p t (m s) -> p m t s", s=PACK),
         )
         product = [
@@ -259,17 +260,13 @@ def tile_list_mimo_beam_channel_kernel(
 
         wr_whole_woven = at(AT_V_REAL, "wr_whole_woven", [P, PACK, P, PACK], BF16)
         weave_wr_on_gpsimd(wr_whole_woven[:], wr_rows[1][:])
-        weave_wr_on_gpsimd(wr_shared_woven[:, :, P // 2 :, :], wr_rows[0][:])
+        weave_wr_on_gpsimd(wr_shared_woven[:, :, WR_EARLY // PACK :, :], wr_rows[0][:])
 
         for t in range(PACK):
             second_products[1].append(im_second_product(1, t, "x"))
         minus_zi(1, second_products[1])
         zi_woven = [at(AT_V_WORDS, "zi_woven0", [P, S2, PACK], BF16), own("zi_woven1", [P, S2, PACK], BF16)]
-        nc.gpsimd.tensor_scalar(
-            out=zi_woven[0][:, chunk(3), :], in0=zi_slices[0][:, :, chunk(3)].rearrange("p t j -> p j t"),
-            scalar1=1.0, scalar2=0.0, op0=MULT, op1=ADD,
-        )
-        for b, users in ((0, user_half(0)), (1, chunk(2))):
+        for b, users in ((0, user_half(0)), (1, user_half(1))):
             weave(nc.scalar.copy, zi_woven[0][:, users, :], zi_slices[0][:, :, users])
             weave(nc.scalar.copy, zr_woven[0][:, user_half(b), :], zr_slices[:, :, user_half(b)])
             if b == 0:
@@ -344,11 +341,11 @@ def tile_list_mimo_beam_channel_kernel(
         quantise_y(0)
         scale_y(3)
         quantise_y(1)
+        store_codes(user_half(0))
         weave(nc.vector.tensor_copy, y_woven[3][:], y_rows[3][:])
         quantise_y(2)
-        store_codes(slice(0, S2 - P))
-        quantise_y(CHUNKS - 1)
-        store_codes(slice(S2 - P, S2))
+        quantise_y(3)
+        store_codes(user_half(1))
         for q in range(4):
             queue = nc.scalar if q % 2 else nc.sync
             queue.dma_start(

@@ -266,12 +266,12 @@ def tile_list_mimo_beam_channel_kernel(
             second_products[1].append(im_second_product(1, t, "x"))
         minus_zi(1, second_products[1])
         zi_woven = [at(AT_V_WORDS, "zi_woven0", [P, S2, PACK], BF16), own("zi_woven1", [P, S2, PACK], BF16)]
-        for b, users in ((0, user_half(0)), (1, user_half(1))):
-            weave(nc.scalar.copy, zi_woven[0][:, users, :], zi_slices[0][:, :, users])
-            weave(nc.scalar.copy, zr_woven[0][:, user_half(b), :], zr_slices[:, :, user_half(b)])
-            if b == 0:
-                for c in (0, 1):
-                    weave(nc.scalar.copy, zi_woven[1][:, chunk(c), :], zi_slices[1][:, :, chunk(c)])
+        weave(nc.scalar.copy, zi_woven[0][:, user_half(0), :], zi_slices[0][:, :, user_half(0)])
+        weave(nc.scalar.copy, zr_woven[0][:, user_half(0), :], zr_slices[:, :, user_half(0)])
+        weave(nc.scalar.copy, zi_woven[0][:, user_half(1), :], zi_slices[0][:, :, user_half(1)])
+        for c in (0, 1):
+            weave(nc.scalar.copy, zi_woven[1][:, chunk(c), :], zi_slices[1][:, :, chunk(c)])
+        weave(nc.scalar.copy, zr_woven[0][:, user_half(1), :], zr_slices[:, :, user_half(1)])
         re_second = []
         for c in range(CHUNKS):
             re_second.append(bank("y", [P, PACK, P]))
@@ -325,12 +325,12 @@ def tile_list_mimo_beam_channel_kernel(
         zr_second_half(0)
         zr_second_half(1)
         first_imag(0)
+        first_imag(1)
         quantise(wr_codes[0][:], wr_scales[0][:], wr_whole_woven[:].rearrange("p s m t -> p (s m) t"))
         first_real(0)
         quantise(wr_codes[1][:], wr_scales[1][:], wr_shared_woven[:].rearrange("p s m t -> p (s m) t"))
         close(0)
         close(1)
-        first_imag(1)
         first_real(1)
         zr_second_half(2)
         scale_y(0)
@@ -339,9 +339,10 @@ def tile_list_mimo_beam_channel_kernel(
         scale_y(1)
         scale_y(2)
         quantise_y(0)
+        store_codes(chunk(0))
         scale_y(3)
         quantise_y(1)
-        store_codes(user_half(0))
+        store_codes(chunk(1))
         weave(nc.vector.tensor_copy, y_woven[3][:], y_rows[3][:])
         quantise_y(2)
         quantise_y(3)

@@ -181,7 +181,6 @@ def tile_list_mimo_beam_channel_kernel(
         v_table_real = at(AT_V_REAL, "v_table_real", [P, T], U32)
         u_scale_table = own("u_scale_table", [P, T2], U8)
         v_scale_table = own("v_scale_table", [P, T], U8)
-        v_scales_listed = own("v_scales_listed", [P, 2, PASS], U8)
         gain_re = own("gain_re", [P, 2, PACK], F32)
         wr_early = at(AT_WR_EARLY, "wr_early", [P, PACK, WR_EARLY], F32)
         wr_shared_woven = own("wr_shared_woven", [P, PACK, P, PACK], BF16)
@@ -224,11 +223,8 @@ def tile_list_mimo_beam_channel_kernel(
         nc.vector.tensor_copy(u_words[REAL][:], u_tables[REAL][:].indirect(idx2[:]))
         nc.vector.tensor_copy(u_scales[:], u_scale_table[:].indirect(idx2[:]))
         for h in halves:
-            nc.vector.tensor_copy(v_scales_listed[:, h, :], v_scale_table[:].indirect(half_list(h)))
-        for h in halves:
             nc.vector.tensor_copy(
-                v_scales[:, h, :].rearrange("p (t m) -> p t m", t=PACK),
-                v_scales_listed[:, h, :].rearrange("p (m t) -> p t m", t=PACK),
+                v_scales[:, h, :].rearrange("p (t m) -> p m t", t=PACK), v_scale_table[:].indirect(half_list(h))
             )
         for h, ring in ((0, "x"), (1, "y")):
             gather_v_words(v_words[IMAG, h], v_table_imag, h)

@@ -29,8 +29,9 @@ KB = 1024
 AT_V_REAL = 0
 AT_WR = 8 * KB
 AT_PRODUCT = AT_WR + 17 * KB
-AT_WR_EARLY = AT_PRODUCT + 13 * KB
+AT_WR_EARLY = AT_PRODUCT + 8 * KB
 AT_V_WORDS = AT_PRODUCT + 16 * KB
+AT_WI = AT_V_WORDS + 4 * KB
 SLICE = 2 * KB
 
 
@@ -84,7 +85,7 @@ def tile_list_mimo_beam_channel_kernel(
             nc.tensor.matmul_mx(
                 out=out,
                 lhsT=v_words[v_pass, h][:, chunk(t)].bitcast(FP8X4),
-                lhsT_scale=v_scales[4 * v_pass :, h, chunk(t)],
+                lhsT_scale=v_scales[h][4 * v_pass :, chunk(t)],
                 rhs=u_words[u_pass][:, users].bitcast(FP8X4),
                 rhs_scale=u_scales[4 * u_pass :, users],
                 start=start,
@@ -95,7 +96,7 @@ def tile_list_mimo_beam_channel_kernel(
             for t in range(PACK):
                 sums = bank(ring, [P, S2])
                 first_stage(sums[:], IMAG, REAL, h, t, everyone, True, True)
-                nc.scalar.activation(out=product[h][t][:], in_=sums[:], func=COPY, scale=gain_im[:, h, t : t + 1])
+                nc.scalar.activation(out=product[h][t], in_=sums[:], func=COPY, scale=gain_im[:, h, t : t + 1])
 
         def im_second_product(h, t, ring):
             sums = bank(ring, [P, S2])
@@ -105,7 +106,7 @@ def tile_list_mimo_beam_channel_kernel(
         def minus_zi(h, banks):
             for t in range(PACK):
                 nc.vector.scalar_tensor_tensor(
-                    out=zi_slices[h][:, t, :], in0=banks[t][:], scalar=gain_im[:, h, t : t + 1], in1=product[h][t][:],
+                    out=zi_slices[h][:, t, :], in0=banks[t][:], scalar=gain_im[:, h, t : t + 1], in1=product[h][t],
                     op0=MULT, op1=SUB,
                 )
 
@@ -160,9 +161,9 @@ def tile_list_mimo_beam_channel_kernel(
         idx = keep.tile([P, S // 16], U16, name="idx")
         idx2 = keep.tile([P, S2 // 16], U16, name="idx2")
         u_scales = own("u_scales", [P, S2], U8)
-        v_scales = own("v_scales", [P, 2, PASS], U8)
+        v_scales = [own("v_scales%d" % h, [P, PASS], U8) for h in halves]
         u_words = {a: own("u_words%d" % a, [P, S2], U32) for a in (REAL, IMAG)}
-        v_words = {(IMAG, h): own("v_words_imag%d" % h, [P, PASS], U32) for h in halves}
+        v_words = {(IMAG, 0): own("v_words_imag0", [P, PASS], U32)}
         v_words[REAL, 0] = at(AT_V_WORDS, "v_words_real0", [P, PASS], U32)
         wr_scales = [own("wr_scales%d" % h, [P, N], U8) for h in halves]
         zr_slices = own("zr_slices", [P, PACK, S2], BF16)
@@ -186,21 +187,21 @@ def tile_list_mimo_beam_channel_kernel(
         wr_shared_woven = own("wr_shared_woven", [P, PACK, P, PACK], BF16)
         wr_rows = [at(AT_WR + 8 * KB, "wr_rows0", [P, PACK, N - WR_EARLY], F32), at(AT_WR, "wr_rows1", [P, PACK, N], F32)]
         power_rows = own("power_rows", [P, S2], F32)
-        wi_codes = own("wi_codes", [P, 2, 2 * N], U8)
+        wi_codes = at(AT_WI, "wi_codes", [P, 2, 2 * N], U8)
 
         for scale_tile in (u_scale_table, v_scale_table, wi_planes):
             nc.gpsimd.memset(scale_tile[:].bitcast(I32), 0)
 
-        nc.sync.dma_start(idx2[:], offs2)
-        nc.sync.dma_start(idx[:], offs)
         load_words(u_tables[REAL], tab2_words[REAL])
+        nc.sync.dma_start(idx2[:], offs2)
         load_table_scales(u_scale_table, tab2_scales)
-        load_table_scales(v_scale_table, tab_scales)
-        load_wr(wr_early, 1, slice(0, WR_EARLY))
+        nc.sync.dma_start(idx[:], offs)
         load_words(v_table_imag, tab_words[IMAG])
+        load_table_scales(v_scale_table, tab_scales)
         load_gains(gain_im, g_im)
-        load_words(u_tables[IMAG], tab2_words[IMAG])
         nc.sync.dma_start(out=wi_codes[:].bitcast(I32), in_=wi_words.bitcast(I32).rearrange("a p n -> p a n"))
+        load_wr(wr_early, 1, slice(0, WR_EARLY))
+        load_words(u_tables[IMAG], tab2_words[IMAG])
         for q in range(4):
             nc.sync.dma_start(
                 out=wi_planes[32 * q : 32 * q + 4, :, :].bitcast(I32),
@@ -212,34 +213,37 @@ def tile_list_mimo_beam_channel_kernel(
         load_wr(wr_rows[0], 1, slice(WR_EARLY, N))
         nc.sync.dma_start(out=power_rows[:], in_=power.partition_broadcast(P))
 
+        wi_dealt = own("wi_dealt", [P, 2, 2 * N], U8)
+        nc.scalar.copy(
+            out=wi_dealt[:].bitcast(U16).rearrange("p h (s m) -> p h s m", s=PACK),
+            in_=wi_codes[:].bitcast(U16).rearrange("p h (m s) -> p h s m", s=PACK),
+        )
         nc.scalar.copy(
             out=wr_shared_woven[:, :, : WR_EARLY // PACK, :].rearrange("p s m t -> p m t s"),
             in_=wr_early[:].rearrange("p t (m s) -> p m t s", s=PACK),
         )
+        product_first = at(AT_PRODUCT + PACK * SLICE, "product0", [P, PACK, S2], F32)
         product = [
-            [at(AT_PRODUCT + SLICE * (7 - PACK * h - t), "product%d_%d" % (h, t), [P, S2], F32) for t in range(PACK)]
-            for h in halves
+            [product_first[:, t, :] for t in range(PACK)],
+            [at(AT_PRODUCT + SLICE * (3 - t), "product1_%d" % t, [P, S2], F32)[:] for t in range(PACK)],
         ]
         nc.vector.tensor_copy(u_words[REAL][:], u_tables[REAL][:].indirect(idx2[:]))
         nc.vector.tensor_copy(u_scales[:], u_scale_table[:].indirect(idx2[:]))
+        gather_v_words(v_words[IMAG, 0], v_table_imag, 0)
         for h in halves:
             nc.vector.tensor_copy(
-                v_scales[:, h, :].rearrange("p (t m) -> p m t", t=PACK), v_scale_table[:].indirect(half_list(h))
+                v_scales[h][:].rearrange("p (t m) -> p m t", t=PACK), v_scale_table[:].indirect(half_list(h))
             )
-        for h, ring in ((0, "x"), (1, "y")):
-            gather_v_words(v_words[IMAG, h], v_table_imag, h)
-            im_first_product(h, ring)
+        im_first_product(0, "x")
+        v_words[IMAG, 1] = at(AT_WI, "v_words_imag1", [P, PASS], U32)
+        gather_v_words(v_words[IMAG, 1], v_table_imag, 1)
+        im_first_product(1, "y")
 
         nc.vector.tensor_copy(u_words[IMAG][:], u_tables[IMAG][:].indirect(idx2[:]))
         re_first = [bank("x", [P, S2]) for t in range(PACK)]
         for t in range(PACK):
             first_stage(re_first[t][:], IMAG, IMAG, 0, t, everyone, True, False)
-        wi_dealt = own("wi_dealt", [P, 2, 2 * N], U8)
         wi_scales_dealt = own("wi_scales_dealt", [P, 2, N], U8)
-        nc.vector.tensor_copy(
-            wi_dealt[:].bitcast(U16).rearrange("p h (s m) -> p h s m", s=PACK),
-            wi_codes[:].bitcast(U16).rearrange("p h (m s) -> p h s m", s=PACK),
-        )
         nc.vector.tensor_copy(
             wi_scales_dealt[:].rearrange("p h (s m) -> p h s m", s=PACK),
             wi_planes[:].rearrange("p h (m s) -> p h s m", s=PACK),

@@ -24,14 +24,12 @@ PASS = P * PACK
 CHUNKS = S2 // P
 RUN = 4
 REAL, IMAG = 0, 1
-WR_EARLY = 128
 KB = 1024
 AT_V_REAL = 0
 AT_WR = 8 * KB
 AT_PRODUCT = AT_WR + 17 * KB
-AT_WR_EARLY = AT_PRODUCT + 8 * KB
 AT_V_WORDS = AT_PRODUCT + 16 * KB
-AT_WI = AT_V_WORDS + 4 * KB
+AT_WI = AT_PRODUCT + 7 * KB
 SLICE = 2 * KB
 
 
@@ -96,7 +94,7 @@ def tile_list_mimo_beam_channel_kernel(
             for t in range(PACK):
                 sums = bank(ring, [P, S2])
                 first_stage(sums[:], IMAG, REAL, h, t, everyone, True, True)
-                nc.scalar.activation(out=product[h][t], in_=sums[:], func=COPY, scale=gain_im[:, h, t : t + 1])
+                nc.scalar.activation(out=product[h][:, t, :], in_=sums[:], func=COPY, scale=gain_im[:, h, t : t + 1])
 
         def im_second_product(h, t, ring):
             sums = bank(ring, [P, S2])
@@ -106,7 +104,7 @@ def tile_list_mimo_beam_channel_kernel(
         def minus_zi(h, banks):
             for t in range(PACK):
                 nc.vector.scalar_tensor_tensor(
-                    out=zi_slices[h][:, t, :], in0=banks[t][:], scalar=gain_im[:, h, t : t + 1], in1=product[h][t],
+                    out=zi_slices[h][:, t, :], in0=banks[t][:], scalar=gain_im[:, h, t : t + 1], in1=product[h][:, t, :],
                     op0=MULT, op1=SUB,
                 )
 
@@ -163,7 +161,7 @@ def tile_list_mimo_beam_channel_kernel(
         u_scales = own("u_scales", [P, S2], U8)
         v_scales = [own("v_scales%d" % h, [P, PASS], U8) for h in halves]
         u_words = {a: own("u_words%d" % a, [P, S2], U32) for a in (REAL, IMAG)}
-        v_words = {(IMAG, 0): own("v_words_imag0", [P, PASS], U32)}
+        v_words = {(IMAG, h): own("v_words_imag%d" % h, [P, PASS], U32) for h in halves}
         v_words[REAL, 0] = at(AT_V_WORDS, "v_words_real0", [P, PASS], U32)
         wr_scales = [own("wr_scales%d" % h, [P, N], U8) for h in halves]
         zr_slices = own("zr_slices", [P, PACK, S2], BF16)
@@ -183,9 +181,8 @@ def tile_list_mimo_beam_channel_kernel(
         u_scale_table = own("u_scale_table", [P, T2], U8)
         v_scale_table = own("v_scale_table", [P, T], U8)
         gain_re = own("gain_re", [P, 2, PACK], F32)
-        wr_early = at(AT_WR_EARLY, "wr_early", [P, PACK, WR_EARLY], F32)
         wr_shared_woven = own("wr_shared_woven", [P, PACK, P, PACK], BF16)
-        wr_rows = [at(AT_WR + 8 * KB, "wr_rows0", [P, PACK, N - WR_EARLY], F32), at(AT_WR, "wr_rows1", [P, PACK, N], F32)]
+        wr_rows = [at(AT_WR + 8 * KB, "wr_rows0", [P, PACK, N], F32), at(AT_WR, "wr_rows1", [P, PACK, N], F32)]
         power_rows = own("power_rows", [P, S2], F32)
         wi_codes = at(AT_WI, "wi_codes", [P, 2, 2 * N], U8)
 
@@ -196,11 +193,10 @@ def tile_list_mimo_beam_channel_kernel(
         nc.sync.dma_start(idx2[:], offs2)
         load_table_scales(u_scale_table, tab2_scales)
         nc.sync.dma_start(idx[:], offs)
-        load_words(v_table_imag, tab_words[IMAG])
         load_table_scales(v_scale_table, tab_scales)
+        load_words(v_table_imag, tab_words[IMAG])
         load_gains(gain_im, g_im)
         nc.sync.dma_start(out=wi_codes[:].bitcast(I32), in_=wi_words.bitcast(I32).rearrange("a p n -> p a n"))
-        load_wr(wr_early, 1, slice(0, WR_EARLY))
         load_words(u_tables[IMAG], tab2_words[IMAG])
         for q in range(4):
             nc.sync.dma_start(
@@ -210,7 +206,7 @@ def tile_list_mimo_beam_channel_kernel(
         load_words(v_table_real, tab_words[REAL])
         load_gains(gain_re, g_re)
         load_wr(wr_rows[1], 0, slice(0, N))
-        load_wr(wr_rows[0], 1, slice(WR_EARLY, N))
+        load_wr(wr_rows[0], 1, slice(0, N))
         nc.sync.dma_start(out=power_rows[:], in_=power.partition_broadcast(P))
 
         wi_dealt = own("wi_dealt", [P, 2, 2 * N], U8)
@@ -218,26 +214,16 @@ def tile_list_mimo_beam_channel_kernel(
             out=wi_dealt[:].bitcast(U16).rearrange("p h (s m) -> p h s m", s=PACK),
             in_=wi_codes[:].bitcast(U16).rearrange("p h (m s) -> p h s m", s=PACK),
         )
-        nc.scalar.copy(
-            out=wr_shared_woven[:, :, : WR_EARLY // PACK, :].rearrange("p s m t -> p m t s"),
-            in_=wr_early[:].rearrange("p t (m s) -> p m t s", s=PACK),
-        )
-        product_first = at(AT_PRODUCT + PACK * SLICE, "product0", [P, PACK, S2], F32)
-        product = [
-            [product_first[:, t, :] for t in range(PACK)],
-            [at(AT_PRODUCT + SLICE * (3 - t), "product1_%d" % t, [P, S2], F32)[:] for t in range(PACK)],
-        ]
+        product = [at(AT_PRODUCT + PACK * SLICE * (1 - h), "product%d" % h, [P, PACK, S2], F32) for h in halves]
         nc.vector.tensor_copy(u_words[REAL][:], u_tables[REAL][:].indirect(idx2[:]))
         nc.vector.tensor_copy(u_scales[:], u_scale_table[:].indirect(idx2[:]))
-        gather_v_words(v_words[IMAG, 0], v_table_imag, 0)
         for h in halves:
             nc.vector.tensor_copy(
                 v_scales[h][:].rearrange("p (t m) -> p m t", t=PACK), v_scale_table[:].indirect(half_list(h))
             )
-        im_first_product(0, "x")
-        v_words[IMAG, 1] = at(AT_WI, "v_words_imag1", [P, PASS], U32)
-        gather_v_words(v_words[IMAG, 1], v_table_imag, 1)
-        im_first_product(1, "y")
+        for h, ring in ((0, "x"), (1, "y")):
+            gather_v_words(v_words[IMAG, h], v_table_imag, h)
+            im_first_product(h, ring)
 
         nc.vector.tensor_copy(u_words[IMAG][:], u_tables[IMAG][:].indirect(idx2[:]))
         re_first = [bank("x", [P, S2]) for t in range(PACK)]
@@ -260,7 +246,7 @@ def tile_list_mimo_beam_channel_kernel(
 
         wr_whole_woven = at(AT_V_REAL, "wr_whole_woven", [P, PACK, P, PACK], BF16)
         weave_wr_on_gpsimd(wr_whole_woven[:], wr_rows[1][:])
-        weave_wr_on_gpsimd(wr_shared_woven[:, :, WR_EARLY // PACK :, :], wr_rows[0][:])
+        weave_wr_on_gpsimd(wr_shared_woven[:], wr_rows[0][:])
 
         for t in range(PACK):
             second_products[1].append(im_second_product(1, t, "x"))

@@ -189,13 +189,13 @@ def tile_list_mimo_beam_channel_kernel(
         for scale_tile in (u_scale_table, v_scale_table, wi_planes):
             nc.gpsimd.memset(scale_tile[:].bitcast(I32), 0)
 
-        load_words(u_tables[REAL], tab2_words[REAL])
         nc.sync.dma_start(idx2[:], offs2)
-        load_table_scales(u_scale_table, tab2_scales)
         nc.sync.dma_start(idx[:], offs)
+        load_words(u_tables[REAL], tab2_words[REAL])
+        load_table_scales(u_scale_table, tab2_scales)
         load_table_scales(v_scale_table, tab_scales)
-        load_words(v_table_imag, tab_words[IMAG])
         load_gains(gain_im, g_im)
+        load_words(v_table_imag, tab_words[IMAG])
         nc.sync.dma_start(out=wi_codes[:].bitcast(I32), in_=wi_words.bitcast(I32).rearrange("a p n -> p a n"))
         load_words(u_tables[IMAG], tab2_words[IMAG])
         for q in range(4):
@@ -249,7 +249,7 @@ def tile_list_mimo_beam_channel_kernel(
         weave_wr_on_gpsimd(wr_shared_woven[:], wr_rows[0][:])
 
         for t in range(PACK):
-            second_products[1].append(im_second_product(1, t, "x"))
+            second_products[1].append(im_second_product(1, t, "y"))
         minus_zi(1, second_products[1])
         zi_woven = [at(AT_V_WORDS, "zi_woven0", [P, S2, PACK], BF16), own("zi_woven1", [P, S2, PACK], BF16)]
         weave(nc.scalar.copy, zi_woven[0][:, user_half(0), :], zi_slices[0][:, :, user_half(0)])
@@ -260,7 +260,7 @@ def tile_list_mimo_beam_channel_kernel(
         weave(nc.scalar.copy, zr_woven[0][:, user_half(1), :], zr_slices[:, :, user_half(1)])
         re_second = []
         for c in range(CHUNKS):
-            re_second.append(bank("y", [P, PACK, P]))
+            re_second.append(bank("x", [P, PACK, P]))
             for t in range(PACK):
                 for a in (REAL, IMAG):
                     first_stage(re_second[c][:, t, :], a, a, 1, t, chunk(c), a == REAL, a == IMAG)
@@ -280,7 +280,7 @@ def tile_list_mimo_beam_channel_kernel(
         def quantise_users(codes, scales, woven, users):
             quantise(codes[:, users], scales[:, users], woven[:, users, :])
 
-        y_sums = [bank("x", [P, PACK, P]) for c in range(CHUNKS)]
+        y_sums = [bank("y", [P, PACK, P]) for c in range(CHUNKS)]
 
         def close(c):
             woven = zr_last_woven[:] if c == CHUNKS - 1 else zr_woven[1][:, chunk(c), :]

@@ -24,6 +24,7 @@ PASS = P * PACK
 CHUNKS = S2 // P
 RUN = 4
 REAL, IMAG = 0, 1
+WR_EARLY = 128
 KB = 1024
 AT_V_REAL = 0
 AT_WR = 8 * KB
@@ -182,7 +183,8 @@ def tile_list_mimo_beam_channel_kernel(
         v_scale_table = own("v_scale_table", [P, T], U8)
         gain_re = own("gain_re", [P, 2, PACK], F32)
         wr_shared_woven = own("wr_shared_woven", [P, PACK, P, PACK], BF16)
-        wr_rows = [at(AT_WR + 8 * KB, "wr_rows0", [P, PACK, N], F32), at(AT_WR, "wr_rows1", [P, PACK, N], F32)]
+        wr_rows = [at(AT_WR + 8 * KB, "wr_rows0", [P, PACK, N - WR_EARLY], F32), at(AT_WR, "wr_rows1", [P, PACK, N], F32)]
+        wr_early = own("wr_early", [P, PACK, WR_EARLY], F32)
         power_rows = own("power_rows", [P, S2], F32)
         wi_codes = at(AT_WI, "wi_codes", [P, 2, 2 * N], U8)
 
@@ -194,8 +196,9 @@ def tile_list_mimo_beam_channel_kernel(
         load_words(u_tables[REAL], tab2_words[REAL])
         load_table_scales(u_scale_table, tab2_scales)
         load_table_scales(v_scale_table, tab_scales)
-        load_gains(gain_im, g_im)
+        load_wr(wr_early, 1, slice(0, WR_EARLY))
         load_words(v_table_imag, tab_words[IMAG])
+        load_gains(gain_im, g_im)
         nc.sync.dma_start(out=wi_codes[:].bitcast(I32), in_=wi_words.bitcast(I32).rearrange("a p n -> p a n"))
         load_words(u_tables[IMAG], tab2_words[IMAG])
         for q in range(4):
@@ -206,9 +209,13 @@ def tile_list_mimo_beam_channel_kernel(
         load_words(v_table_real, tab_words[REAL])
         load_gains(gain_re, g_re)
         load_wr(wr_rows[1], 0, slice(0, N))
-        load_wr(wr_rows[0], 1, slice(0, N))
+        load_wr(wr_rows[0], 1, slice(WR_EARLY, N))
         nc.sync.dma_start(out=power_rows[:], in_=power.partition_broadcast(P))
 
+        nc.scalar.copy(
+            out=wr_shared_woven[:, :, : WR_EARLY // PACK, :].rearrange("p s m t -> p m t s"),
+            in_=wr_early[:].rearrange("p t (m s) -> p m t s", s=PACK),
+        )
         wi_dealt = own("wi_dealt", [P, 2, 2 * N], U8)
         nc.scalar.copy(
             out=wi_dealt[:].bitcast(U16).rearrange("p h (s m) -> p h s m", s=PACK),
@@ -246,7 +253,7 @@ def tile_list_mimo_beam_channel_kernel(
 
         wr_whole_woven = at(AT_V_REAL, "wr_whole_woven", [P, PACK, P, PACK], BF16)
         weave_wr_on_gpsimd(wr_whole_woven[:], wr_rows[1][:])
-        weave_wr_on_gpsimd(wr_shared_woven[:], wr_rows[0][:])
+        weave_wr_on_gpsimd(wr_shared_woven[:, :, WR_EARLY // PACK :, :], wr_rows[0][:])
 
         for t in range(PACK):
             second_products[1].append(im_second_product(1, t, "y"))

@@ -137,7 +137,7 @@ def tile_list_mimo_beam_channel_kernel(
             second_stage(c, wr_codes[h][:], wr_scales[h][:], FP8X4, zr_codes[h], zr_scales[h], start, False)
 
         def imag_pass(c, h, start, stop):
-            second_stage(c, wi_dealt[:, h, :], wi_scales_dealt[:, h, :], FP4X4, zi_codes[h], zi_scales[h], start, stop)
+            second_stage(c, wi_dealt[:, h, :], wi_scales_by_half[h][:], FP4X4, zi_codes[h], zi_scales[h], start, stop)
 
         def zr_second_half(c):
             nc.vector.tensor_tensor(
@@ -175,7 +175,8 @@ def tile_list_mimo_beam_channel_kernel(
         y_codes = own("y_codes", [P, S2], U32)
         y_scales = own("y_scales", [P, S2], U8)
         gain_im = own("gain_im", [P, 2, PACK], F32)
-        wi_planes = own("wi_planes", [P, 2, N], U8)
+        wi_planes = own("wi_planes", [P, N], U8)
+        wi_scales_second = own("wi_scales_second", [P, N], U8)
         u_tables = [own("u_table%d" % a, [P, T2], U32) for a in (REAL, IMAG)]
         v_table_imag = own("v_table_imag", [P, T], U32)
         v_table_real = at(AT_V_REAL, "v_table_real", [P, T], U32)
@@ -188,7 +189,7 @@ def tile_list_mimo_beam_channel_kernel(
         power_rows = own("power_rows", [P, S2], F32)
         wi_codes = at(AT_WI, "wi_codes", [P, 2, 2 * N], U8)
 
-        for scale_tile in (u_scale_table, v_scale_table, wi_planes):
+        for scale_tile in (u_scale_table, v_scale_table, wi_planes, wi_scales_second):
             nc.gpsimd.memset(scale_tile[:].bitcast(I32), 0)
 
         nc.sync.dma_start(idx2[:], offs2)
@@ -201,11 +202,7 @@ def tile_list_mimo_beam_channel_kernel(
         load_gains(gain_im, g_im)
         nc.sync.dma_start(out=wi_codes[:].bitcast(I32), in_=wi_words.bitcast(I32).rearrange("a p n -> p a n"))
         load_words(u_tables[IMAG], tab2_words[IMAG])
-        for q in range(4):
-            nc.sync.dma_start(
-                out=wi_planes[32 * q : 32 * q + 4, :, :].bitcast(I32),
-                in_=wi_scales[:, 4 * q : 4 * q + 4, :].bitcast(I32).rearrange("a r n -> r a n"),
-            )
+        load_table_scales(wi_planes, wi_scales)
         load_words(v_table_real, tab_words[REAL])
         load_gains(gain_re, g_re)
         load_wr(wr_rows[1], 0, slice(0, N))
@@ -236,11 +233,16 @@ def tile_list_mimo_beam_channel_kernel(
         re_first = [bank("x", [P, S2]) for t in range(PACK)]
         for t in range(PACK):
             first_stage(re_first[t][:], IMAG, IMAG, 0, t, everyone, True, False)
-        wi_scales_dealt = own("wi_scales_dealt", [P, 2, N], U8)
+        wi_scales_dealt = own("wi_scales_dealt", [P, N], U8)
         nc.vector.tensor_copy(
-            wi_scales_dealt[:].rearrange("p h (s m) -> p h s m", s=PACK),
-            wi_planes[:].rearrange("p h (m s) -> p h s m", s=PACK),
+            wi_scales_dealt[:].rearrange("p (s m) -> p s m", s=PACK), wi_planes[:].rearrange("p (m s) -> p s m", s=PACK)
         )
+        for q in range(4):
+            nc.sync.dma_start(
+                out=wi_scales_second[32 * q : 32 * q + 4, :].bitcast(I32),
+                in_=wi_scales_dealt[32 * q + 4 : 32 * q + 8, :].bitcast(I32),
+            )
+        wi_scales_by_half = (wi_scales_dealt, wi_scales_second)
         gather_v_words(v_words[REAL, 0], v_table_real, 0)
         second_products = [[], []]
         for t in range(PACK):
@@ -318,9 +320,9 @@ def tile_list_mimo_beam_channel_kernel(
         zr_second_half(0)
         zr_second_half(1)
         first_imag(0)
-        first_imag(1)
         quantise(wr_codes[0][:], wr_scales[0][:], wr_whole_woven[:].rearrange("p s m t -> p (s m) t"))
         first_real(0)
+        first_imag(1)
         quantise(wr_codes[1][:], wr_scales[1][:], wr_shared_woven[:].rearrange("p s m t -> p (s m) t"))
         close(0)
         close(1)

@@ -24,13 +24,13 @@ PASS = P * PACK
 CHUNKS = S2 // P
 RUN = 4
 REAL, IMAG = 0, 1
-WR_EARLY = 128
 KB = 1024
 AT_V_REAL = 0
 AT_WR = 8 * KB
 AT_PRODUCT = AT_WR + 17 * KB
 AT_V_WORDS = AT_PRODUCT + 16 * KB
 AT_WI = AT_PRODUCT + 7 * KB
+AT_V_IMAG = AT_V_WORDS + 4 * KB
 SLICE = 2 * KB
 
 
@@ -80,11 +80,18 @@ def tile_list_mimo_beam_channel_kernel(
         def gather_v_words(words, table, h):
             nc.vector.tensor_copy(words[:].rearrange("p (t m) -> p m t", t=PACK), table[:].indirect(half_list(h)))
 
+        def move_v_scales(a):
+            for q in range(4):
+                nc.sync.dma_start(
+                    out=v_scales[a][32 * q : 32 * q + 4, :, :].bitcast(I32),
+                    in_=v_scales_listed[16 * a + 4 * q : 16 * a + 4 * q + 4, :, :].bitcast(I32),
+                )
+
         def first_stage(out, v_pass, u_pass, h, t, users, start, stop):
             nc.tensor.matmul_mx(
                 out=out,
                 lhsT=v_words[v_pass, h][:, chunk(t)].bitcast(FP8X4),
-                lhsT_scale=v_scales[h][4 * v_pass :, chunk(t)],
+                lhsT_scale=v_scales[v_pass][:, h, chunk(t)],
                 rhs=u_words[u_pass][:, users].bitcast(FP8X4),
                 rhs_scale=u_scales[4 * u_pass :, users],
                 start=start,
@@ -160,7 +167,8 @@ def tile_list_mimo_beam_channel_kernel(
         idx = keep.tile([P, S // 16], U16, name="idx")
         idx2 = keep.tile([P, S2 // 16], U16, name="idx2")
         u_scales = own("u_scales", [P, S2], U8)
-        v_scales = [own("v_scales%d" % h, [P, PASS], U8) for h in halves]
+        v_scales_listed = own("v_scales_listed", [P, 2, PASS], U8)
+        v_scales = [own("v_scales%d" % a, [P, 2, PASS], U8) for a in (REAL, IMAG)]
         u_words = {a: own("u_words%d" % a, [P, S2], U32) for a in (REAL, IMAG)}
         v_words = {(IMAG, h): own("v_words_imag%d" % h, [P, PASS], U32) for h in halves}
         v_words[REAL, 0] = at(AT_V_WORDS, "v_words_real0", [P, PASS], U32)
@@ -178,41 +186,44 @@ def tile_list_mimo_beam_channel_kernel(
         wi_planes = own("wi_planes", [P, N], U8)
         wi_scales_second = own("wi_scales_second", [P, N], U8)
         u_tables = [own("u_table%d" % a, [P, T2], U32) for a in (REAL, IMAG)]
-        v_table_imag = own("v_table_imag", [P, T], U32)
+        v_table_imag = at(AT_V_IMAG, "v_table_imag", [P, T], U32)
         v_table_real = at(AT_V_REAL, "v_table_real", [P, T], U32)
         u_scale_table = own("u_scale_table", [P, T2], U8)
         v_scale_table = own("v_scale_table", [P, T], U8)
         gain_re = own("gain_re", [P, 2, PACK], F32)
         wr_shared_woven = own("wr_shared_woven", [P, PACK, P, PACK], BF16)
-        wr_rows = [at(AT_WR + 8 * KB, "wr_rows0", [P, PACK, N - WR_EARLY], F32), at(AT_WR, "wr_rows1", [P, PACK, N], F32)]
-        wr_early = own("wr_early", [P, PACK, WR_EARLY], F32)
+        wr_rows = [at(AT_WR + 8 * KB, "wr_rows0", [P, PACK, N], F32), at(AT_WR, "wr_rows1", [P, PACK, N], F32)]
         power_rows = own("power_rows", [P, S2], F32)
         wi_codes = at(AT_WI, "wi_codes", [P, 2, 2 * N], U8)
 
-        for scale_tile in (u_scale_table, v_scale_table, wi_planes, wi_scales_second):
+        for rows in (slice(32, 64), slice(64, P)):
+            nc.vector.memset(v_scale_table[rows, :].bitcast(I32), 0)
+        for scale_tile in (u_scale_table, wi_planes, v_scales[IMAG], v_scales[REAL], wi_scales_second):
             nc.gpsimd.memset(scale_tile[:].bitcast(I32), 0)
 
-        nc.sync.dma_start(idx2[:], offs2)
+        nc.sync.dma_start(
+            out=v_scale_table[0:32, :].bitcast(I32), in_=tab_scales.rearrange("a q t -> (a q) t").bitcast(I32)
+        )
         nc.sync.dma_start(idx[:], offs)
+        nc.sync.dma_start(idx2[:], offs2)
         load_words(u_tables[REAL], tab2_words[REAL])
         load_table_scales(u_scale_table, tab2_scales)
-        load_table_scales(v_scale_table, tab_scales)
-        load_wr(wr_early, 1, slice(0, WR_EARLY))
         load_words(v_table_imag, tab_words[IMAG])
+        load_table_scales(wi_planes, wi_scales)
         load_gains(gain_im, g_im)
         nc.sync.dma_start(out=wi_codes[:].bitcast(I32), in_=wi_words.bitcast(I32).rearrange("a p n -> p a n"))
         load_words(u_tables[IMAG], tab2_words[IMAG])
-        load_table_scales(wi_planes, wi_scales)
+        nc.vector.tensor_copy(
+            v_scales_listed[:].rearrange("p h (t m) -> p h m t", t=PACK), v_scale_table[:].indirect(idx[:])
+        )
+        move_v_scales(IMAG)
         load_words(v_table_real, tab_words[REAL])
+        move_v_scales(REAL)
         load_gains(gain_re, g_re)
         load_wr(wr_rows[1], 0, slice(0, N))
-        load_wr(wr_rows[0], 1, slice(WR_EARLY, N))
+        load_wr(wr_rows[0], 1, slice(0, N))
         nc.sync.dma_start(out=power_rows[:], in_=power.partition_broadcast(P))
 
-        nc.scalar.copy(
-            out=wr_shared_woven[:, :, : WR_EARLY // PACK, :].rearrange("p s m t -> p m t s"),
-            in_=wr_early[:].rearrange("p t (m s) -> p m t s", s=PACK),
-        )
         wi_dealt = own("wi_dealt", [P, 2, 2 * N], U8)
         nc.scalar.copy(
             out=wi_dealt[:].bitcast(U16).rearrange("p h (s m) -> p h s m", s=PACK),
@@ -221,10 +232,6 @@ def tile_list_mimo_beam_channel_kernel(
         product = [at(AT_PRODUCT + PACK * SLICE * (1 - h), "product%d" % h, [P, PACK, S2], F32) for h in halves]
         nc.vector.tensor_copy(u_words[REAL][:], u_tables[REAL][:].indirect(idx2[:]))
         nc.vector.tensor_copy(u_scales[:], u_scale_table[:].indirect(idx2[:]))
-        for h in halves:
-            nc.vector.tensor_copy(
-                v_scales[h][:].rearrange("p (t m) -> p m t", t=PACK), v_scale_table[:].indirect(half_list(h))
-            )
         for h, ring in ((0, "x"), (1, "y")):
             gather_v_words(v_words[IMAG, h], v_table_imag, h)
             im_first_product(h, ring)
@@ -233,7 +240,7 @@ def tile_list_mimo_beam_channel_kernel(
         re_first = [bank("x", [P, S2]) for t in range(PACK)]
         for t in range(PACK):
             first_stage(re_first[t][:], IMAG, IMAG, 0, t, everyone, True, False)
-        wi_scales_dealt = own("wi_scales_dealt", [P, N], U8)
+        wi_scales_dealt = at(AT_V_IMAG, "wi_scales_dealt", [P, N], U8)
         nc.vector.tensor_copy(
             wi_scales_dealt[:].rearrange("p (s m) -> p s m", s=PACK), wi_planes[:].rearrange("p (m s) -> p s m", s=PACK)
         )
@@ -255,7 +262,7 @@ def tile_list_mimo_beam_channel_kernel(
 
         wr_whole_woven = at(AT_V_REAL, "wr_whole_woven", [P, PACK, P, PACK], BF16)
         weave_wr_on_gpsimd(wr_whole_woven[:], wr_rows[1][:])
-        weave_wr_on_gpsimd(wr_shared_woven[:, :, WR_EARLY // PACK :, :], wr_rows[0][:])
+        weave_wr_on_gpsimd(wr_shared_woven[:], wr_rows[0][:])
 
         for t in range(PACK):
             second_products[1].append(im_second_product(1, t, "y"))
@@ -319,6 +326,7 @@ def tile_list_mimo_beam_channel_kernel(
 
         zr_second_half(0)
         zr_second_half(1)
+        zr_second_half(2)
         first_imag(0)
         quantise(wr_codes[0][:], wr_scales[0][:], wr_whole_woven[:].rearrange("p s m t -> p (s m) t"))
         first_real(0)
@@ -327,11 +335,10 @@ def tile_list_mimo_beam_channel_kernel(
         close(0)
         close(1)
         first_real(1)
-        zr_second_half(2)
         scale_y(0)
         close(2)
-        close(3)
         scale_y(1)
+        close(3)
         scale_y(2)
         quantise_y(0)
         store_codes(chunk(0))

@@ -31,6 +31,7 @@ AT_PRODUCT = AT_WR + 17 * KB
 AT_V_WORDS = AT_PRODUCT + 16 * KB
 AT_WI = AT_PRODUCT + 7 * KB
 AT_V_IMAG = AT_V_WORDS + 4 * KB
+AT_WR_SECOND = AT_V_IMAG + 8 * KB
 SLICE = 2 * KB
 
 
@@ -124,7 +125,7 @@ def tile_list_mimo_beam_channel_kernel(
 
         def weave_wr_on_gpsimd(woven, rows):
             nc.gpsimd.tensor_scalar(
-                out=woven.rearrange("p s m t -> p m s t"), in0=rows.rearrange("p t (m s) -> p m s t", s=PACK),
+                out=woven.rearrange("p s m t -> p m t s"), in0=rows.rearrange("p t (m s) -> p m t s", s=PACK),
                 scalar1=1.0, scalar2=0.0, op0=MULT, op1=ADD,
             )
 
@@ -136,15 +137,16 @@ def tile_list_mimo_beam_channel_kernel(
             for t in range(PACK):
                 nc.tensor.matmul_mx(
                     out=y_sums[c][:, t, :], lhsT=weights[:, t * width : (t + 1) * width].bitcast(dtype),
-                    lhsT_scale=weight_scales[:, chunk(t)], rhs=codes[:, chunk(c)].bitcast(FP8X4),
+                    lhsT_scale=weight_scales[:, chunk(t)], rhs=codes.bitcast(FP8X4),
                     rhs_scale=scales[:, chunk(c)], start=start and t == 0, stop=stop and t == PACK - 1,
                 )
 
-        def real_pass(c, h, start):
-            second_stage(c, wr_codes[h][:], wr_scales[h][:], FP8X4, zr_codes[h], zr_scales[h], start, False)
+        def real_pass(c, h, start, stop=False):
+            codes = zr_codes[1][:, chunk(c)] if h else zr_first_codes[c // 2][:, chunk(c % 2)]
+            second_stage(c, wr_codes[h][:], wr_scales[h][:], FP8X4, codes, zr_scales[h], start, stop)
 
         def imag_pass(c, h, start, stop):
-            second_stage(c, wi_dealt[:, h, :], wi_scales_by_half[h][:], FP4X4, zi_codes[h], zi_scales[h], start, stop)
+            second_stage(c, wi_dealt[:, h, :], wi_scales_dealt[:, h, :], FP4X4, zi_codes[h][:, chunk(c)], zi_scales[h], start, stop)
 
         def zr_second_half(c):
             nc.vector.tensor_tensor(
@@ -183,22 +185,21 @@ def tile_list_mimo_beam_channel_kernel(
         y_codes = own("y_codes", [P, S2], U32)
         y_scales = own("y_scales", [P, S2], U8)
         gain_im = own("gain_im", [P, 2, PACK], F32)
-        wi_planes = own("wi_planes", [P, N], U8)
-        wi_scales_second = own("wi_scales_second", [P, N], U8)
+        wi_planes = own("wi_planes", [P, 2, N], U8)
         u_tables = [own("u_table%d" % a, [P, T2], U32) for a in (REAL, IMAG)]
         v_table_imag = at(AT_V_IMAG, "v_table_imag", [P, T], U32)
         v_table_real = at(AT_V_REAL, "v_table_real", [P, T], U32)
         u_scale_table = own("u_scale_table", [P, T2], U8)
         v_scale_table = own("v_scale_table", [P, T], U8)
         gain_re = own("gain_re", [P, 2, PACK], F32)
-        wr_shared_woven = own("wr_shared_woven", [P, PACK, P, PACK], BF16)
+        wr_shared_woven = at(AT_WR_SECOND, "wr_shared_woven", [P, PACK, P, PACK], BF16)
         wr_rows = [at(AT_WR + 8 * KB, "wr_rows0", [P, PACK, N], F32), at(AT_WR, "wr_rows1", [P, PACK, N], F32)]
         power_rows = own("power_rows", [P, S2], F32)
         wi_codes = at(AT_WI, "wi_codes", [P, 2, 2 * N], U8)
 
         for rows in (slice(32, 64), slice(64, P)):
             nc.vector.memset(v_scale_table[rows, :].bitcast(I32), 0)
-        for scale_tile in (u_scale_table, wi_planes, v_scales[IMAG], v_scales[REAL], wi_scales_second):
+        for scale_tile in (u_scale_table, wi_planes, v_scales[IMAG], v_scales[REAL]):
             nc.gpsimd.memset(scale_tile[:].bitcast(I32), 0)
 
         nc.sync.dma_start(
@@ -208,15 +209,19 @@ def tile_list_mimo_beam_channel_kernel(
         nc.sync.dma_start(idx2[:], offs2)
         load_words(u_tables[REAL], tab2_words[REAL])
         load_table_scales(u_scale_table, tab2_scales)
-        load_words(v_table_imag, tab_words[IMAG])
-        load_table_scales(wi_planes, wi_scales)
         load_gains(gain_im, g_im)
+        load_words(v_table_imag, tab_words[IMAG])
         nc.sync.dma_start(out=wi_codes[:].bitcast(I32), in_=wi_words.bitcast(I32).rearrange("a p n -> p a n"))
-        load_words(u_tables[IMAG], tab2_words[IMAG])
         nc.vector.tensor_copy(
             v_scales_listed[:].rearrange("p h (t m) -> p h m t", t=PACK), v_scale_table[:].indirect(idx[:])
         )
         move_v_scales(IMAG)
+        load_words(u_tables[IMAG], tab2_words[IMAG])
+        for q in range(4):
+            nc.sync.dma_start(
+                out=wi_planes[32 * q : 32 * q + 4, :, :].bitcast(I32),
+                in_=wi_scales[:, 4 * q : 4 * q + 4, :].bitcast(I32).rearrange("a r n -> r a n"),
+            )
         load_words(v_table_real, tab_words[REAL])
         move_v_scales(REAL)
         load_gains(gain_re, g_re)
@@ -240,16 +245,11 @@ def tile_list_mimo_beam_channel_kernel(
         re_first = [bank("x", [P, S2]) for t in range(PACK)]
         for t in range(PACK):
             first_stage(re_first[t][:], IMAG, IMAG, 0, t, everyone, True, False)
-        wi_scales_dealt = at(AT_V_IMAG, "wi_scales_dealt", [P, N], U8)
+        wi_scales_dealt = at(AT_V_IMAG, "wi_scales_dealt", [P, 2, N], U8)
         nc.vector.tensor_copy(
-            wi_scales_dealt[:].rearrange("p (s m) -> p s m", s=PACK), wi_planes[:].rearrange("p (m s) -> p s m", s=PACK)
+            wi_scales_dealt[:].rearrange("p h (s m) -> p h s m", s=PACK),
+            wi_planes[:].rearrange("p h (m s) -> p h s m", s=PACK),
         )
-        for q in range(4):
-            nc.sync.dma_start(
-                out=wi_scales_second[32 * q : 32 * q + 4, :].bitcast(I32),
-                in_=wi_scales_dealt[32 * q + 4 : 32 * q + 8, :].bitcast(I32),
-            )
-        wi_scales_by_half = (wi_scales_dealt, wi_scales_second)
         gather_v_words(v_words[REAL, 0], v_table_real, 0)
         second_products = [[], []]
         for t in range(PACK):
@@ -280,19 +280,22 @@ def tile_list_mimo_beam_channel_kernel(
             for t in range(PACK):
                 for a in (REAL, IMAG):
                     first_stage(re_second[c][:, t, :], a, a, 1, t, chunk(c), a == REAL, a == IMAG)
+        weave(nc.scalar.copy, zi_woven[1][:, chunk(2), :], zi_slices[1][:, :, chunk(2)])
         zr_last_slices = own("zr_last_slices", [P, PACK, P], BF16)
         zr_last_woven = own("zr_last_woven", [P, P, PACK], BF16)
         for t in range(PACK):
             nc.scalar.activation(
                 out=zr_last_slices[:, t, :], in_=re_second[CHUNKS - 1][:, t, :], func=COPY, scale=gain_re[:, 1, t : t + 1]
             )
-        weave(nc.scalar.copy, zi_woven[1][:, chunk(2), :], zi_slices[1][:, :, chunk(2)])
-        weave(nc.scalar.copy, zr_last_woven[:], zr_last_slices[:])
         weave(nc.scalar.copy, zi_woven[1][:, chunk(3), :], zi_slices[1][:, :, chunk(3)])
+        weave(nc.scalar.copy, zr_last_woven[:], zr_last_slices[:])
 
-        wr_codes = [at(AT_PRODUCT - KB, "wr_codes0", [P, N], U32), at(AT_PRODUCT + KB, "wr_codes1", [P, N], U32)]
-        zi_codes = [at(AT_WR, "zi_codes0", [P, S2], U32), own("zi_codes1", [P, S2], U32)]
-        zr_codes = [own("zr_codes0", [P, S2], U32), at(AT_WR + 2 * KB, "zr_codes1", [P, S2], U32)]
+        wr_codes = [at(AT_WR + 8 * KB, "wr_codes0", [P, N], U32), at(AT_PRODUCT + KB, "wr_codes1", [P, N], U32)]
+        zi_codes = [at(AT_WR, "zi_codes0", [P, S2], U32), at(AT_V_REAL + 2 * KB, "zi_codes1", [P, S2], U32)]
+        zr_codes = [None, at(AT_V_REAL, "zr_codes1", [P, S2], U32)]
+        zr_first_codes = [
+            at(AT_WR + 2 * KB, "zr_first_codes0", [P, S2 // 2], U32), at(AT_WR_SECOND, "zr_first_codes1", [P, S2 // 2], U32)
+        ]
         def quantise_users(codes, scales, woven, users):
             quantise(codes[:, users], scales[:, users], woven[:, users, :])
 
@@ -300,13 +303,16 @@ def tile_list_mimo_beam_channel_kernel(
 
         def close(c):
             woven = zr_last_woven[:] if c == CHUNKS - 1 else zr_woven[1][:, chunk(c), :]
+            if c == CHUNKS - 1:
+                quantise_users(zi_codes[1], zi_scales[1], zi_woven[1], chunk(c))
+                imag_pass(c, 1, False, False)
             quantise(zr_codes[1][:, chunk(c)], zr_scales[1][:, chunk(c)], woven)
-            real_pass(c, 1, False)
-            quantise_users(zi_codes[1], zi_scales[1], zi_woven[1], chunk(c))
-            imag_pass(c, 1, False, True)
+            real_pass(c, 1, False, c == CHUNKS - 1)
+            if c < CHUNKS - 1:
+                quantise_users(zi_codes[1], zi_scales[1], zi_woven[1], chunk(c))
+                imag_pass(c, 1, False, True)
 
         def first_real(b):
-            quantise_users(zr_codes[0], zr_scales[0], zr_woven[0], user_half(b))
             for c in (2 * b, 2 * b + 1):
                 real_pass(c, 0, False)
 
@@ -328,12 +334,14 @@ def tile_list_mimo_beam_channel_kernel(
         zr_second_half(1)
         zr_second_half(2)
         first_imag(0)
+        quantise(zr_first_codes[0][:], zr_scales[0][:, user_half(0)], zr_woven[0][:, user_half(0), :])
+        first_imag(1)
         quantise(wr_codes[0][:], wr_scales[0][:], wr_whole_woven[:].rearrange("p s m t -> p (s m) t"))
         first_real(0)
-        first_imag(1)
         quantise(wr_codes[1][:], wr_scales[1][:], wr_shared_woven[:].rearrange("p s m t -> p (s m) t"))
         close(0)
         close(1)
+        quantise(zr_first_codes[1][:], zr_scales[0][:, user_half(1)], zr_woven[0][:, user_half(1), :])
         first_real(1)
         scale_y(0)
         close(2)

from contextlib import ExitStack

import concourse.mybir as mybir

K, T, S, T2, S2, N = 1024, 2048, 1024, 1024, 512, 512
FLOPS = 2 * (2 * K * S * S2 + 2 * S * N * S2)

F32 = mybir.dt.float32
BF16 = mybir.dt.bfloat16
I32 = mybir.dt.int32
U32 = mybir.dt.uint32
U16 = mybir.dt.uint16
U8 = mybir.dt.uint8
FP8X4 = mybir.dt.float8_e4m3fn_x4
FP4X4 = mybir.dt.float4_e2m1fn_x4
MULT = mybir.AluOpType.mult
ADD = mybir.AluOpType.add
SUB = mybir.AluOpType.subtract
COPY = mybir.ActivationFunctionType.Copy

P = 128
PACK = 4
PASS = P * PACK
CHUNKS = S2 // P
RUN = 4
REAL, IMAG = 0, 1
KB = 1024
AT_V_REAL = 0
AT_WR = 8 * KB
AT_PRODUCT = AT_WR + 17 * KB
AT_V_WORDS = AT_PRODUCT + 16 * KB
AT_WI = AT_PRODUCT + 7 * KB
AT_V_IMAG = AT_V_WORDS + 4 * KB
AT_WR_SECOND = AT_V_IMAG + 8 * KB
SLICE = 2 * KB


def tile_list_mimo_beam_channel_kernel(
    tc, tab_words, tab_scales, tab2_words, tab2_scales, offs, offs2, g_re, g_im, wr, wi_words, wi_scales, power,
    out_0, out_1, out_2,
):
    nc = tc.nc
    with ExitStack() as ctx:
        keep = ctx.enter_context(tc.tile_pool(name="keep", bufs=1))
        reused = ctx.enter_context(tc.tile_pool(name="reused", bufs=1))
        psum = ctx.enter_context(tc.psum_pool(name="psum", bufs=4))

        def own(name, shape, dtype):
            return keep.tile(shape, dtype, name=name, align_bytes=64)

        def at(offset, name, shape, dtype):
            return reused.tile(shape, dtype, name=name, align_bytes=64, offset=offset)

        def bank(ring, shape):
            return psum.tile(shape, F32, name=ring, tag=ring)

        def chunk(c):
            return slice(c * P, (c + 1) * P)

        def user_half(b):
            return slice(b * (S2 // 2), (b + 1) * (S2 // 2))

        def load_words(table, src):
            nc.sync.dma_start(out=table[:].bitcast(I32), in_=src.rearrange("p t i -> p (t i)").bitcast(I32))

        def load_table_scales(table, src):
            for q in range(4):
                nc.sync.dma_start(
                    out=table[32 * q : 32 * q + 8, :].bitcast(I32), in_=src[:, 4 * q : 4 * q + 4, :].bitcast(I32)
                )

        def load_wr(rows, h, cols):
            nc.sync.dma_start(out=rows[:], in_=wr[h * PASS : (h + 1) * PASS, cols].rearrange("(p t) n -> p t n", t=PACK))

        def load_gains(gains, src):
            nc.sync.dma_start(out=gains[:], in_=src.rearrange("(h p t) -> p h t", h=2, t=PACK))

        def half_list(h):
            return idx[:, h * (PASS // 16) : (h + 1) * (PASS // 16)]

        def gather_v_words(words, table, h):
            nc.vector.tensor_copy(words[:].rearrange("p (t m) -> p m t", t=PACK), table[:].indirect(half_list(h)))

        def move_v_scales(a):
            for q in range(4):
                nc.sync.dma_start(
                    out=v_scales[a][32 * q : 32 * q + 4, :, :].bitcast(I32),
                    in_=v_scales_listed[16 * a + 4 * q : 16 * a + 4 * q + 4, :, :].bitcast(I32),
                )

        def first_stage(out, v_pass, u_pass, h, t, users, start, stop):
            nc.tensor.matmul_mx(
                out=out,
                lhsT=v_words[v_pass, h][:, chunk(t)].bitcast(FP8X4),
                lhsT_scale=v_scales[v_pass][:, h, chunk(t)],
                rhs=u_words[u_pass][:, users].bitcast(FP8X4),
                rhs_scale=u_scales[4 * u_pass :, users],
                start=start,
                stop=stop,
            )

        def im_first_product(h, ring):
            for t in range(PACK):
                sums = bank(ring, [P, S2])
                first_stage(sums[:], IMAG, REAL, h, t, everyone, True, True)
                nc.scalar.activation(out=product[h][:, t, :], in_=sums[:], func=COPY, scale=gain_im[:, h, t : t + 1])

        def im_second_product(h, t, ring):
            sums = bank(ring, [P, S2])
            first_stage(sums[:], REAL, IMAG, h, t, everyone, True, True)
            return sums

        def minus_zi(h, banks):
            for t in range(PACK):
                nc.vector.scalar_tensor_tensor(
                    out=zi_slices[h][:, t, :], in0=banks[t][:], scalar=gain_im[:, h, t : t + 1], in1=product[h][:, t, :],
                    op0=MULT, op1=SUB,
                )

        def weave(copy, woven, slices):
            copy(
                out=woven.rearrange("p (c i) t -> p c t i", i=RUN),
                in_=slices.rearrange("p t (c i) -> p c t i", i=RUN),
            )

        def weave_wr_on_gpsimd(woven, rows):
            nc.gpsimd.tensor_scalar(
                out=woven.rearrange("p s m t -> p m t s"), in0=rows.rearrange("p t (m s) -> p m t s", s=PACK),
                scalar1=1.0, scalar2=0.0, op0=MULT, op1=ADD,
            )

        def quantise(codes, scales, woven):
            nc.vector.quantize_mx(out=codes.bitcast(FP8X4), scales=scales, in_=woven.rearrange("p j t -> p (j t)"))

        def second_stage(c, weights, weight_scales, dtype, codes, scales, start, stop):
            width = weights.shape[1] // PACK
            for t in range(PACK):
                nc.tensor.matmul_mx(
                    out=y_sums[c][:, t, :], lhsT=weights[:, t * width : (t + 1) * width].bitcast(dtype),
                    lhsT_scale=weight_scales[:, chunk(t)], rhs=codes.bitcast(FP8X4),
                    rhs_scale=scales[:, chunk(c)], start=start and t == 0, stop=stop and t == PACK - 1,
                )

        def real_pass(c, h, start, stop=False):
            codes = zr_codes[1][:, chunk(c)] if h else zr_first_codes[c // 2][:, chunk(c % 2)]
            second_stage(c, wr_codes[h][:], wr_scales[h][:], FP8X4, codes, zr_scales[h], start, stop)

        def imag_pass(c, h, start, stop):
            second_stage(c, wi_dealt[:, h, :], wi_scales_dealt[:, h, :], FP4X4, zi_codes[h][:, chunk(c)], zi_scales[h], start, stop)

        def zr_second_half(c):
            nc.vector.tensor_tensor(
                out=zr_woven[1][:, chunk(c), :],
                in0=re_second[c][:].rearrange("p t j -> p j t"),
                in1=gain_re[:, 1, :].unsqueeze(1).to_broadcast([P, P, PACK]),
                op=MULT,
            )

        def quantise_y(c):
            quantise(y_codes[:, chunk(c)], y_scales[:, chunk(c)], y_woven[c][:])

        def store_codes(cols):
            nc.sync.dma_start(
                out=out_1[0].rearrange("p m t -> p (m t)").bitcast(I32)[:, cols], in_=y_codes[:, cols].bitcast(I32)
            )

        halves = range(2)
        everyone = slice(0, S2)
        idx = keep.tile([P, S // 16], U16, name="idx")
        idx2 = keep.tile([P, S2 // 16], U16, name="idx2")
        u_scales = own("u_scales", [P, S2], U8)
        v_scales_listed = own("v_scales_listed", [P, 2, PASS], U8)
        v_scales = [own("v_scales%d" % a, [P, 2, PASS], U8) for a in (REAL, IMAG)]
        u_words = {a: own("u_words%d" % a, [P, S2], U32) for a in (REAL, IMAG)}
        v_words = {(IMAG, h): own("v_words_imag%d" % h, [P, PASS], U32) for h in halves}
        v_words[REAL, 0] = at(AT_V_WORDS, "v_words_real0", [P, PASS], U32)
        wr_scales = [own("wr_scales%d" % h, [P, N], U8) for h in halves]
        zr_slices = own("zr_slices", [P, PACK, S2], BF16)
        zi_slices = [own("zi_slices%d" % h, [P, PACK, S2], BF16) for h in halves]
        zr_woven = [own("zr_woven%d" % h, [P, S2, PACK], BF16) for h in halves]
        zr_scales = [own("zr_scales%d" % h, [P, S2], U8) for h in halves]
        zi_scales = [own("zi_scales%d" % h, [P, S2], U8) for h in halves]
        y_rows = [own("y_rows%d" % c, [P, PACK, P], F32) for c in range(CHUNKS)]
        y_woven = [own("y_woven%d" % c, [P, P, PACK], BF16) for c in range(CHUNKS)]
        y_codes = own("y_codes", [P, S2], U32)
        y_scales = own("y_scales", [P, S2], U8)
        gain_im = own("gain_im", [P, 2, PACK], F32)
        wi_planes = own("wi_planes", [P, 2, N], U8)
        u_tables = [own("u_table%d" % a, [P, T2], U32) for a in (REAL, IMAG)]
        v_table_imag = at(AT_V_IMAG, "v_table_imag", [P, T], U32)
        v_table_real = at(AT_V_REAL, "v_table_real", [P, T], U32)
        u_scale_table = own("u_scale_table", [P, T2], U8)
        v_scale_table = own("v_scale_table", [P, T], U8)
        gain_re = own("gain_re", [P, 2, PACK], F32)
        wr_shared_woven = at(AT_WR_SECOND, "wr_shared_woven", [P, PACK, P, PACK], BF16)
        wr_rows = [at(AT_WR + 8 * KB, "wr_rows0", [P, PACK, N], F32), at(AT_WR, "wr_rows1", [P, PACK, N], F32)]
        power_rows = own("power_rows", [P, S2], F32)
        wi_codes = at(AT_WI, "wi_codes", [P, 2, 2 * N], U8)

        for rows in (slice(32, 64), slice(64, P)):
            nc.vector.memset(v_scale_table[rows, :].bitcast(I32), 0)
        for scale_tile in (u_scale_table, wi_planes, v_scales[IMAG], v_scales[REAL]):
            nc.gpsimd.memset(scale_tile[:].bitcast(I32), 0)

        nc.sync.dma_start(
            out=v_scale_table[0:32, :].bitcast(I32), in_=tab_scales.rearrange("a q t -> (a q) t").bitcast(I32)
        )
        nc.sync.dma_start(idx[:], offs)
        nc.sync.dma_start(idx2[:], offs2)
        load_words(u_tables[REAL], tab2_words[REAL])
        load_table_scales(u_scale_table, tab2_scales)
        load_gains(gain_im, g_im)
        load_words(v_table_imag, tab_words[IMAG])
        nc.sync.dma_start(out=wi_codes[:].bitcast(I32), in_=wi_words.bitcast(I32).rearrange("a p n -> p a n"))
        nc.vector.tensor_copy(
            v_scales_listed[:].rearrange("p h (t m) -> p h m t", t=PACK), v_scale_table[:].indirect(idx[:])
        )
        move_v_scales(IMAG)
        load_words(u_tables[IMAG], tab2_words[IMAG])
        for q in range(4):
            nc.sync.dma_start(
                out=wi_planes[32 * q : 32 * q + 4, :, :].bitcast(I32),
                in_=wi_scales[:, 4 * q : 4 * q + 4, :].bitcast(I32).rearrange("a r n -> r a n"),
            )
        load_words(v_table_real, tab_words[REAL])
        move_v_scales(REAL)
        load_gains(gain_re, g_re)
        load_wr(wr_rows[1], 0, slice(0, N))
        load_wr(wr_rows[0], 1, slice(0, N))
        nc.sync.dma_start(out=power_rows[:], in_=power.partition_broadcast(P))

        wi_dealt = own("wi_dealt", [P, 2, 2 * N], U8)
        nc.scalar.copy(
            out=wi_dealt[:].bitcast(U16).rearrange("p h (s m) -> p h s m", s=PACK),
            in_=wi_codes[:].bitcast(U16).rearrange("p h (m s) -> p h s m", s=PACK),
        )
        product = [at(AT_PRODUCT + PACK * SLICE * (1 - h), "product%d" % h, [P, PACK, S2], F32) for h in halves]
        nc.vector.tensor_copy(u_words[REAL][:], u_tables[REAL][:].indirect(idx2[:]))
        nc.vector.tensor_copy(u_scales[:], u_scale_table[:].indirect(idx2[:]))
        for h, ring in ((0, "x"), (1, "y")):
            gather_v_words(v_words[IMAG, h], v_table_imag, h)
            im_first_product(h, ring)

        nc.vector.tensor_copy(u_words[IMAG][:], u_tables[IMAG][:].indirect(idx2[:]))
        re_first = [bank("x", [P, S2]) for t in range(PACK)]
        for t in range(PACK):
            first_stage(re_first[t][:], IMAG, IMAG, 0, t, everyone, True, False)
        wi_scales_dealt = at(AT_V_IMAG, "wi_scales_dealt", [P, 2, N], U8)
        nc.vector.tensor_copy(
            wi_scales_dealt[:].rearrange("p h (s m) -> p h s m", s=PACK),
            wi_planes[:].rearrange("p h (m s) -> p h s m", s=PACK),
        )
        gather_v_words(v_words[REAL, 0], v_table_real, 0)
        second_products = [[], []]
        for t in range(PACK):
            second_products[0].append(im_second_product(0, t, "y"))
            first_stage(re_first[t][:], REAL, REAL, 0, t, everyone, False, True)
            nc.scalar.activation(out=zr_slices[:, t, :], in_=re_first[t][:], func=COPY, scale=gain_re[:, 0, t : t + 1])
        v_words[REAL, 1] = own("v_words_real1", [P, PASS], U32)
        gather_v_words(v_words[REAL, 1], v_table_real, 1)
        minus_zi(0, second_products[0])

        wr_whole_woven = at(AT_V_REAL, "wr_whole_woven", [P, PACK, P, PACK], BF16)
        weave_wr_on_gpsimd(wr_whole_woven[:], wr_rows[1][:])
        weave_wr_on_gpsimd(wr_shared_woven[:], wr_rows[0][:])

        for t in range(PACK):
            second_products[1].append(im_second_product(1, t, "y"))
        minus_zi(1, second_products[1])
        zi_woven = [at(AT_V_WORDS, "zi_woven0", [P, S2, PACK], BF16), own("zi_woven1", [P, S2, PACK], BF16)]
        weave(nc.scalar.copy, zi_woven[0][:, user_half(0), :], zi_slices[0][:, :, user_half(0)])
        weave(nc.scalar.copy, zr_woven[0][:, user_half(0), :], zr_slices[:, :, user_half(0)])
        weave(nc.scalar.copy, zi_woven[0][:, user_half(1), :], zi_slices[0][:, :, user_half(1)])
        for c in (0, 1):
            weave(nc.scalar.copy, zi_woven[1][:, chunk(c), :], zi_slices[1][:, :, chunk(c)])
        weave(nc.scalar.copy, zr_woven[0][:, user_half(1), :], zr_slices[:, :, user_half(1)])
        re_second = []
        for c in range(CHUNKS):
            re_second.append(bank("x", [P, PACK, P]))
            for t in range(PACK):
                for a in (REAL, IMAG):
                    first_stage(re_second[c][:, t, :], a, a, 1, t, chunk(c), a == REAL, a == IMAG)
        weave(nc.scalar.copy, zi_woven[1][:, chunk(2), :], zi_slices[1][:, :, chunk(2)])
        zr_last_slices = own("zr_last_slices", [P, PACK, P], BF16)
        zr_last_woven = own("zr_last_woven", [P, P, PACK], BF16)
        for t in range(PACK):
            nc.scalar.activation(
                out=zr_last_slices[:, t, :], in_=re_second[CHUNKS - 1][:, t, :], func=COPY, scale=gain_re[:, 1, t : t + 1]
            )
        weave(nc.scalar.copy, zi_woven[1][:, chunk(3), :], zi_slices[1][:, :, chunk(3)])
        weave(nc.scalar.copy, zr_last_woven[:], zr_last_slices[:])

        wr_codes = [at(AT_WR + 8 * KB, "wr_codes0", [P, N], U32), at(AT_PRODUCT + KB, "wr_codes1", [P, N], U32)]
        zi_codes = [at(AT_WR, "zi_codes0", [P, S2], U32), at(AT_V_REAL + 2 * KB, "zi_codes1", [P, S2], U32)]
        zr_codes = [None, at(AT_V_REAL, "zr_codes1", [P, S2], U32)]
        zr_first_codes = [
            at(AT_WR + 2 * KB, "zr_first_codes0", [P, S2 // 2], U32), at(AT_WR_SECOND, "zr_first_codes1", [P, S2 // 2], U32)
        ]
        def quantise_users(codes, scales, woven, users):
            quantise(codes[:, users], scales[:, users], woven[:, users, :])

        y_sums = [bank("y", [P, PACK, P]) for c in range(CHUNKS)]

        def close(c):
            woven = zr_last_woven[:] if c == CHUNKS - 1 else zr_woven[1][:, chunk(c), :]
            if c == CHUNKS - 1:
                quantise_users(zi_codes[1], zi_scales[1], zi_woven[1], chunk(c))
                imag_pass(c, 1, False, False)
            quantise(zr_codes[1][:, chunk(c)], zr_scales[1][:, chunk(c)], woven)
            real_pass(c, 1, False, c == CHUNKS - 1)
            if c < CHUNKS - 1:
                quantise_users(zi_codes[1], zi_scales[1], zi_woven[1], chunk(c))
                imag_pass(c, 1, False, True)

        def first_real(b):
            for c in (2 * b, 2 * b + 1):
                real_pass(c, 0, False)

        def first_imag(b):
            quantise_users(zi_codes[0], zi_scales[0], zi_woven[0], user_half(b))
            for c in (2 * b, 2 * b + 1):
                imag_pass(c, 0, True, False)

        def scale_y(c):
            nc.vector.tensor_tensor(
                out=y_rows[c][:], in0=y_sums[c][:],
                in1=power_rows[:, chunk(c)].unsqueeze(1).to_broadcast([P, PACK, P]), op=MULT,
            )
            nc.sync.dma_start(out=out_0.rearrange("(p t) j -> p t j", t=PACK)[:, :, chunk(c)], in_=y_rows[c][:])
            if c < CHUNKS - 1:
                weave(nc.scalar.copy, y_woven[c][:], y_rows[c][:])

        zr_second_half(0)
        zr_second_half(1)
        zr_second_half(2)
        first_imag(0)
        quantise(zr_first_codes[0][:], zr_scales[0][:, user_half(0)], zr_woven[0][:, user_half(0), :])
        first_imag(1)
        quantise(wr_codes[0][:], wr_scales[0][:], wr_whole_woven[:].rearrange("p s m t -> p (s m) t"))
        first_real(0)
        quantise(wr_codes[1][:], wr_scales[1][:], wr_shared_woven[:].rearrange("p s m t -> p (s m) t"))
        close(0)
        close(1)
        quantise(zr_first_codes[1][:], zr_scales[0][:, user_half(1)], zr_woven[0][:, user_half(1), :])
        first_real(1)
        scale_y(0)
        close(2)
        scale_y(1)
        close(3)
        scale_y(2)
        quantise_y(0)
        store_codes(chunk(0))
        scale_y(3)
        quantise_y(1)
        store_codes(chunk(1))
        weave(nc.vector.tensor_copy, y_woven[3][:], y_rows[3][:])
        quantise_y(2)
        quantise_y(3)
        store_codes(user_half(1))
        for q in range(4):
            queue = nc.scalar if q % 2 else nc.sync
            queue.dma_start(
                out=out_2[0, 4 * q : 4 * q + 4, :].bitcast(I32), in_=y_scales[32 * q : 32 * q + 4, :].bitcast(I32)
            )
